import numpy as np, ml_dtypes
CORES = [35,38,43,46]
N = 4
BF = ml_dtypes.bfloat16
CA, LV, NS, RO, HA, HB = 16, 256, 5, 2, 1, 2
W, KC = CA * LV, LV // 4
K = CA * KC
def water(rng, m=16):
    z = np.linspace(1.5, -1.5, LV); res = []
    for sg in (1.0, -1.0):
        v = sg * rng.uniform(0.5, 1.5, (N, 8, 1, CA, 1)) * z + 0.5 * rng.standard_normal((N, 8, 1, CA, 1))
        v = v.astype(np.float32) + 0.25 * rng.standard_normal((N, 8, 1, CA, LV), dtype=np.float32)
        res.append(v + 0.35 * rng.standard_normal((N, 8, m, CA, LV), dtype=np.float32))
    return res
def coef(rng, m=16):
    return np.stack([rng.uniform(0.5, 1.5, (N, 8, m)), rng.uniform(2.0 ** -13, 2.0 ** -11, (N, 8, m)), rng.uniform(0.5, 1.5, (N, 8, m))], axis=-1)
def pack(te, sa, co, cu):
    return {"te": np.ascontiguousarray(te.reshape(N, 128, W)).astype(BF), "sa": np.ascontiguousarray(sa.reshape(N, 128, W)).astype(BF),
            "co": np.ascontiguousarray(co.reshape(N, 128, 3)).astype(np.float32), "cu": np.ascontiguousarray(cu.reshape(N, 8, W)).astype(np.int32)}
def setup_inputs(rng):
    te, sa = water(rng)
    return pack(te, sa, coef(rng), rng.integers(0, CA, (N, 8, W)))
def setup_inputs_spread(rng):
    te, sa = water(rng); k = (N, 8, 1, CA, LV)
    te = te * np.exp2(rng.integers(-3, 4, k)) * (rng.random(k) > 0.0625); sa = sa * np.exp2(rng.integers(-3, 4, k)) * (rng.random(k) > 0.0625)
    co = np.stack([np.exp2(rng.uniform(-2, 2, (N, 8, 16))), rng.uniform(2.0 ** -20, 2.0 ** -10, (N, 8, 16)), np.exp2(rng.uniform(-2, 2, (N, 8, 16)))], axis=-1)
    cu = np.minimum((CA * rng.random((N, 8, W)) ** 3).astype(np.int64), CA - 1)
    return pack(te, sa, co, cu)
def setup_inputs_ends(rng):
    b = 4096.0; pt = np.ones((8, CA, LV)); ps = np.ones((8, CA, LV)); pc = np.zeros((8, CA, LV), np.int64)
    pt[:, 0] = -1; ps[:, 0] = -1; pc[:, 0] = CA - 1
    for c in range(1, CA - 1):
        if c % 4 == 3: ps[:, c] = -1; pt[:, c, :2] = -1; ps[:, c, :2] = 1; pc[:, c] = CA - 1
        else: pt[:, c] = -1; pt[:, c, LV - 2:] = 1; ps[:, c, LV - 2:] = -1
    pt[1::2, CA - 1, LV - 4] = -1; ps[1::2, CA - 1, LV - 2:] = -1
    def turned(m, share, col):
        t = (rng.random((N, 8, m, CA, LV), dtype=np.float32) < share) ^ (rng.random((N, 8, 1, CA, LV), dtype=np.float32) < col)
        t[..., :8] = False; t[..., LV - 8:] = False; t[:, :, :, 0] = False; t[:, :, :, CA - 1] = False
        return t
    te = np.where(turned(16, 0.15, 0.1), -b, b).astype(np.float32) * pt[None, :, None].astype(np.float32)
    sa = np.where(turned(16, 0.15, 0.1), -b, b).astype(np.float32) * ps[None, :, None].astype(np.float32)
    n = te[:, :, :, 4:CA - 1:4].shape
    te[:, :, :, 4:CA - 1:4] = rng.uniform(-b, b, n); sa[:, :, :, 4:CA - 1:4] = rng.uniform(-b, b, n)
    cu = np.where(turned(1, 0.2, 0.0)[:, :, 0], CA - 1 - pc[None], pc[None])
    cu[:, :, 4:CA - 1:4] = (CA - 1) * rng.integers(0, 2, cu[:, :, 4:CA - 1:4].shape)
    good = np.argsort(rng.random((N, 8, 16)), axis=-1) < 11
    co = np.stack([np.where(good | (rng.random((N, 8, 16)) < 0.5), 4.0, 0.25), np.where(rng.random((N, 8, 16)) < 0.5, 0.0, 2.0 ** -10), np.where(good | (rng.random((N, 8, 16)) < 0.5), 0.25, 4.0)], axis=-1)
    return pack(te, sa, co, cu)
def setup_inputs_corners(rng):
    te, sa = water(rng); te = te + rng.choice(np.array([-3.0, 0.0, 3.0]), (N, 8, 1, 1, 1))
    own = np.repeat(np.arange(CA), LV); lev = np.arange(W) % LV; cu = rng.integers(0, CA, (N, 8, W)); any3 = rng.integers(0, 3, (N, 8, W))
    for r in range(N):
        for g in range(8):
            k = (r + g) % 8
            if k == 0: cu[r, g] = own
            elif k == 1: cu[r, g] = 0
            elif k == 2: cu[r, g] = CA - 1
            elif k == 3: cu[r, g] = (own + 1) % CA
            elif k == 4: cu[r, g] = CA - 1 - own
            elif k == 5: cu[r, g] = np.where((lev >> 2) % 2 == 0, 0, CA - 1)
            elif k == 6: cu[r, g] = np.where(any3[r, g] == 0, 0, np.where(any3[r, g] == 1, CA - 1, own))
    co = coef(rng); h = CA // 2
    te[:, 2::4, :, :h] = 0; te[:, 2::4, :, h:] = 1; sa[:, 2::4, :, :h] = 0; sa[:, 2::4, :, h:] = 1
    for r in range(N):
        for g in (2, 6):
            x0 = 128 * (KC // 4 + 1 + 2 * int(rng.integers(0, KC // 8)))
            a0 = rng.uniform(0.5, 1.5, 4096).astype(np.float32); a1 = (rng.uniform(0.5, 1.0, 4096) / x0).astype(np.float32)
            two = a1 * np.float32(x0) + a0; one = (a1.astype(np.float64) * x0 + a0.astype(np.float64)).astype(np.float32)
            k = np.argsort(np.where(one > two, 0, 1), kind="stable")[:16]
            co[r, g] = np.stack([a0[k], a1[k], two[k]], axis=-1); cu[r, g] = rng.integers(h, CA, W)
    f4 = np.float32
    for r in range(N):
        ra = (r + HA) % N; rb = (r + HB) % N
        for g in (1, 3, 4, 5, 7):
            j = KC // 4 + 1 + int(rng.integers(0, KC // 4)); l = 4 * j + 1; x0 = 128 * j + (28 if g == 4 else 24)
            a0 = rng.uniform(0.5, 1.5, 4096).astype(f4); a1 = (rng.uniform(0.5, 1.0, 4096) / x0).astype(f4); w = a1 * f4(x0) + a0
            tu = np.full(4096, 32, f4); su = np.full(4096, 32, f4); b0 = np.nextafter(w, f4(0)); ok = np.ones(4096, bool)
            if g == 1:
                b0 = w; ok = ((a1 * f4(x0 - 8) + a0) + a1 * f4(8)) > w
            if g in (3, 7):
                tu = (2 * rng.integers(64, 128, 4096)).astype(f4); su = (2 * rng.integers(64, 128, 4096)).astype(f4)
                left = tu * w; b0 = left / su; ok = (su * b0 == left) & (b0 < 4)
                if g == 3: ok = ok & (tu.astype(np.float64) * w.astype(np.float64) > su.astype(np.float64) * b0.astype(np.float64))
                else: ok = ok & (left * (f4(1) / b0) > su)
                b0 = np.minimum(b0, f4(4))
            k = np.argsort(np.where(ok, 0, 1), kind="stable")[:16]
            tl, tr = (2816, -1280) if g == 4 else (1792, -2304)
            sl, sr, s1 = 0.0, 0.0, -su[k]
            if g == 4: sl, sr, s1 = 1.25 * 2.0 ** -18, -128.0, np.full(16, -128.0)
            if g == 5: sl, sr, s1 = -224.0, 288.0, np.full(16, -2.0 ** -18)
            te[ra, g, :, 1, :l + 1] = tl; te[ra, g, :, 1, l + 1:] = tr
            sa[ra, g, :, 1, :l + 1] = sl; sa[ra, g, :, 1, l + 1:] = sr
            te[r, g, :, 4:, 4 * j] = (-256 - tu[k])[:, None]; sa[r, g, :, 4:, 4 * j] = s1[:, None]
            cu[r, g, 4 * LV + 4 * j::LV] = 1; cu[ra, g, LV + l] = int(rng.integers(4, CA))
            co[ra, g] = np.stack([a0[k], a1[k], b0[k]], axis=-1)
        te[r, 7, :, 4:, LV - 4] = -544; sa[r, 7, :, 4:, LV - 4] = -32; cu[r, 7, 5 * LV - 4::LV] = 2
        te[ra, 7, :, 2] = -288; sa[ra, 7, :, 2] = -32; cu[ra, 7, 3 * LV - 2] = 3
        te[rb, 0, :, 3, LV - 2] = 3328; te[rb, 0, :, 3, LV - 1] = -768; sa[rb, 0, :, 3, LV - 2:] = 0
        xm = 32 * (LV - 2) + 28
        a0 = rng.uniform(0.5, 1.5, 16).astype(f4); a1 = (rng.uniform(0.5, 1.0, 16) / xm).astype(f4)
        co[rb, 0] = np.stack([a0, a1, a1 * f4(xm - 1) + a0], axis=-1)
    return pack(te, sa, co, cu)
def setup_inputs_crowd(rng):
    te, sa = water(rng, 1); e = rng.permutation(16); sg = np.ones((8, 16), np.float32)
    for g in range(8): sg[g, e[:(0, 1, 7, 8)[g % 4]]] = -1
    te = te * sg[None, :, :, None, None]; sa = sa * sg[None, :, :, None, None]
    co = np.repeat(coef(rng, 1), 16, axis=2)
    one = rng.integers(0, CA, (N, 8)); cu = np.repeat(one[:, :, None], W, axis=2)
    for r in range(N):
        for g in range(1, 8, 2): cu[r, g, 4 * int(rng.integers(0, K))] = (one[r, g] + 1 + int(rng.integers(0, CA - 1))) % CA
    return pack(te, sa, co, cu)
def setup_inputs_calm(rng):
    te, sa = water(rng); co = coef(rng); cu = rng.integers(0, CA, (N, 8, CA, LV))
    e = rng.permutation(16); up = np.zeros(16, bool); up[e[:8]] = True
    t = 0.25 * rng.integers(-4, 5, 16); s = 0.25 * rng.integers(-4, 5, 16)
    sa[:, :, :, :4] = s[None, None, :, None, None]; sa[:, :, :, :, :2] = s[None, None, :, None, None]; sa[:, :, :, :, LV - 4:] = s[None, None, :, None, None]
    te[:, :, :, :4] = t[None, None, :, None, None]; te[:, :, :, 3] += 1; te[:, :, int(e[0]), 0] += 0.9
    for g in range(4):
        a1 = t + 1 - 16 / (2 * g + 1); b1 = t - 1 + 16 / (1.0, 1.0, 1.5, 1.8)[g]
        te[:, g, :, 4:, 0] = np.where(up, t + 1, t - 1)[None, :, None]; te[:, g, :, 4:, 1] = np.where(up, a1, b1)[None, :, None]
    for g in range(4, 8):
        for lv, v in ((LV - 4, -1.0), (LV - 3, -1.3684), (LV - 2, 2.0), (LV - 1, 2.0 if g % 2 == 0 else 2 - 16 / 13)): te[:, g, :, 4:, lv] = (t + v)[None, :, None]
    cu[:, :4, 4:, :4] = 0; cu[:, 4:, 4:, LV - 4:] = 2; cu[:, :, 0] = 1; cu[:, :, 2] = 3
    cu[:, :, 0, 8:] = rng.integers(4, CA, (N, 8, LV - 8))
    return pack(te, sa, co, cu)
def check_inputs(d):
    bad = []
    if np.min(d["cu"]) < 0 or np.max(d["cu"]) > CA - 1: bad.append("range of cu")
    for k in ("te", "sa"):
        a = np.abs(np.asarray(d[k]).astype(np.float32))
        if not np.max(a) <= 4096: bad.append("range of " + k)
        if np.any((a > 0) & (a < 2.0 ** -60)): bad.append("least size in " + k)
    c = np.asarray(d["co"]).astype(np.float64)
    for j, lo, hi in ((0, 0.25, 4.0), (1, 0.0, 2.0 ** -10), (2, 0.25, 4.0)):
        if not (np.min(c[..., j]) >= lo and np.max(c[..., j]) <= hi): bad.append("range of co, column " + str(j))
    if np.any((c[..., 1] > 0) & (c[..., 1] < 2.0 ** -20)): bad.append("least size in co, column 1")
    return bad
def reference(te, sa, co, cu):
    tw = te.astype(np.float32).reshape(N, 8, 16, W); sw = sa.astype(np.float32).reshape(N, 8, 16, W)
    cf = co.astype(np.float32).reshape(N, 8, 16, 3); cr = cu.astype(np.int64)
    base = (np.arange(N * 128) * W).reshape(N, 8, 16, 1); cbase = (np.arange(N * 8) * W).reshape(N, 8, 1)
    def pick(a, at):
        return np.take(a.reshape(-1), base + at[:, :, None, :])
    def moved(a, o, sh):
        return np.roll(a, (-o, -sh), (0, 1))
    def frac(k):
        return k.astype(np.float32)[:, :, None, :] * np.float32(0.0625)
    def passed(tv, sv, t1, s1, x, c):
        w = c[..., 1:2] * x.astype(np.float32)[:, :, None, :] + c[..., 0:1]
        yes = (tv - t1) * w > (sv - s1) * c[..., 2:3]
        return np.add.reduce(yes.astype(np.int64), axis=2) >= 9
    home = np.ascontiguousarray(np.broadcast_to(np.arange(K) // KC, (N, 8, K)))
    dep = np.ascontiguousarray(np.broadcast_to(64 * (np.arange(K) % KC), (N, 8, K)))
    for rnd in range(RO):
        d = dep; c = home; col = c * LV + (d >> 4); k = frac(d & 15)
        lo = pick(tw, col); t1 = lo + (pick(tw, col + 1) - lo) * k
        lo = pick(sw, col); s1 = lo + (pick(sw, col + 1) - lo) * k
        cnow = cr
        for hop, (o, sh) in enumerate(((HA, 0), (HB, 1), (0, 0))):
            c = np.take(cnow.reshape(-1), cbase + c * LV + (d >> 4)) if hop < 2 else home
            cnow = moved(cr, o, sh); th = moved(tw, o, sh); sh_ = moved(sw, o, sh); ch = moved(cf, o, sh)
            l = d >> 4
            for j in range(NS - 1, -1, -1):
                st = 2 ** j
                ok = passed(pick(th, c * LV + l), pick(sh_, c * LV + l), t1, s1, d + 16 * l, ch)
                l = np.where(ok, np.minimum(l + st, LV - 2), np.maximum(l - st, 0))
            ta = pick(th, c * LV + l); tb = pick(th, c * LV + l + 1) - ta
            sa_ = pick(sh_, c * LV + l); sb = pick(sh_, c * LV + l + 1) - sa_
            q = np.zeros_like(l)
            for h in (8, 4, 2):
                k = frac(q + h)
                ok = passed(ta + tb * k, sa_ + sb * k, t1, s1, d + 16 * l + q + h, ch)
                q = np.where(ok, q + h, q)
            k = frac(q); t1 = ta + tb * k; s1 = sa_ + sb * k; d = 16 * l + q
        dep = dep + ((d - dep) >> 1)
        old = tw[..., rnd::4]; tw[..., rnd::4] = old + (t1 - old) * np.float32(0.25)
        old = sw[..., rnd::4]; sw[..., rnd::4] = old + (s1 - old) * np.float32(0.25)
    return {"yt": np.ascontiguousarray(tw[..., RO - 1::4]).reshape(N, 128, K), "ys": np.ascontiguousarray(sw[..., RO - 1::4]).reshape(N, 128, K), "yd": dep.astype(np.float32)}

@@ -1,0 +1,929 @@
+import math
+from concourse.mybir import AluOpType, ActivationFunctionType
+
+AL = AluOpType
+AF = ActivationFunctionType
+NC, NW = 512, 32
+WE = 4080
+
+OPT = {"search0": "pe", "search1": "pe", "refine": "pe", "bias": {}, "relay": True, "sweeps": 3, "heat": 100.0, "moves": 800, "lodve": "", "seldve": False, "wact": (1, 2, 3), "share0": 0, "share1": 128, "hold": False, "slope0": "", "slope1": "", "halves": True, "pieces": 2, "lead": [2500.0] * 12,
+       "tact": ((), ()), "slack": {"dve": 100.0, "act": 450.0, "pe": 300.0},
+       "g": 1.56, "f": 1.0, "pe": 0.42, "lat": 80.0, "link": 70.0, "hbm": 250.0}
+
+MS = (16, 8, 4, 2, 1, 256, 768, 0.5)
+IS = (1.0, 8.0, 16.0, 0.5, 256.0, 4080.0, -1.0)
+MT_COLS = 128 * (2 * len(MS) + len(IS) + 3) + 144 * 3
+SCRATCH = {
+    "SA": ("sbuf", [128, 8192], "float32"), "SB": ("sbuf", [128, 8192], "float32"),
+    "WO": ("sbuf", [128, 2 * WE], "float32"), "WN": ("sbuf", [128, WE], "float32"), "WP": ("sbuf", [128, WE], "float32"),
+    "CH0": ("sbuf", [128, 6176], "float32"), "CH1": ("sbuf", [128, 6176], "float32"),
+    "LND": ("sbuf", [128, 2112], "float32"), "FI": ("sbuf", [128, 256], "float32"),
+    "CO": ("sbuf", [128, 16], "float32"), "SM": ("sbuf", [128, 192], "float32"),
+    "OB": ("sbuf", [128, 8192], "bfloat16"), "CU": ("sbuf", [128, 4096], "bfloat16"),
+    "AR0": ("sbuf", [128, 2080], "bfloat16"), "AR1": ("sbuf", [128, 2080], "bfloat16"),
+    "FL": ("sbuf", [128, 2112], "bfloat16"), "MT": ("sbuf", [128, MT_COLS], "bfloat16"),
+    "WS0": ("sbuf", [128, 512], "bfloat16"), "WS1": ("sbuf", [128, 512], "bfloat16"),
+    "ST": ("sbuf", [128, 608], "bfloat16"), "CB": ("sbuf", [128, 256], "bfloat16"),
+    "OF0": ("sbuf", [128, 128], "uint16"), "OF1": ("sbuf", [128, 128], "uint16"), "OFS": ("sbuf", [128, 64], "uint16"),
+    "CI": ("sbuf", [128, 256], "int32"), "PI": ("sbuf", [128, 4], "int32"),
+    "DN": ("dram", [2, 128, 4096], "bfloat16"), "DP": ("dram", [2, 128, 4096], "bfloat16"),
+    "DC": ("dram", [128, 256], "bfloat16"),
+    "DU": ("dram", [2, 128, 1024], "float32"), "DS": ("dram", [2, 128, 1024], "float32"),
+}
+for _k in range(2):
+    for _b in ("PS", "PV", "PT", "PK"):
+        SCRATCH[_b + str(_k)] = ("psum", [128, 512], "float32")
+SEMAPHORES = ["c_pe", "c_act", "c_dve", "c_pool"] + ["s%d" % _i for _i in range(110)]
+BYTES = {"float32": 4, "int32": 4, "bfloat16": 2, "uint16": 2}
+
+
+def R(buf, a, b, step=1):
+    return (buf, a, b, step)
+
+
+def sub(r, a, b, step=1):
+    return (r[0], r[1] + a, r[1] + b, step)
+
+
+def IND(win, off):
+    return ("*", win, off)
+
+
+def count(r):
+    if r[0] == "*":
+        return 16 * count(r[2])
+    return len(range(r[1], r[2], r[3]))
+
+
+def is_psum(r):
+    return r[0] != "*" and SCRATCH[r[0]][0] == "psum"
+
+
+def width(r):
+    return BYTES[SCRATCH[(r[1] if r[0] == "*" else r)[0]][2]]
+
+
+def ap(T, r):
+    if isinstance(r, tuple):
+        if r[0] == "*":
+            return ap(T, r[1]).indirect(ap(T, r[2]))
+        if r[3] == 1:
+            return T[r[0]][:, r[1]:r[2]]
+        return T[r[0]][:, r[1]:r[2]:r[3]]
+    return r
+
+
+def parts(rs):
+    out = []
+    for r in rs:
+        if isinstance(r, tuple):
+            out.extend([r[1], r[2]] if r[0] == "*" else [r])
+    return out
+
+
+def build():
+    ops, hist, banks, nsem, phase = [], {}, {}, [0], [0]
+    cyc = 0.83 * OPT["f"]
+    held = {}
+    step = ["-", 0]
+
+    def kind_of():
+        step[1] += 1
+        return "-" if step[0] == "-" else step[0] + str(step[1])
+
+    def new_sem():
+        nsem[0] += 1
+        return "s%d" % (nsem[0] - 1)
+
+    def add(eng, dur, fn, reads, writes, after=(), kind="c", lat=0.0, **kw):
+        i = len(ops)
+        deps = {}
+        for rs, wr in ((parts(reads), False), (parts(writes), True)):
+            for r in rs:
+                if r[0] in SCRATCH and SCRATCH[r[0]][0] == "psum":
+                    st = banks.setdefault(r[0], {"touch": {}, "w": None})
+                    for e, j in st["touch"].items():
+                        if e != eng:
+                            deps[j] = "raw"
+                        else:
+                            deps.setdefault(j, "ord")
+                w = BYTES[SCRATCH[r[0]][2]] if r[0] in SCRATCH else 4
+                lo, hi = (r[1] * w) // 16, (r[2] * w + 15) // 16
+                for (l2, h2, j, w2, e2) in hist.get(r[0], ()):
+                    if j != i and l2 < hi and lo < h2 and (wr or w2):
+                        if w2 and not wr:
+                            deps[j] = "raw"
+                        else:
+                            deps[j] = "raw"
+        for rs, wr in ((parts(reads), False), (parts(writes), True)):
+            for r in rs:
+                if r[0] in SCRATCH and SCRATCH[r[0]][0] == "psum":
+                    banks[r[0]]["touch"][eng] = i
+                w = BYTES[SCRATCH[r[0]][2]] if r[0] in SCRATCH else 4
+                lo, hi = (r[1] * w) // 16, (r[2] * w + 15) // 16
+                h = hist.setdefault(r[0], [])
+                if wr and r[3] == 1 and (r[1] * w) % 16 == 0 and (r[2] * w) % 16 == 0:
+                    h[:] = [x for x in h if not (lo <= x[0] and x[1] <= hi)]
+                elif not wr and step[0] != "-" and r[0] in ("MT", "ST", "FI", "CO"):
+                    continue
+                h.append((lo, hi, i, wr, eng))
+        for j in after:
+            deps[j] = "raw"
+        o = {"eng": eng, "dur": dur, "fn": fn, "deps": deps, "kind": kind, "lat": lat, "phase": phase[0], "cls": kind_of(),
+             "lead": any(r[0][-1] == "0" for r in parts(reads) + parts(writes))}
+        o.update(kw)
+        ops.append(o)
+        return i
+
+    def dve_time(n, c, gather):
+        if gather:
+            return 50.0 + n * OPT["g"] * cyc
+        return 20.0 + max(64.0, n * c) * cyc
+
+    def tt(out, a, b, op):
+        c = 1.0 if (is_psum(a) or is_psum(b)) else 2.0
+        return add("dve", dve_time(count(out), c, a[0] == "*"),
+                   lambda g, T: g.vector.tensor_tensor(ap(T, out), ap(T, a), ap(T, b), op), [a, b], [out])
+
+    def ts(out, a, s1, s2, op0, op1=None, **kw):
+        c = 0.5 if (width(out) == 2 and width(a) == 2) else 1.0
+
+        def fn(g, T):
+            if op1 is None:
+                return g.vector.tensor_scalar(ap(T, out), ap(T, a), ap(T, s1), None, op0)
+            return g.vector.tensor_scalar(ap(T, out), ap(T, a), ap(T, s1), ap(T, s2), op0, op1)
+        return add("dve", dve_time(count(out), c, a[0] == "*"), fn, [a, s1, s2], [out], **kw)
+
+    def cp(out, a):
+        c = 0.5 if (width(out) == 2 and width(a) == 2) else 1.0
+        return add("dve", dve_time(count(out), c, a[0] == "*"),
+                   lambda g, T: g.vector.tensor_copy(ap(T, out), ap(T, a)), [a], [out])
+
+    def ms(out, v):
+        return add("dve", dve_time(count(out), width(out) / 4.0, False),
+                   lambda g, T: g.vector.memset(ap(T, out), v), [], [out])
+
+    def act(out, a, func=None, scale=1.0, bias=0.0, **kw):
+        func = func or (AF.Copy if bias == 0.0 else AF.Identity)
+        n = count(out)
+        d = 65.0 + n * OPT["g"] * cyc if a[0] == "*" else 60.0 + max(64, n) * cyc
+        return add("act", d, lambda g, T: g.scalar.activation(ap(T, out), ap(T, a), func, bias=ap(T, bias), scale=ap(T, scale)),
+                   [a, scale, bias], [out], **kw)
+
+    def mm(groups, start=True, stop=True):
+        d = 30.0
+        rd, wr = [], []
+        for out, pairs in groups:
+            wr.append(out)
+            for l, r in pairs:
+                d += max(64, count(r)) * (4 if width(r) == 4 else 1) * OPT["pe"] * OPT["f"]
+                rd.extend([l, r])
+
+        def fn(g, T):
+            ins = None
+            for out, pairs in groups:
+                for n, (l, r) in enumerate(pairs):
+                    ins = g.tensor.matmul(ap(T, out), ap(T, l), ap(T, r), start and n == 0, stop and n == len(pairs) - 1)
+            return ins
+        i = add("pe", d, fn, rd, wr)
+        if start and stop:
+            held[wr[0][0][-1]] = i
+        return i
+
+    def iota(out, pattern, base, cm):
+        def fn(g, T):
+            if SCRATCH[out[0]][2] == "int32":
+                return g.iota(ap(T, out), pattern, base, cm)
+            return g.iota(ap(T, out), pattern, base, cm, allow_small_or_imprecise_dtypes=True)
+        return add("pool", 130.0 + 2 * count(out) * cyc, fn, [], [out])
+
+    def dma(q, pairs, reads, writes, nbytes, after=()):
+        return add(q, 700.0 if q == "pool" else 100.0, pairs, reads, writes, after, "dma",
+                   1800.0 + nbytes / OPT["hbm"], sem=new_sem(), res="hbm" if nbytes > 200000 else "small", busy=nbytes / OPT["hbm"])
+
+    def send(to, src, dst, src_r, dst_r, nbytes, after=(), relay=None):
+        if relay is not None and OPT["relay"]:
+            i = add("pool", 300.0, (src, dst), src_r, [], after, "send", 1500.0 + 0.7 * nbytes / OPT["link"],
+                    sem=new_sem(), rsem=new_sem(), hsem=new_sem(), relay=relay, to=to, res="relay", busy=nbytes / OPT["link"])
+            j = add("none", 0.0, None, [], dst_r, [i], "recv", 2500.0 + nbytes / OPT["link"], sem=ops[i]["rsem"], to=to, relay=relay)
+            return i, j
+        i = add("pool", 300.0, (src, dst), src_r, [], after, "send", 1500.0 + nbytes / OPT["link"],
+                sem=new_sem(), rsem=new_sem(), to=to, res="link%d" % to, busy=nbytes / OPT["link"])
+        j = add("none", 0.0, None, [], dst_r, [i], "recv", 500.0, sem=ops[i]["rsem"], to=to)
+        return i, j
+
+    def sbsend(to, src, dst, after=(), relay=None):
+        return send(to, lambda T: ap(T, src), lambda T: ap(T, dst), [src], [dst], 128 * count(src) * width(src), after, relay)
+
+    mt = [0]
+
+    def mat(n=128):
+        mt[0] += n
+        return R("MT", mt[0] - n, mt[0])
+    I = {s: mat() for s in IS}
+    M = {(s, a): mat() for s in MS for a in (0, 1)}
+    BO, K4, K2 = mat(), mat(), mat()
+    Z8, ZC = mat(144), [mat(144), mat(144)]
+    FIp, FIn = R("FI", 0, 128), R("FI", 128, 256)
+    st = [R("ST", 32 * i, 32 * i + 32) for i in range(11)]
+    ONE, FOUR, SEVEN, ZERO, J1, J2, H1, H2, DL0, HB0, HB1 = st
+    HB = (HB0, HB1)
+    IO, QG = R("ST", 352, 480), R("ST", 480, 608)
+    col = lambda i: R("SM", 4 * i, 4 * i + 1)
+    MC, PG, MK0, MK1, M4, BK, K4C, K2C, E15 = [col(i) for i in range(9)]
+    KT = R("SM", 40, 56)
+    C64 = R("SM", 64, 128)
+    DH = (R("SM", 128, 160), R("SM", 160, 192))
+    CO_O, CO_P, CO_N = [[R("CO", a + j, a + j + 1) for j in range(3)] for a in (0, 8, 12)]
+    CUW = R("CU", 0, 4096)
+
+    def masked(s, sg):
+        return [(M[(s, 0)], sub(sg, 0, 64, 2)), (M[(s, 1)], sub(sg, 1, 64, 2))]
+
+    def chunk(k):
+        c, a, w, o = "CH%d" % k, "AR%d" % k, "WS%d" % k, "OF%d" % k
+        d = {"k": k, "VT": R(c, 0, 2048), "VS": R(c, 2048, 4096), "tb": R(c, 4096, 4608), "sb": R(c, 4608, 5120),
+             "D": R(c, 5120, 5152), "T1": R(c, 5152, 5664), "S1": R(c, 5664, 6176),
+             "Sgb": R(a, 0, 512), "yes": R(a, 512, 1024), "sr8": R(a, 1024, 1536), "sr4": R(a, 1536, 2048),
+             "first": R(a, 1024, 2080), "OF": R(o, 0, 128),
+             "PS": R("PS%d" % k, 0, 512), "PV": R("PV%d" % k, 0, 512), "PT": R("PT%d" % k, 0, 512), "PK": R("PK%d" % k, 0, 512)}
+        for n, nm in enumerate(("L0", "L1", "dq", "B0", "B1", "dqh", "par", "x")):
+            d[nm] = R(w, 32 * n, 32 * n + 32)
+        for n, nm in enumerate(("sg8", "sg4", "sg2", "sAB")):
+            d[nm] = R(w, 256 + 64 * n, 320 + 64 * n)
+        d["low"] = R("SM", 64 + 32 * k, 96 + 32 * k)
+        return d
+    C = [chunk(0), chunk(1)]
+    slot = lambda v, n: sub(v, 512 * n, 512 * n + 512)
+
+    ld_cu = dma("sync", lambda T: [(T.CI[:], T.cu[:])], [], [R("CI", 0, 256)], 131072)
+    ld_co = dma("act", lambda T: [(T.CO[:, 0:3], T.co[:]), (T.CO[0:112, 4:7], T.co[16:128, :]), (T.CO[112:128, 4:7], T.co[0:16, :])],
+                [], [R("CO", 0, 8)], 4096)
+    before = [ld_cu, ld_co]
+    for hf in range(2):
+        for q, name, a in (("sync", "te", 0), ("act", "sa", 4096)):
+            i_ = dma(q, lambda T, name=name, a=a, hf=hf: [(T.OB[:, a + 2048 * hf:a + 2048 * hf + 2048], T[name][:, 2048 * hf:2048 * hf + 2048])],
+                     [], [R("OB", a + 2048 * hf, a + 2048 * hf + 2048)], 524288)
+            ops[i_]["behind"] = list(before)
+            before.append(i_)
+    sbsend(-1, R("CO", 4, 7), R("CO", 12, 15))
+    sbsend(1, R("CO", 0, 3), R("CO", 8, 11))
+
+    ms(CUW, 0.0)
+    cp(R("CB", 0, 256), R("CI", 0, 256))
+    dma("sync", lambda T: [(T.CU[0:128:16, :], T.CB[:])], [R("CB", 0, 256)], [CUW], 65536)
+    iota(MC, [[0, 1]], 0, 1)
+    iota(C64, [[64, 64]], 0, 0)
+    iota(IO, [[1, 128]], 0, -1)
+    iota(QG, [[1, 8], [0, 16]], 0, 0)
+    iota(R("SB", 0, 256), [[2, 256]], 0, 0)
+    iota(H1, [[0, 8], [512, 4]], 0, 0)
+    iota(J1, [[16, 32]], 768, 0)
+    for k in range(2):
+        iota(HB[k], [[256, 8], [0, 4]], 2048 * k, 0)
+    iota(KT, [[1, 16]], 0, 0)
+    ts(PG, MC, -7.5, 0.0625, AL.add, AL.mult)
+    PGI = R("PI", 0, 1)
+    cp(PGI, PG)
+    cp(PG, PGI)
+    ts(E15, PG, -16.0, None, AL.mult)
+    tt(MC, MC, E15, AL.add)
+    ts(M4, MC, 4.0, None, AL.mult)
+    ts(R("OFS", 0, 64), C64, M4, None, AL.add)
+    for s in IS:
+        ts(I[s], IO, 0.0, s, AL.is_equal, AL.mult)
+    for r in range(2):
+        ms(ZC[r], 0.0)
+        cp(sub(ZC[r], 16, 144, 16), sub(I[256.0], r, 128, 16))
+    ts(MK0, MC, 8.0, None, AL.is_lt)
+    ts(MK1, MC, 8.0, None, AL.is_ge)
+    for a, mk in ((0, MK0), (1, MK1)):
+        ts(M[(1, a)], I[1.0], mk, None, AL.mult)
+        for s in MS:
+            if s != 1:
+                act(M[(s, a)], M[(1, a)], scale=float(s))
+    ts(BO, QG, PG, None, AL.is_equal)
+    ms(Z8, 0.0)
+    cp(sub(Z8, 8, 136, 8), sub(BO, 0, 128, 8))
+    ts(E15, MC, 15.0, None, AL.is_equal)
+    ts(BK, E15, 9.5, -8.5, AL.mult, AL.add)
+    ts(K2C, MC, 0.0, 0.125, AL.is_equal, AL.mult)
+    ts(K4C, E15, 0.25, K2C, AL.mult, AL.add)
+    ts(K2, BO, K2C, None, AL.mult)
+    ts(K4, BO, K4C, 2.0, AL.mult, AL.mult)
+    act(FIp, I[1.0])
+    act(FIn, I[-1.0])
+    for t_, v in ((ONE, 1.0), (FOUR, 4.0), (SEVEN, 7.0), (ZERO, 0.0)):
+        ms(t_, v)
+    ts(J2, ONE, MC, None, AL.mult)
+    ts(H2, ONE, MC, 32.0, AL.mult, AL.mult)
+    ts(DL0, H1, 0.125, M4, AL.mult, AL.add)
+    ts(KT, KT, 0.0625, None, AL.mult)
+
+    def cast_of(c, off, row, dst, win=CUW):
+        act(c["Sgb"], IND(win, off))
+        pw = sub(c["PV"], 320, 352)
+        mm([(pw, [(sub(ZC[row], 16 - m, 144 - m), sub(c["Sgb"], m, 512, 16)) for m in range(16)])])
+        act(dst, pw)
+
+    firsts = []
+    for k, c in enumerate(C):
+        cast_of(c, R("OFS", 32 * k, 32 * k + 32), 0, sub(c["first"], 1024, 1056))
+        cp(sub(c["first"], 0, 512), R("OB", 2048 * k, 2048 * k + 2048, 4))
+        act(sub(c["first"], 512, 1024), R("OB", 4096 + 2048 * k, 4096 + 2048 * k + 2048, 4))
+        firsts.append(sbsend(1, c["first"], R("FL", 1056 * k, 1056 * k + 1056))[0])
+    prev = firsts[-1]
+    for to, name in ((-1, "DN"), (1, "DP")):
+        for j in range(2):
+            src = R("OB", 4096 * j, 4096 * j + 4096)
+            prev = send(to, lambda T, src=src: ap(T, src), lambda T, name=name, j=j: T[name][j], [src],
+                        [R(name, 64 * j, 64 * j + 64)], 1 << 20)[0]
+            ops[prev]["behind"] = firsts
+    i_, _ = send(1, lambda T: T.CB[:], lambda T: T.DC[:], [R("CB", 0, 256)], [R("DC", 0, 256)], 65536)
+    ops[i_]["behind"] = firsts
+    dma("sync", lambda T: [(T.CU[1:128:16, :], T.DC[:])], [R("DC", 0, 256)], [CUW], 65536)
+
+    for a, b in ((256, 512), (512, 1024), (1024, 2048), (2048, 3072), (3072, WE)):
+        base = 2048 if a >= 2048 else a
+        act(R("SB", a, b), R("SB", a - base, b - base), bias=float(2 * base))
+    pieces = [(1020 * j, 1020 * j + 1020) for j in range(4)]
+    for name, co in (("WO", CO_O), ("WN", CO_N), ("WP", CO_P)):
+        for a, b in pieces:
+            ts(R(name, a, b), R("SB", a, b), co[1], co[0], AL.mult, AL.add, low=(name != "WO"))
+    for j in range(8):
+        o = R("WO", WE + 512 * j, min(2 * WE, WE + 512 * j + 512))
+        ops[iota(o, [[2, count(o)]], 1024 * j + 1, 0)]["behind"] = [prev]
+        act(o, o, scale=CO_O[1], low=True)
+        act(o, o, func=AF.Identity, bias=CO_O[0], low=True)
+
+    def table(buf):
+        return R(buf, 0, 4096), R(buf, 4096, 8192)
+
+    def load_table(buf, src, shifted):
+        for j in range(2):
+            def pairs(T, j=j):
+                s = T[("te", "sa")[j]] if src is None else T[src][j]
+                o = T[buf]
+                a, b = 4096 * j, 4096 * j + 4096
+                if not shifted:
+                    return [(o[:, a:b], s[:, :])]
+                if src is None:
+                    return []
+                return [(o[0:112, a:b], T[src][j, 16:128, :]), (o[112:128, a:b], T[src][j, 0:16, :])]
+            dma("pool", pairs, [] if src is None else [R(src, 64 * j, 64 * j + 64)], [R(buf, 4096 * j, 4096 * j + 4096)], 1 << 21)
+
+    def put_new(buf, k, src):
+        for j in range(2):
+            a = 4096 * j + 2048 * k
+            act(R(buf, a, a + 2048, 4), sub(src, 512 * j, 512 * j + 512))
+
+    def offsets(c, lo, hi):
+        cp(sub(c["OF"], lo, hi), sub(c["PV"], lo, hi))
+
+    def vote(c, sg):
+        pv = sub(c["PV"], 128, 192)
+        mm([(pv, [(sub(Z8, 8 - m, 136 - m), sub(c["yes"], m, 512, 8)) for m in range(8)])])
+        act(sg, pv, func=AF.Sign, bias=-8.5)
+
+    def minus(bank, w, v, first):
+        cols = count(bank)
+        n = max(1, OPT["pieces"] * cols // 512) if width(v) == 4 else 1
+        for j in range(n):
+            a, b = cols * j // n, cols * (j + 1) // n
+            i = mm([(sub(bank, a, b), [(w, (v[0], v[1] + a * v[3], v[1] + (b - 1) * v[3] + 1, v[3]))])], first and j == 0, (not first) and j == n - 1)
+            if first and OPT["hold"] and bank[0][-1] in held:
+                ops[i]["behind"] = [held[bank[0][-1]]]
+
+    def hop(c, rnd, h, tabs, W, co, T1, S1, dl, dx, base, L, nbase, cast_row):
+        Tt, St = tabs
+        OF, PV, PS, PK, PT, VT, VS = c["OF"], c["PV"], c["PS"], c["PK"], c["PT"], c["VT"], c["VS"]
+        off1, off, x, sel = [sub(OF, 32 * n, 32 * n + 32) for n in range(4)]
+        p1, p0, px, psel = [sub(PV, 32 * n, 32 * n + 32) for n in range(4)]
+        neg = I[-1.0] if width(S1) == 2 else FIn
+        dpart = [(I[8.0], dl)] + dx
+        l = dl
+        act(PT, T1)
+        dT = slot(VT, 3)
+        phase[0] = 2 * (3 * rnd + h)
+        for s in (16, 8, 4, 2, 1):
+            step[:] = ["ab"[rnd], 0]
+            if OPT["search%d" % rnd] == "pe":
+                Sg = c["Sgb"] if rnd == 0 else slot(VS, 3)
+                hv = [(sub(PS, 0, 256), 0, 256), (sub(PK, 0, 256), 256, 512)] if OPT["halves"] else [(PS, 0, 512)]
+                cut = 512 - OPT["share%d" % rnd]
+                if cut < 512:
+                    sd = sub(slot(VS, 2), cut, 512)
+                    tt(sd, IND(St, sub(off, cut // 16, 32)), sub(S1, cut, 512), AL.subtract)
+                    act(sub(PK, cut - 256, 256), sd, scale=co[2])
+                for bank, a, b in hv:
+                    b = min(b, cut)
+                    if a == b:
+                        continue
+                    bank = sub(bank, 0, b - a)
+                    minus(bank, neg, sub(S1, a, b), True)
+                    act(sub(Sg, a, b), IND(St, sub(off, a // 16, b // 16)))
+                    minus(bank, I[1.0] if rnd == 0 else FIp, sub(Sg, a, b), False)
+                    act(bank, bank, scale=co[2])
+            else:
+                hv = [(PS, 0, 512)]
+                Sg = slot(VS, 3)
+                tt(Sg, IND(St, off), S1, AL.subtract)
+                act(PS, Sg, scale=co[2])
+            if s in OPT["tact"][c["k"]]:
+                act(dT, IND(Tt, off))
+                tt(dT, dT, PT, AL.subtract)
+            else:
+                tt(dT, IND(Tt, off), T1, AL.subtract)
+            tt(dT, IND(W, x), dT, AL.mult)
+            for bank, a, b in hv:
+                tt(sub(c["yes"], a, b), sub(dT, a, b), bank, AL.is_gt)
+            vote(c, c["sg2"])
+            pu = sub(PV, 192, 224)
+            mm([(pu, [(I[1.0], l)] + masked(s, c["sg2"]))])
+            ts(L, pu, 0.0, 254.0, AL.max, AL.min)
+            l = L
+            if s > 1:
+                mm([(p0, [(I[1.0], base), (I[1.0], l)]), (px, dpart + [(I[8.0], l)])])
+                offsets(c, 32, 96)
+            else:
+                mm([(p0, [(I[1.0], base), (I[1.0], l)]), (p1, [(I[1.0], base), (I[1.0], ONE), (I[1.0], l)]),
+                    (px, dpart + [(I[1.0], FOUR), (I[8.0], l)])])
+                offsets(c, 0, 96)
+        xb = dpart + [(I[1.0], FOUR), (I[8.0], l)]
+        phase[0] += 1
+        step[:] = ["c", 0]
+        ta, sa_ = slot(VT, 0), slot(VS, 0)
+        bype = OPT["slope%d" % rnd]
+        for nm, tab, lo_, b_, bank, V in (("s", St, sa_, c["sb"], PV, VS), ("t", Tt, ta, c["tb"], PK, VT)):
+            (cp if nm in OPT["lodve"] else act)(lo_, IND(tab, off))
+            if nm in bype:
+                hi_ = (c["Sgb"] if nm == "s" else c["sr4"]) if rnd == 0 else slot(V, 2)
+                act(hi_, IND(tab, off1))
+                minus(bank, FIn, lo_, True)
+                minus(bank, I[1.0] if rnd == 0 else FIp, hi_, False)
+                act(b_, bank)
+            else:
+                tt(b_, IND(tab, off1), lo_, AL.subtract)
+        for n, sg in ((1, c["sg8"]), (2, c["sg4"]), (3, c["sg2"])):
+            step[:] = ["def"[n - 1], 0]
+            if n == 1 and cast_row is None:
+                step[0] = "g"
+            if OPT["refine"] == "pe":
+                minus(PS, neg, S1, True)
+            if n == 1:
+                act(PV, PV if "s" in bype else c["sb"], scale=0.5)
+                act(PK, PK if "t" in bype else c["tb"], scale=0.5)
+            else:
+                tt(PV, c["sb"], PK, AL.mult)
+            tt(slot(VS, n), PV, sa_, AL.add)
+            if OPT["refine"] == "pe":
+                minus(PS, FIp, slot(VS, n), False)
+            else:
+                tt(PS, slot(VS, n), S1, AL.subtract)
+            act(PS, PS, scale=co[2])
+            if n == 3:
+                s8, s4, sA = c["sg8"], c["sg4"], sub(c["sAB"], 0, 32)
+                mm([(sub(PV, 224, 256), masked(1, s8) + masked(1, s4)),
+                    (sub(PV, 288, 320), [(I[1.0], SEVEN)] + masked(4, s8) + masked(2, s4))])
+                act(sA, sub(PV, 224, 256), func=AF.Sign, bias=1.0)
+                act(c["x"], sub(PV, 288, 320))
+                mm([(sub(PV, 256, 288), [(I[1.0], J1), (I[1.0], J2), (I[256.0], sA)] + masked(256, s4))])
+                act(c["low"], sub(PV, 256, 288), bias=-256.0)
+            if n > 1:
+                tt(PK, c["tb"], PK, AL.mult)
+            tt(slot(VT, n), PK, ta, AL.add)
+            dT = slot(VT, 3) if n < 3 else c["tb"]
+            if n in OPT["wact"]:
+                act(dT, IND(W, x))
+                tt(PK, slot(VT, n), PT, AL.subtract)
+                tt(dT, dT, PK, AL.mult)
+            else:
+                tt(dT, slot(VT, n), PT, AL.subtract)
+                tt(dT, IND(W, x), dT, AL.mult)
+            if n == 1 and cast_row is not None:
+                cast_of(c, off, cast_row, nbase)
+            tt(c["yes"], dT, PS, AL.is_gt)
+            if n < 3:
+                mm([(PK, [(BO, c["yes"])])])
+                sr = c["sr8"] if n == 1 else c["sr4"]
+                act(sr, PK, func=AF.Sign, bias=BK)
+            vote(c, sg)
+            if n < 3:
+                mm([(px, xb + masked(2, c["sg8"]) + (masked(1, c["sg4"]) if n == 2 else []))])
+                offsets(c, 64, 96)
+                mm([(PK, [(K4, c["sr8"])] + ([(K2, c["sr4"])] if n == 2 else []))])
+        s8, s4, s2 = c["sg8"], c["sg4"], c["sg2"]
+        gs = [(psel, [(I[1.0], J1), (I[1.0], J2)] + masked(768, s2))]
+        lo = 96
+        if h < 2:
+            gs += [(p0, [(I[1.0], nbase), (I[1.0], l)]), (px, [(I[16.0], l), (I[0.5], c["x"])] + masked(0.5, s2))]
+            lo = 32
+        mm(gs)
+        tt(psel, psel, c["low"], AL.max)
+        offsets(c, lo, 128)
+        mm([(sub(PV, 288, 320), [(I[1.0], c["x"])] + masked(1, s2))])
+        act(c["dq"], sub(PV, 288, 320))
+        for a, b in (((0, 256), (256, 512)) if OPT["halves"] else ((0, 512),)):
+            act(sub(c["S1"], a, b), IND(VS, sub(sel, a // 16, b // 16)))
+        (cp if OPT["seldve"] else act)(c["T1"], IND(VT, sel))
+        step[0] = "-"
+
+    def relax(c, oldT, oldS):
+        minus(c["PS"], I[-1.0] if width(oldS) == 2 else FIn, oldS, True)
+        minus(c["PS"], FIp, c["S1"], False)
+        act(c["PS"], c["PS"], scale=0.25)
+        tt(c["sb"], c["PS"], oldS, AL.add)
+        tt(c["PK"], c["T1"], oldT, AL.subtract)
+        act(c["PK"], c["PK"], scale=0.25)
+        tt(c["tb"], c["PK"], oldT, AL.add)
+
+    half = lambda c: [(I[0.5], c["dq"])]
+    WOE, WOF, WNn, WPp = R("WO", 0, WE), R("WO", 0, 2 * WE), R("WN", 0, WE), R("WP", 0, WE)
+    fl = [[R("FL", 1056 * k + a, 1056 * k + b) for a, b in ((0, 512), (512, 1024), (1024, 1056))] for k in range(2)]
+    lnd = [R("LND", 1056 * k, 1056 * k + 1056) for k in range(2)]
+    new = [R("CH%d" % k, 4096, 5120) for k in range(2)]
+
+    load_table("SA", "DN", True)
+    for k, c in enumerate(C):
+        mm([(sub(c["PV"], 32, 64), [(I[1.0], DL0), (I[1.0], fl[k][2])]), (sub(c["PV"], 64, 96), [(I[16.0], DL0)])])
+        offsets(c, 32, 96)
+        hop(c, 0, 0, table("OB"), WOE, CO_O, fl[k][0], fl[k][1], DL0, [], fl[k][2], c["L0"], c["B0"], 0)
+    load_table("SB", "DP", False)
+    for k, c in enumerate(C):
+        hop(c, 0, 1, table("SA"), WNn, CO_N, c["T1"], c["S1"], c["L0"], half(c), c["B0"], c["L1"], HB[k], None)
+    load_table("SA", None, False)
+    for k, c in enumerate(C):
+        hop(c, 0, 2, table("SB"), WPp, CO_P, c["T1"], c["S1"], c["L1"], half(c), HB[k], c["L0"], None, None)
+    for k, c in enumerate(C):
+        relax(c, fl[k][0], fl[k][1])
+        sbsend(-1, c["sb"], sub(lnd[k], 512, 1024), relay=R("SA", 512 * k, 512 * k + 512))
+        c["sent"] = sbsend(-1, c["tb"], sub(lnd[k], 0, 512))[0]
+        pd = sub(c["PV"], 352, 384)
+        mm([(pd, [(I[1.0], H1), (I[1.0], H2), (I[8.0], c["L0"]), (I[0.5], c["dq"])])])
+        di, dj = R("CI", 128 * k, 128 * k + 32), R("CI", 128 * k + 32, 128 * k + 64)
+        d2, d3, = R("CI", 128 * k + 64, 128 * k + 96), R("CI", 128 * k + 96, 128 * k + 128)
+        cp(di, pd)
+        ts(dj, di, 4, None, AL.arith_shift_right)
+        ts(d2, di, 15, None, AL.bitwise_and)
+        ts(d3, di, 1, None, AL.bitwise_and)
+        cp(c["L1"], dj)
+        cp(c["dq"], d2)
+        cp(c["par"], d3)
+        ts(dj, di, 1, None, AL.arith_shift_right)
+        ts(d3, d2, 1, None, AL.arith_shift_right)
+        cp(DH[k], dj)
+        cp(c["dqh"], d3)
+    for k, c in enumerate(C):
+        put_new("SB", k, new[k])
+    for k, c in enumerate(C):
+        i_, _ = send(2, lambda T, k=k: ap(T, new[k]), lambda T, k=k: T.DU[k], [new[k]], [R("DU", 64 * k, 64 * k + 64)], 1 << 19)
+        ops[i_]["behind"] = [C[0]["sent"], C[1]["sent"]]
+        i_ = dma("sync", lambda T, k=k: [(T.DS[k], ap(T, new[k]))], [new[k]], [R("DS", 64 * k, 64 * k + 64)], 1 << 19,
+                 after=[C[1]["sent"]])
+
+    odd = lambda c: [(I[1.0], c["dqh"]), (I[4080.0], c["par"])]
+    for k, c in enumerate(C):
+        PV, OF, VT, VS = c["PV"], c["OF"], c["VT"], c["VS"]
+        dl = c["L1"]
+        mm([(sub(PV, 0, 32), [(I[1.0], HB0), (I[1.0], ONE), (I[1.0], dl)]), (sub(PV, 32, 64), [(I[1.0], HB0), (I[1.0], dl)]),
+            (sub(PV, 64, 96), [(I[16.0], dl)] + odd(c)), (sub(PV, 96, 128), [(I[1.0], c["dq"])])])
+        offsets(c, 0, 128)
+        cast_of(c, sub(OF, 32, 64), 1, c["B0"], sub(CUW, 2048 * k, 2048 * k + 2048))
+        homes = [sub(t_, 2048 * k, 2048 * k + 2048) for t_ in table("SB")]
+        for V, tab, o, bank in ((VS, homes[1], c["S1"], c["PS"]), (VT, homes[0], c["T1"], c["PK"])):
+            act(slot(V, 0), IND(tab, sub(OF, 32, 64)))
+            tt(slot(V, 1), IND(tab, sub(OF, 0, 32)), slot(V, 0), AL.subtract)
+            act(bank, slot(V, 0))
+            tt(slot(V, 1), IND(KT, sub(OF, 96, 128)), slot(V, 1), AL.mult)
+            tt(o, bank, slot(V, 1), AL.add)
+        mm([(sub(PV, 32, 64), [(I[1.0], c["B0"]), (I[1.0], dl)])])
+        offsets(c, 32, 64)
+    for k in range(2):
+        put_new("SA", k, lnd[k])
+    load_table("SB", "DN", True)
+    for k in range(2):
+        dma("sync", lambda T, k=k: [(T.LND[0:112, 1056 * k:1056 * k + 1024], T.DU[k, 16:128, :]),
+                                    (T.LND[112:128, 1056 * k:1056 * k + 1024], T.DU[k, 0:16, :])],
+            [R("DU", 64 * k, 64 * k + 64)], [sub(lnd[k], 0, 1024)], 1 << 19)
+        put_new("SB", k, lnd[k])
+    for k, c in enumerate(C):
+        hop(c, 1, 0, table("SA"), WOF, CO_O, c["T1"], c["S1"], c["L1"], odd(c), c["B0"], c["L0"], c["B1"], 0)
+    load_table("SA", "DP", False)
+    for k in range(2):
+        dma("sync", lambda T, k=k: [(T.LND[:, 1056 * k:1056 * k + 1024], T.DS[k])],
+            [R("DS", 64 * k, 64 * k + 64)], [sub(lnd[k], 0, 1024)], 1 << 19)
+        put_new("SA", k, lnd[k])
+    free = [len(ops) - 1, len(ops) - 2, len(ops) - 4, len(ops) - 5]
+    _, credit = send(1, None, None, [], [], 0, after=free)
+    for k, c in enumerate(C):
+        hop(c, 1, 1, table("SB"), WNn, CO_N, c["T1"], c["S1"], c["L0"], half(c), c["B1"], c["L1"], HB[k], None)
+    for k, c in enumerate(C):
+        hop(c, 1, 2, table("SA"), WPp, CO_P, c["T1"], c["S1"], c["L1"], half(c), HB[k], c["L0"], None, None)
+        pd = sub(c["PV"], 352, 384)
+        mm([(pd, [(I[8.0], c["L0"]), (I[0.5], c["dq"])])])
+        tt(DH[k], pd, DH[k], AL.add)
+        add("dve", 80.0, lambda g, T, c=c, k=k: g.vector.transpose(ap(T, c["D"]), ap(T, DH[k])), [DH[k]], [c["D"]])
+        ld = sub(lnd[k], 1024, 1056)
+        sbsend(-1, c["D"], ld)
+        dma("sync", lambda T, k=k, ld=ld: [(T.yd[gg, 512 * k:512 * k + 512],
+                                           T.LND[32 * (gg // 2):32 * (gg // 2) + 32, ld[1] + 16 * (gg % 2):ld[1] + 16 * (gg % 2) + 16])
+                                          for gg in range(8)], [ld], [], 16384)
+        relax(c, R("SA", 2048 * k + 1, 2048 * k + 2048, 4), R("SA", 4096 + 2048 * k + 1, 4096 + 2048 * k + 2048, 4))
+        for j, name, q in ((1, "ys", "sync"), (0, "yt", "act")):
+            ld = sub(lnd[k], 512 * j, 512 * j + 512)
+            sbsend(-1, sub(new[k], 512 * j, 512 * j + 512), ld, after=[credit],
+                   relay=R("SA", 1024 + 512 * k, 1536 + 512 * k) if j else None)
+            dma(q if k == 1 else "sync", lambda T, k=k, ld=ld, name=name: [(T[name][:, 512 * k:512 * k + 512], ap(T, ld))], [ld], [], 1 << 18)
+    return ops
+
+
+QUEUE = {"pe": "pe", "act": "act", "dve": "dve", "pool": "pool", "sync": "sync"}
+
+
+def schedule(ops):
+    n = len(ops)
+    succ = [[] for _ in ops]
+    for i, o in enumerate(ops):
+        o["pre"] = set(o["deps"]) | set(o.get("behind", ()))
+        for j in o["pre"]:
+            succ[j].append(i)
+    lat = OPT["lat"]
+    prio = [0.0] * n
+    for i in range(n - 1, -1, -1):
+        o = ops[i]
+        prio[i] = o["dur"] + o["lat"] + max([prio[s] + lat for s in succ[i]] or [0.0])
+    for i, o in enumerate(ops):
+        prio[i] += (OPT["lead"][o["phase"]] if o["lead"] else 0.0) + OPT["bias"].get(o["cls"], 0.0)
+    left = [len(o["pre"]) for o in ops]
+    ready = {e: [] for e in ("pe", "act", "dve", "pool", "sync", "none")}
+    est = [0.0] * n
+    for i, o in enumerate(ops):
+        if not left[i]:
+            ready[o["eng"]].append(i)
+    free = {e: 0.0 for e in ready}
+    res = {}
+    order = []
+    while len(order) < n:
+        best = None
+        for e, lst in ready.items():
+            if lst:
+                t0 = max(free[e], min(est[i] for i in lst))
+                if best is None or t0 < best[0]:
+                    best = (t0, e)
+        t0, e = best
+        cand = [i for i in ready[e] if est[i] <= t0 + OPT["slack"].get(e, 0.0)]
+        i = max(cand, key=lambda j: (prio[j], -j))
+        ready[e].remove(i)
+        o = ops[i]
+        s = max(t0, est[i])
+        o["start"] = s
+        issued = s + o["dur"]
+        if e != "none":
+            free[e] = issued
+        end = issued + o["lat"]
+        if "res" in o:
+            r0 = max(res.get(o["res"], 0.0), issued)
+            res[o["res"]] = r0 + o["busy"]
+            end = r0 + o["lat"]
+        o["end"] = end
+        order.append(i)
+        for j in succ[i]:
+            p = ops[j]
+            kind = p["deps"].get(i)
+            if kind is None or not needs_wait(o, p, kind):
+                t = issued
+            else:
+                t = end + lat
+            est[j] = max(est[j], t)
+            left[j] -= 1
+            if not left[j]:
+                ready[p["eng"]].append(j)
+    return order
+
+
+def improve(sets, order):
+    n = len(order)
+    eng = [o["eng"] for o in sets[0]]
+    pre = [sets[0][i]["pre"] for i in range(n)]
+    waits = [[(j, o["deps"].get(j) is not None and needs_wait(sets[0][j], o, o["deps"][j])) for j in sorted(o["pre"])] for o in sets[0]]
+    seed = [12345]
+
+    def rand():
+        seed[0] = (seed[0] * 1103515245 + 12345) % 2147483648
+        return (seed[0] >> 8) / 8388608.0
+
+    def frame(ops, lat, a, b):
+        st, tot, free, res = [0.0] * n, [0.0] * n, {}, {}
+        first = {}
+        for pos, i in enumerate(order):
+            if pos == a:
+                first = dict(free)
+            o = ops[i]
+            t = free.get(eng[i], 0.0)
+            for j, w in waits[i]:
+                t = max(t, st[j] + (tot[j] + lat if w else ops[j]["dur"]))
+            st[i] = t
+            tot[i] = o["dur"] + o["lat"]
+            if eng[i] != "none":
+                free[eng[i]] = t + o["dur"]
+            if "res" in o:
+                r0 = max(res.get(o["res"], 0.0), t + o["dur"])
+                res[o["res"]] = r0 + o["busy"]
+                tot[i] += r0 - t - o["dur"]
+        tail, nxt = list(tot), {}
+        for i in reversed(order[b:]):
+            if eng[i] != "none":
+                tail[i] = max(tail[i], ops[i]["dur"] + nxt.get(eng[i], 0.0))
+                nxt[eng[i]] = tail[i]
+            for j, w in waits[i]:
+                tail[j] = max(tail[j], (tot[j] + lat if w else ops[j]["dur"]) + tail[i])
+        inside = set(order[a:b])
+        head, edge = {}, {}
+        for i in inside:
+            head[i] = max([st[j] + (tot[j] + lat if w else ops[j]["dur"]) for j, w in waits[i] if j not in inside] + [first.get(eng[i], 0.0)])
+            edge[i] = [(j, tot[j] + lat if w else ops[j]["dur"]) for j, w in waits[i] if j in inside]
+            if eng[i] != "none":
+                tail[i] = max(tail[i], ops[i]["dur"] + nxt.get(eng[i], 0.0))
+        return head, edge, tail, [o["dur"] for o in ops]
+
+    def walk(win, fr):
+        head, edge, tail, dur = fr
+        st, par, last = {}, {}, {}
+        top, at = 0.0, -1
+        for i in win:
+            t, p = head[i], -1
+            for j, w in edge[i]:
+                v = st[j] + w
+                if v > t:
+                    t, p = v, j
+            e = eng[i]
+            j = last.get(e)
+            if j is not None and e != "none":
+                v = st[j] + dur[j]
+                if v >= t:
+                    t, p = v, -2 - j
+            last[e] = i
+            st[i], par[i] = t, p
+            if t + tail[i] > top:
+                top, at = t + tail[i], i
+        return top, at, par
+
+    size = 300
+    for sweep in range(OPT["sweeps"]):
+        for a in range(0, n - size // 3, size // 2):
+            b = min(n, a + size)
+            frs = [frame(ops, m["lat"], a, b) for ops, m in zip(sets, GUESS)]
+            win = order[a:b]
+            cur = [walk(win, fr) for fr in frs]
+            score = sum(c[0] for c in cur)
+            best = (score, win)
+            for move in range(OPT["moves"]):
+                c = cur[int(rand() * len(cur))]
+                i, pairs = c[1], []
+                while i != -1:
+                    p = c[2][i]
+                    if p <= -2:
+                        p = -2 - p
+                        if p not in pre[i]:
+                            pairs.append((p, i))
+                    i = p
+                if not pairs:
+                    continue
+                u, v = pairs[int(rand() * len(pairs))]
+                x, y = win.index(u), win.index(v)
+                front = [v]
+                for z in reversed(win[x:y]):
+                    if any(z in pre[f] or (eng[z] == eng[f] and f != v and eng[z] != "none") for f in front):
+                        front.append(z)
+                if u in front:
+                    continue
+                new = win[:x] + front[::-1] + [z for z in win[x:y] if z not in front] + win[y + 1:]
+                res = [walk(new, fr) for fr in frs]
+                s = sum(r[0] for r in res)
+                if s < score - OPT["heat"] * math.log(rand() + 1e-9) * (1.0 - move / OPT["moves"]):
+                    win, cur, score = new, res, s
+                    if s < best[0]:
+                        best = (s, new)
+            order[a:b] = best[1]
+    return order
+
+
+GUESS = [{"g": 1.56, "f": 1.25, "pe": 0.42, "lat": 100.0, "link": 70.0},
+         {"g": 1.3, "f": 1.25, "pe": 0.42, "lat": 220.0, "link": 70.0},
+         {"g": 1.3, "f": 1.1, "pe": 0.38, "lat": 60.0, "link": 100.0}]
+
+
+def needs_wait(o, p, kind):
+    if o["kind"] == "c" and p["kind"] == "c" and o["eng"] == p["eng"]:
+        if o["eng"] == "pe":
+            return False
+        return kind == "raw"
+    return True
+
+
+PLAN = {}
+
+
+def plan():
+    if not PLAN:
+        sets = []
+        for m in GUESS[::-1]:
+            OPT.update(m)
+            sets.append(build())
+        PLAN["ops"] = sets[-1]
+        PLAN["order"] = improve(sets[::-1], schedule(sets[-1]))
+    return PLAN["ops"], PLAN["order"]
+
+
+def rank_program(g, core, T, topo):
+    rank = T.rank_of(core)
+    cores = T.cores
+    n = len(cores)
+    ops, order = plan()
+
+    def helper(src, dst):
+        if topo.chip(src) == topo.chip(dst):
+            return None
+        for h in topo.cores_of(src):
+            if h not in cores and topo.die(h) != topo.die(src) and topo.may_write(h, dst):
+                return h
+        return None
+
+    def spare(src, h, dst):
+        return [e for e in topo.engines(src, h) if e not in topo.engines(src, dst)]
+
+    if rank is None:
+        ends = []
+        for i in order:
+            o = ops[i]
+            if o["kind"] != "send" or "relay" not in o:
+                continue
+            for r in range(n):
+                src, dst = cores[r], cores[(r + o["to"]) % n]
+                if helper(src, dst) == core:
+                    rid, pid, _ = topo.addr(dst)
+                    g.wait_ge(T.sem[o["hsem"]], len(spare(src, core, dst)))
+                    g.remote_dma(o["fn"][1](T), ap(T, o["relay"]), T.sem[o["rsem"]], T.sem[o["sem"]], pid, rid, topo.mask(core, dst))
+                    ends.append((o["sem"], len(topo.engines(core, dst))))
+        for sem, cnt in ends:
+            g.wait_ge(T.sem[sem], cnt)
+        return
+    queue = {"pe": g.tensor, "act": g.scalar, "dve": g.vector, "pool": g, "sync": g.sync}
+    known = {e: {} for e in queue}
+    done = {}
+    counter = {e: 0 for e in queue}
+    total = {}
+    for i in order:
+        o = ops[i]
+        e = o["eng"]
+        if o["kind"] == "recv":
+            src = cores[(rank - o["to"]) % n]
+            if "relay" in o and helper(src, core) is not None:
+                src = helper(src, core)
+            cnt = len(topo.engines(src, core))
+            done[i] = (o["sem"], cnt, {})
+            total[o["sem"]] = cnt
+            continue
+        kn = known[e]
+        need = [done[j] for j, kind in o["deps"].items() if needs_wait(ops[j], o, kind)]
+        for sem, cnt, clock in sorted(need, key=lambda d: -len(d[2])):
+            top = max(d[1] for d in need if d[0] == sem)
+            if cnt == top and kn.get(sem, 0) < cnt:
+                queue[e].wait_ge(T.sem[sem], cnt)
+                kn[sem] = cnt
+                for s, v in clock.items():
+                    if kn.get(s, 0) < v:
+                        kn[s] = v
+        if o["kind"] == "c":
+            counter[e] += 1
+            sem, cnt = "c_" + e, counter[e]
+            o["fn"](g, T).then_inc(T.sem[sem], 1)
+        elif o["kind"] == "dma":
+            pairs = o["fn"](T)
+            sem, cnt = o["sem"], 16 * len(pairs)
+            for out, src in pairs:
+                queue[e].dma_start(out, src).then_inc(T.sem[sem], 16)
+        else:
+            dst = cores[(rank + o["to"]) % n]
+            rid, pid, _ = topo.addr(dst)
+            sem, cnt = o["sem"], len(topo.engines(core, dst))
+            src, land = o["fn"]
+            h = helper(core, dst) if "relay" in o else None
+            if h is not None:
+                rid, pid, _ = topo.addr(h)
+                es = spare(core, h, dst)
+                cnt = len(es)
+                g.remote_dma(ap(T, o["relay"]), src(T), T.sem[o["hsem"]], T.sem[sem], pid, rid, sum(1 << x for x in es))
+            elif src is None:
+                g.remote_sem_update(T.sem[o["rsem"]], T.sem[sem], pid, rid, topo.mask(core, dst))
+            else:
+                g.remote_dma(land(T), src(T), T.sem[o["rsem"]], T.sem[sem], pid, rid, topo.mask(core, dst))
+        done[i] = (sem, cnt, dict(kn))
+        total[sem] = cnt
+    waited = {}
+    for kn in known.values():
+        for s, v in kn.items():
+            waited[s] = max(waited.get(s, 0), v)
+    for sem, cnt in total.items():
+        if waited.get(sem, 0) < cnt:
+            g.sync.wait_ge(T.sem[sem], cnt)

@@ -3,37 +3,44 @@ from concourse.mybir import AluOpType, ActivationFunctionType
 
 AL = AluOpType
 AF = ActivationFunctionType
-NC, NW = 512, 32
 WE = 4080
+NCH, NC, WM = 2, 512, 32
+STEPS = (16, 8, 4, 2, 1)
 
-OPT = {"search0": "pe", "search1": "pe", "refine": "pe", "bias": {}, "relay": True, "sweeps": 3, "heat": 100.0, "moves": 800, "lodve": "", "seldve": False, "wact": (1, 2, 3), "share0": 0, "share1": 128, "hold": False, "slope0": "", "slope1": "", "halves": True, "pieces": 2, "lead": [2500.0] * 12,
-       "tact": ((), ()), "slack": {"dve": 100.0, "act": 450.0, "pe": 300.0},
-       "g": 1.56, "f": 1.0, "pe": 0.42, "lat": 80.0, "link": 70.0, "hbm": 250.0}
+MODES = {
+    (0, 0): (("1A", "1A", "1A", "1A", "1A"), ("ba", "ba", "ba"), "pp"),
+    (0, 1): (("1AC", "1AC", "1AC", "1AC", "1AC"), ("ba", "ba", "ba"), "pp"),
+    (0, 2): (("1AC", "1AC", "1AC", "1AC", "1AC"), ("ba", "ba", "ba"), "pp"),
+    (1, 0): (("1CB", "1C", "1C", "1C", "1CB"), ("ea", "ea", "ea"), "ww"),
+    (1, 1): (("1CB", "1C", "1C", "1C", "1CB"), ("ea", "ea", "ea"), "ww"),
+    (1, 2): (("1CB", "1C", "1C", "1C", "1CB"), ("ea", "ea", "ea"), "ww"),
+}
+OPT = {"sweeps": 8, "heat": 500.0, "moves": 400, "size": 160, "lead": [1500.0] * 6, "pieces": 2, "pslope": "", "back": 0.5, "slack": {"dve": 100.0, "act": 450.0, "pe": 300.0},
+       "wdve": (0, 0, 1), "step1": "wp", "relax": ("pp", "vp"), "halves": 1, "strict": False, "early": True, "relay": (384, 384),
+       "g": 1.56, "f": 1.0, "pe": 0.42, "lat": 120.0, "link": 70.0, "hbm": 250.0}
 
-MS = (16, 8, 4, 2, 1, 256, 768, 0.5)
-IS = (1.0, 8.0, 16.0, 0.5, 256.0, 4080.0, -1.0)
-MT_COLS = 128 * (2 * len(MS) + len(IS) + 3) + 144 * 3
 SCRATCH = {
     "SA": ("sbuf", [128, 8192], "float32"), "SB": ("sbuf", [128, 8192], "float32"),
     "WO": ("sbuf", [128, 2 * WE], "float32"), "WN": ("sbuf", [128, WE], "float32"), "WP": ("sbuf", [128, WE], "float32"),
-    "CH0": ("sbuf", [128, 6176], "float32"), "CH1": ("sbuf", [128, 6176], "float32"),
-    "LND": ("sbuf", [128, 2112], "float32"), "FI": ("sbuf", [128, 256], "float32"),
-    "CO": ("sbuf", [128, 16], "float32"), "SM": ("sbuf", [128, 192], "float32"),
+    "LND": ("sbuf", [128, 2048], "float32"), "FIN": ("sbuf", [128, 2048 + 32 * NCH], "float32"),
+    "FI": ("sbuf", [128, 256], "float32"), "CO": ("sbuf", [128, 32], "float32"), "SM": ("sbuf", [128, 192], "float32"),
     "OB": ("sbuf", [128, 8192], "bfloat16"), "CU": ("sbuf", [128, 4096], "bfloat16"),
-    "AR0": ("sbuf", [128, 2080], "bfloat16"), "AR1": ("sbuf", [128, 2080], "bfloat16"),
-    "FL": ("sbuf", [128, 2112], "bfloat16"), "MT": ("sbuf", [128, MT_COLS], "bfloat16"),
-    "WS0": ("sbuf", [128, 512], "bfloat16"), "WS1": ("sbuf", [128, 512], "bfloat16"),
-    "ST": ("sbuf", [128, 608], "bfloat16"), "CB": ("sbuf", [128, 256], "bfloat16"),
-    "OF0": ("sbuf", [128, 128], "uint16"), "OF1": ("sbuf", [128, 128], "uint16"), "OFS": ("sbuf", [128, 64], "uint16"),
-    "CI": ("sbuf", [128, 256], "int32"), "PI": ("sbuf", [128, 4], "int32"),
-    "DN": ("dram", [2, 128, 4096], "bfloat16"), "DP": ("dram", [2, 128, 4096], "bfloat16"),
-    "DC": ("dram", [128, 256], "bfloat16"),
-    "DU": ("dram", [2, 128, 1024], "float32"), "DS": ("dram", [2, 128, 1024], "float32"),
+    "FL": ("sbuf", [128, 2048 + 32 * NCH], "bfloat16"), "MT": ("sbuf", [128, 128 * 29 + 144 * 4], "bfloat16"),
+    "ST": ("sbuf", [128, 1792], "bfloat16"), "CB": ("sbuf", [128, 256], "bfloat16"),
+    "OFS": ("sbuf", [128, 64], "uint16"), "CI": ("sbuf", [128, 256], "int32"), "PI": ("sbuf", [128, 4], "int32"),
+    "DN": ("dram", [4, 128, 2048], "bfloat16"), "DP": ("dram", [4, 128, 2048], "bfloat16"),
+    "DC": ("dram", [128, 256], "bfloat16"), "DU": ("dram", [NCH, 128, 2 * NC], "float32"),
+    "DS": ("dram", [NCH, 128, 2 * NC], "float32"),
 }
-for _k in range(2):
-    for _b in ("PS", "PV", "PT", "PK"):
+for _k in range(NCH):
+    SCRATCH["F%d" % _k] = ("sbuf", [128, 9 * NC + 32], "float32")
+    SCRATCH["B%d" % _k] = ("sbuf", [128, 4 * NC + 32], "bfloat16")
+    SCRATCH["W%d" % _k] = ("sbuf", [128, 30 * WM], "bfloat16")
+    SCRATCH["I%d" % _k] = ("sbuf", [128, 8 * WM], "int32")
+    SCRATCH["OF%d" % _k] = ("sbuf", [128, 6 * WM], "uint16")
+    for _b in ("XS", "XT", "XK", "V"):
         SCRATCH[_b + str(_k)] = ("psum", [128, 512], "float32")
-SEMAPHORES = ["c_pe", "c_act", "c_dve", "c_pool"] + ["s%d" % _i for _i in range(110)]
+SEMAPHORES = ["c_pe", "c_act", "c_dve", "c_pool"] + ["s%d" % _i for _i in range(120)]
 BYTES = {"float32": 4, "int32": 4, "bfloat16": 2, "uint16": 2}
 
 
@@ -42,7 +49,7 @@ def R(buf, a, b, step=1):
 
 
 def sub(r, a, b, step=1):
-    return (r[0], r[1] + a, r[1] + b, step)
+    return (r[0], r[1] + a * r[3], min(r[2], r[1] + b * r[3]), step * r[3])
 
 
 def IND(win, off):
@@ -82,14 +89,8 @@ def parts(rs):
 
 
 def build():
-    ops, hist, banks, nsem, phase = [], {}, {}, [0], [0]
+    ops, hist, groups, nsem, where = [], {}, {}, [0], {"phase": 0, "chunk": -1, "const": True}
     cyc = 0.83 * OPT["f"]
-    held = {}
-    step = ["-", 0]
-
-    def kind_of():
-        step[1] += 1
-        return "-" if step[0] == "-" else step[0] + str(step[1])
 
     def new_sem():
         nsem[0] += 1
@@ -98,39 +99,26 @@ def build():
     def add(eng, dur, fn, reads, writes, after=(), kind="c", lat=0.0, **kw):
         i = len(ops)
         deps = {}
+        spans = []
         for rs, wr in ((parts(reads), False), (parts(writes), True)):
             for r in rs:
-                if r[0] in SCRATCH and SCRATCH[r[0]][0] == "psum":
-                    st = banks.setdefault(r[0], {"touch": {}, "w": None})
-                    for e, j in st["touch"].items():
-                        if e != eng:
-                            deps[j] = "raw"
-                        else:
-                            deps.setdefault(j, "ord")
-                w = BYTES[SCRATCH[r[0]][2]] if r[0] in SCRATCH else 4
-                lo, hi = (r[1] * w) // 16, (r[2] * w + 15) // 16
-                for (l2, h2, j, w2, e2) in hist.get(r[0], ()):
-                    if j != i and l2 < hi and lo < h2 and (wr or w2):
-                        if w2 and not wr:
-                            deps[j] = "raw"
-                        else:
-                            deps[j] = "raw"
-        for rs, wr in ((parts(reads), False), (parts(writes), True)):
-            for r in rs:
-                if r[0] in SCRATCH and SCRATCH[r[0]][0] == "psum":
-                    banks[r[0]]["touch"][eng] = i
-                w = BYTES[SCRATCH[r[0]][2]] if r[0] in SCRATCH else 4
-                lo, hi = (r[1] * w) // 16, (r[2] * w + 15) // 16
-                h = hist.setdefault(r[0], [])
-                if wr and r[3] == 1 and (r[1] * w) % 16 == 0 and (r[2] * w) % 16 == 0:
-                    h[:] = [x for x in h if not (lo <= x[0] and x[1] <= hi)]
-                elif not wr and step[0] != "-" and r[0] in ("MT", "ST", "FI", "CO"):
-                    continue
-                h.append((lo, hi, i, wr, eng))
+                w = BYTES[SCRATCH[r[0]][2]]
+                spans.append((r, wr, w, (r[1] * w) // 16, (r[2] * w + 15) // 16))
+        for r, wr, w, lo, hi in spans:
+            for (l2, h2, j, w2) in hist.get(r[0], ()):
+                if j != i and l2 < hi and lo < h2 and (wr or w2):
+                    deps[j] = "raw"
+        for r, wr, w, lo, hi in spans:
+            h = hist.setdefault(r[0], [])
+            if wr and r[3] == 1 and (r[1] * w) % 16 == 0 and (r[2] * w) % 16 == 0:
+                h[:] = [x for x in h if not (lo <= x[0] and x[1] <= hi)]
+            elif not wr and not where["const"] and r[0] in ("MT", "ST", "FI", "CO", "SM"):
+                continue
+            h.append((lo, hi, i, wr))
         for j in after:
             deps[j] = "raw"
-        o = {"eng": eng, "dur": dur, "fn": fn, "deps": deps, "kind": kind, "lat": lat, "phase": phase[0], "cls": kind_of(),
-             "lead": any(r[0][-1] == "0" for r in parts(reads) + parts(writes))}
+        o = {"eng": eng, "dur": dur, "fn": fn, "deps": deps, "kind": kind, "lat": lat, "phase": where["phase"],
+             "chunk": where["chunk"], "banks": sorted({s[0][0] for s in spans if is_psum(s[0])})}
         o.update(kw)
         ops.append(o)
         return i
@@ -145,14 +133,14 @@ def build():
         return add("dve", dve_time(count(out), c, a[0] == "*"),
                    lambda g, T: g.vector.tensor_tensor(ap(T, out), ap(T, a), ap(T, b), op), [a, b], [out])
 
-    def ts(out, a, s1, s2, op0, op1=None, **kw):
+    def ts(out, a, s1, s2, op0, op1=None):
         c = 0.5 if (width(out) == 2 and width(a) == 2) else 1.0
 
         def fn(g, T):
             if op1 is None:
                 return g.vector.tensor_scalar(ap(T, out), ap(T, a), ap(T, s1), None, op0)
             return g.vector.tensor_scalar(ap(T, out), ap(T, a), ap(T, s1), ap(T, s2), op0, op1)
-        return add("dve", dve_time(count(out), c, a[0] == "*"), fn, [a, s1, s2], [out], **kw)
+        return add("dve", dve_time(count(out), c, a[0] == "*"), fn, [a, s1, s2], [out])
 
     def cp(out, a):
         c = 0.5 if (width(out) == 2 and width(a) == 2) else 1.0
@@ -163,31 +151,33 @@ def build():
         return add("dve", dve_time(count(out), width(out) / 4.0, False),
                    lambda g, T: g.vector.memset(ap(T, out), v), [], [out])
 
-    def act(out, a, func=None, scale=1.0, bias=0.0, **kw):
+    def act(out, a, func=None, scale=1.0, bias=0.0):
         func = func or (AF.Copy if bias == 0.0 else AF.Identity)
         n = count(out)
         d = 65.0 + n * OPT["g"] * cyc if a[0] == "*" else 60.0 + max(64, n) * cyc
         return add("act", d, lambda g, T: g.scalar.activation(ap(T, out), ap(T, a), func, bias=ap(T, bias), scale=ap(T, scale)),
-                   [a, scale, bias], [out], **kw)
+                   [a, scale, bias], [out])
 
-    def mm(groups, start=True, stop=True):
-        d = 30.0
-        rd, wr = [], []
-        for out, pairs in groups:
-            wr.append(out)
-            for l, r in pairs:
-                d += max(64, count(r)) * (4 if width(r) == 4 else 1) * OPT["pe"] * OPT["f"]
-                rd.extend([l, r])
+    def mm(items, start=True, stop=True):
+        bank = items[0][0][0]
+        d = 30.0 + sum(max(64, count(r)) * (4 if width(r) == 4 else 1) * OPT["pe"] * OPT["f"] for _, _, r in items)
+        new, head = [], None
+        for o, _, _ in items:
+            new.append(start and (head is None or head[3] > 1 or o[1] < head[1] or o[2] > head[2]))
+            head = o if new[-1] else head
 
         def fn(g, T):
             ins = None
-            for out, pairs in groups:
-                for n, (l, r) in enumerate(pairs):
-                    ins = g.tensor.matmul(ap(T, out), ap(T, l), ap(T, r), start and n == 0, stop and n == len(pairs) - 1)
+            for n, (o, l, r) in enumerate(items):
+                ins = g.tensor.matmul(ap(T, o), ap(T, l), ap(T, r), new[n], (new + [stop])[n + 1])
             return ins
-        i = add("pe", d, fn, rd, wr)
-        if start and stop:
-            held[wr[0][0][-1]] = i
+        i = add("pe", d, fn, [x for _, l, r in items for x in (l, r)], [o for o, _, _ in items])
+        if bank[0] == "X":
+            if bank in groups:
+                ops[i]["deps"].setdefault(groups[bank], "ord")
+            groups[bank] = i
+            if not stop and (OPT["strict"] or bank[1] == "K"):
+                ops[i]["deps"].update({x[2]: "raw" for x in hist[bank] if x[2] != i})
         return i
 
     def iota(out, pattern, base, cm):
@@ -201,75 +191,94 @@ def build():
         return add(q, 700.0 if q == "pool" else 100.0, pairs, reads, writes, after, "dma",
                    1800.0 + nbytes / OPT["hbm"], sem=new_sem(), res="hbm" if nbytes > 200000 else "small", busy=nbytes / OPT["hbm"])
 
-    def send(to, src, dst, src_r, dst_r, nbytes, after=(), relay=None):
-        if relay is not None and OPT["relay"]:
+    def send(to, src, dst, src_r, dst_r, nbytes, relay=None, after=()):
+        if relay is not None:
             i = add("pool", 300.0, (src, dst), src_r, [], after, "send", 1500.0 + 0.7 * nbytes / OPT["link"],
                     sem=new_sem(), rsem=new_sem(), hsem=new_sem(), relay=relay, to=to, res="relay", busy=nbytes / OPT["link"])
-            j = add("none", 0.0, None, [], dst_r, [i], "recv", 2500.0 + nbytes / OPT["link"], sem=ops[i]["rsem"], to=to, relay=relay)
-            return i, j
+            add("none", 0.0, None, [], dst_r, [i], "recv", 2500.0 + nbytes / OPT["link"], sem=ops[i]["rsem"], to=to, relay=relay)
+            return i
         i = add("pool", 300.0, (src, dst), src_r, [], after, "send", 1500.0 + nbytes / OPT["link"],
                 sem=new_sem(), rsem=new_sem(), to=to, res="link%d" % to, busy=nbytes / OPT["link"])
-        j = add("none", 0.0, None, [], dst_r, [i], "recv", 500.0, sem=ops[i]["rsem"], to=to)
-        return i, j
+        add("none", 0.0, None, [], dst_r, [i], "recv", 500.0, sem=ops[i]["rsem"], to=to)
+        return i
 
-    def sbsend(to, src, dst, after=(), relay=None):
-        return send(to, lambda T: ap(T, src), lambda T: ap(T, dst), [src], [dst], 128 * count(src) * width(src), after, relay)
+    def sbsend(to, src, dst, relay=None, after=()):
+        return send(to, lambda T: ap(T, src), lambda T: ap(T, dst), [src], [dst], 128 * count(src) * width(src), relay, after)
 
-    mt = [0]
+    used = {"MT": 0, "ST": 0, "SM": 0}
 
-    def mat(n=128):
-        mt[0] += n
-        return R("MT", mt[0] - n, mt[0])
-    I = {s: mat() for s in IS}
-    M = {(s, a): mat() for s in MS for a in (0, 1)}
-    BO, K4, K2 = mat(), mat(), mat()
-    Z8, ZC = mat(144), [mat(144), mat(144)]
+    def tile(buf, n):
+        used[buf] += n
+        return R(buf, used[buf] - n, used[buf])
+    mat = lambda: tile("MT", 128)
+    col = lambda: sub(tile("SM", 4), 0, 1)
+    I1, In, IL, IU, UP, DN_, BO, N2, N3, KC = [mat() for _ in range(10)]
+    TM = {s: mat() for s in STEPS}
+    S = {1: (IL, UP), 8: (mat(), mat())}
+    D = {1: (mat(), mat()), 8: (mat(), mat())}
+    SP = [mat() for _ in range(8)]
+    Z8, ZL, ZC = tile("MT", 144), tile("MT", 144), [tile("MT", 144), tile("MT", 144)]
     FIp, FIn = R("FI", 0, 128), R("FI", 128, 256)
-    st = [R("ST", 32 * i, 32 * i + 32) for i in range(11)]
-    ONE, FOUR, SEVEN, ZERO, J1, J2, H1, H2, DL0, HB0, HB1 = st
-    HB = (HB0, HB1)
-    IO, QG = R("ST", 352, 480), R("ST", 480, 608)
-    col = lambda i: R("SM", 4 * i, 4 * i + 1)
-    MC, PG, MK0, MK1, M4, BK, K4C, K2C, E15 = [col(i) for i in range(9)]
-    KT = R("SM", 40, 56)
-    C64 = R("SM", 64, 128)
-    DH = (R("SM", 128, 160), R("SM", 160, 192))
-    CO_O, CO_P, CO_N = [[R("CO", a + j, a + j + 1) for j in range(3)] for a in (0, 8, 12)]
+    ZT, IO, QG = tile("ST", 512), tile("ST", 128), tile("ST", 128)
+    CS = {s: tile("ST", 128) for s in STEPS}
+    CN = [tile("ST", 64) for _ in range(3)]
+    FOUR, H4, HB = tile("ST", 64), tile("ST", 64), tile("ST", 64)
+    MC, PG, MK0, MK1, M4, M8, SG, TMP = [col() for _ in range(8)]
+    BIAS = {s: col() for s in STEPS}
+    LO, HI = [col() for _ in range(3)], [col() for _ in range(3)]
+    RM = [col() for _ in range(8)]
+    C64 = tile("SM", 64)
+    CO_O, CO_P, CO_N = [[R("CO", a + j, a + j + 1) for j in range(3)] + [R("CO", b, b + 1)] for a, b in ((0, 16), (8, 20), (12, 24))]
     CUW = R("CU", 0, 4096)
-
-    def masked(s, sg):
-        return [(M[(s, 0)], sub(sg, 0, 64, 2)), (M[(s, 1)], sub(sg, 1, 64, 2))]
+    n, w, N = NC, WM, 2 * WM
 
     def chunk(k):
-        c, a, w, o = "CH%d" % k, "AR%d" % k, "WS%d" % k, "OF%d" % k
-        d = {"k": k, "VT": R(c, 0, 2048), "VS": R(c, 2048, 4096), "tb": R(c, 4096, 4608), "sb": R(c, 4608, 5120),
-             "D": R(c, 5120, 5152), "T1": R(c, 5152, 5664), "S1": R(c, 5664, 6176),
-             "Sgb": R(a, 0, 512), "yes": R(a, 512, 1024), "sr8": R(a, 1024, 1536), "sr4": R(a, 1536, 2048),
-             "first": R(a, 1024, 2080), "OF": R(o, 0, 128),
-             "PS": R("PS%d" % k, 0, 512), "PV": R("PV%d" % k, 0, 512), "PT": R("PT%d" % k, 0, 512), "PK": R("PK%d" % k, 0, 512)}
-        for n, nm in enumerate(("L0", "L1", "dq", "B0", "B1", "dqh", "par", "x")):
-            d[nm] = R(w, 32 * n, 32 * n + 32)
-        for n, nm in enumerate(("sg8", "sg4", "sg2", "sAB")):
-            d[nm] = R(w, 256 + 64 * n, 320 + 64 * n)
-        d["low"] = R("SM", 64 + 32 * k, 96 + 32 * k)
+        d = {"k": k, "i0": n * k, "held": None}
+        for j, nm in enumerate(("tb", "sb", "ta", "sa", "T1", "S1", "A", "Q", "Cw")):
+            d[nm] = R("F%d" % k, n * j, n * j + n)
+        d["new"], d["D"] = R("F%d" % k, 0, 2 * n), R("F%d" % k, 9 * n, 9 * n + 32)
+        for j, nm in enumerate(("yes", "Q16", "ta16", "sa16")):
+            d[nm] = R("B%d" % k, n * j, n * j + n)
+        d["first"], d["Cg"] = R("B%d" % k, 2 * n, 4 * n + w), d["Q16"]
+        for j, nm in enumerate(("r", "Lw", "v0", "v1", "v2", "l1", "qh", "par", "a", "lm")):
+            d[nm] = R("W%d" % k, N * j, N * j + N)
+        d["al"] = R("W%d" % k, 8 * N, 10 * N)
+        d["BH"] = [R("W%d" % k, (10 + 2 * j) * N, (12 + 2 * j) * N) for j in range(2)]
+        v, of = "V%d" % k, "OF%d" % k
+        d["VO"], d["room"], d["base"], d["V"] = R(v, 0, N), R(v, N, 3 * N), R(v, 3 * N, 5 * N), R(v, 5 * N, 6 * N)
+        d["off"], d["x"], d["off1"], d["both"] = R(of, 0, w), R(of, w, N), R(of, N, N + w), R(of, 0, N)
+        d["XS"], d["XT"], d["K"] = R("XS%d" % k, 0, n), R("XT%d" % k, 0, n), R("XK%d" % k, 0, n)
+        f0 = (2 * n + w) * k
+        d["fT"], d["fS"], d["fC"], d["fl"] = R("FL", f0, f0 + n), R("FL", f0 + n, f0 + 2 * n), R("FL", f0 + 2 * n, f0 + 2 * n + w), R("FL", f0, f0 + 2 * n + w)
+        d["lnd"] = R("LND", 2 * n * k, 2 * n * k + 2 * n)
+        d["kept"], d["finD"] = R("FIN", 2 * n * k, 2 * n * k + 2 * n), R("FIN", 2048 + w * k, 2048 + w * k + w)
+        d["of"] = R(of, 0, 3 * w)
+        d["own"] = dict(d, of=R(of, 3 * w, 6 * w), off=R(of, 3 * w, 4 * w), off1=R(of, 5 * w, 6 * w), v2=R("W%d" % k, 14 * N, 15 * N),
+                        ta=sub(d["kept"], 0, n), sa=sub(d["kept"], n, 2 * n), tb=sub(d["lnd"], 0, n), sb=sub(d["lnd"], n, 2 * n))
         return d
-    C = [chunk(0), chunk(1)]
-    slot = lambda v, n: sub(v, 512 * n, 512 * n + 512)
+    C = [chunk(k) for k in range(NCH)]
+
+    def each():
+        for c in C:
+            where["chunk"] = c["k"]
+            yield c
+        where["chunk"] = -1
 
     ld_cu = dma("sync", lambda T: [(T.CI[:], T.cu[:])], [], [R("CI", 0, 256)], 131072)
     ld_co = dma("act", lambda T: [(T.CO[:, 0:3], T.co[:]), (T.CO[0:112, 4:7], T.co[16:128, :]), (T.CO[112:128, 4:7], T.co[0:16, :])],
                 [], [R("CO", 0, 8)], 4096)
     before = [ld_cu, ld_co]
-    for hf in range(2):
-        for q, name, a in (("sync", "te", 0), ("act", "sa", 4096)):
-            i_ = dma(q, lambda T, name=name, a=a, hf=hf: [(T.OB[:, a + 2048 * hf:a + 2048 * hf + 2048], T[name][:, 2048 * hf:2048 * hf + 2048])],
-                     [], [R("OB", a + 2048 * hf, a + 2048 * hf + 2048)], 524288)
+    for c in C:
+        a, b = 4 * c["i0"], 4 * c["i0"] + 4 * n
+        for q, name, o in (("sync", "te", 0), ("act", "sa", 4096)):
+            i_ = dma(q, lambda T, name=name, a=a, b=b, o=o: [(T.OB[:, o + a:o + b], T[name][:, a:b])], [], [R("OB", o + a, o + b)], 256 * (b - a))
             ops[i_]["behind"] = list(before)
             before.append(i_)
     sbsend(-1, R("CO", 4, 7), R("CO", 12, 15))
     sbsend(1, R("CO", 0, 3), R("CO", 8, 11))
 
     ms(CUW, 0.0)
+    ms(ZT, 0.0)
     cp(R("CB", 0, 256), R("CI", 0, 256))
     dma("sync", lambda T: [(T.CU[0:128:16, :], T.CB[:])], [R("CB", 0, 256)], [CUW], 65536)
     iota(MC, [[0, 1]], 0, 1)
@@ -277,375 +286,438 @@ def build():
     iota(IO, [[1, 128]], 0, -1)
     iota(QG, [[1, 8], [0, 16]], 0, 0)
     iota(R("SB", 0, 256), [[2, 256]], 0, 0)
-    iota(H1, [[0, 8], [512, 4]], 0, 0)
-    iota(J1, [[16, 32]], 768, 0)
-    for k in range(2):
-        iota(HB[k], [[256, 8], [0, 4]], 2048 * k, 0)
-    iota(KT, [[1, 16]], 0, 0)
+    iota(H4, [[0, 8], [32, 8]], 0, 0)
+    iota(HB, [[256, 16], [0, 4]], 0, 0)
     ts(PG, MC, -7.5, 0.0625, AL.add, AL.mult)
     PGI = R("PI", 0, 1)
     cp(PGI, PG)
     cp(PG, PGI)
-    ts(E15, PG, -16.0, None, AL.mult)
-    tt(MC, MC, E15, AL.add)
+    ts(TMP, PG, -16.0, None, AL.mult)
+    tt(MC, MC, TMP, AL.add)
     ts(M4, MC, 4.0, None, AL.mult)
     ts(R("OFS", 0, 64), C64, M4, None, AL.add)
-    for s in IS:
-        ts(I[s], IO, 0.0, s, AL.is_equal, AL.mult)
+    ts(I1, IO, 0.0, None, AL.is_equal)
     for r in range(2):
         ms(ZC[r], 0.0)
-        cp(sub(ZC[r], 16, 144, 16), sub(I[256.0], r, 128, 16))
+        ts(sub(ZC[r], 16, 144, 16), sub(I1, r, 128, 16), 256.0, None, AL.mult)
     ts(MK0, MC, 8.0, None, AL.is_lt)
     ts(MK1, MC, 8.0, None, AL.is_ge)
-    for a, mk in ((0, MK0), (1, MK1)):
-        ts(M[(1, a)], I[1.0], mk, None, AL.mult)
-        for s in MS:
-            if s != 1:
-                act(M[(s, a)], M[(1, a)], scale=float(s))
+    ts(SG, MK1, 2.0, -1.0, AL.mult, AL.add)
+    ts(M8, MK1, -8.0, MC, AL.mult, AL.add)
+    ts(TMP, M8, 4.0, None, AL.mult)
+    ts(H4, H4, TMP, None, AL.add)
+    act(In, I1, scale=-1.0)
+    ts(IL, I1, MK0, None, AL.mult)
+    ts(IU, I1, MK1, None, AL.mult)
+    ts(UP, IO, 8.0, MK0, AL.is_equal, AL.mult)
+    ts(DN_, IO, -8.0, MK1, AL.is_equal, AL.mult)
+    tt(D[1][0], IL, DN_, AL.subtract)
+    tt(D[1][1], UP, IU, AL.subtract)
+    tt(N2, UP, IL, AL.subtract)
+    tt(N3, D[1][1], D[1][0], AL.subtract)
+    act(KC, D[1][1], scale=-1.0)
+    for a in range(2):
+        act(S[8][a], S[1][a], scale=8.0)
+        act(D[8][a], D[1][a], scale=8.0)
     ts(BO, QG, PG, None, AL.is_equal)
     ms(Z8, 0.0)
     cp(sub(Z8, 8, 136, 8), sub(BO, 0, 128, 8))
-    ts(E15, MC, 15.0, None, AL.is_equal)
-    ts(BK, E15, 9.5, -8.5, AL.mult, AL.add)
-    ts(K2C, MC, 0.0, 0.125, AL.is_equal, AL.mult)
-    ts(K4C, E15, 0.25, K2C, AL.mult, AL.add)
-    ts(K2, BO, K2C, None, AL.mult)
-    ts(K4, BO, K4C, 2.0, AL.mult, AL.mult)
-    act(FIp, I[1.0])
-    act(FIn, I[-1.0])
-    for t_, v in ((ONE, 1.0), (FOUR, 4.0), (SEVEN, 7.0), (ZERO, 0.0)):
-        ms(t_, v)
-    ts(J2, ONE, MC, None, AL.mult)
-    ts(H2, ONE, MC, 32.0, AL.mult, AL.mult)
-    ts(DL0, H1, 0.125, M4, AL.mult, AL.add)
-    ts(KT, KT, 0.0625, None, AL.mult)
+    ms(ZL, 0.0)
+    cp(sub(ZL, 8, 136, 16), sub(BO, 0, 128, 16))
+    ts(FOUR, sub(ZT, 0, N), MK1, -254.0, AL.add, AL.mult)
+    for s in STEPS:
+        ts(TM[s], I1, SG, 0.5 / s, AL.mult, AL.mult)
+        ts(BIAS[s], MK1, -2.0 * s, -16.0 * s, AL.mult, AL.add)
+        ts(sub(CS[s], 0, N), FOUR, 1.0 * s, None, AL.add)
+        ts(sub(CS[s], N, 2 * N), sub(ZT, 0, N), MK0, -1.0 * s, AL.add, AL.mult)
+    ts(TMP, MK0, -8.5, None, AL.mult)
+    for j, (up, dl) in enumerate(((-0.5, 0.25), (0.0, 0.125), (0.0625, 0.0625))):
+        ts(HI[j], MK1, up, TMP, AL.mult, AL.add)
+        ts(CN[j], sub(ZT, 0, N), HI[j], None, AL.add)
+        ts(HI[j], MK1, 2.0 - dl, dl, AL.mult, AL.add)
+        ts(LO[j], HI[j], -1.0, None, AL.mult)
+    ms(FOUR, 4.0)
+    for m in range(8):
+        ts(RM[m], M8, 1.0 * m, SG, AL.is_equal, AL.mult)
+        ts(RM[m], RM[m], -1.0, None, AL.mult)
+        act(SP[m], BO, scale=RM[m])
+    act(FIp, I1)
+    act(FIn, I1, scale=-1.0)
+    for co in (CO_O, CO_P, CO_N):
+        act(co[3], co[2], scale=-1.0)
 
-    def cast_of(c, off, row, dst, win=CUW):
-        act(c["Sgb"], IND(win, off))
-        pw = sub(c["PV"], 320, 352)
-        mm([(pw, [(sub(ZC[row], 16 - m, 144 - m), sub(c["Sgb"], m, 512, 16)) for m in range(16)])])
-        act(dst, pw)
+    def wrapped(out, mats, t):
+        return [(out, mats[0], sub(t, 0, N, 2)), (out, mats[1], sub(t, 1, N, 2))]
+
+    def casts(c, out, off, row, win=CUW):
+        act(c["Cg"], IND(win, off))
+        return [(out, sub(ZC[row], 16 - m, 144 - m), sub(c["Cg"], m, n, 16)) for m in range(16)]
 
     firsts = []
-    for k, c in enumerate(C):
-        cast_of(c, R("OFS", 32 * k, 32 * k + 32), 0, sub(c["first"], 1024, 1056))
-        cp(sub(c["first"], 0, 512), R("OB", 2048 * k, 2048 * k + 2048, 4))
-        act(sub(c["first"], 512, 1024), R("OB", 4096 + 2048 * k, 4096 + 2048 * k + 2048, 4))
-        firsts.append(sbsend(1, c["first"], R("FL", 1056 * k, 1056 * k + 1056))[0])
+    for c in each():
+        a, pw = 4 * c["i0"], sub(c["base"], 0, w)
+        mm(casts(c, pw, R("OFS", w * c["k"], w * c["k"] + w), 0))
+        act(sub(c["first"], 2 * n, 2 * n + w), pw)
+        cp(c["ta16"], R("OB", a, a + 4 * n, 4))
+        act(c["sa16"], R("OB", 4096 + a, 4096 + a + 4 * n, 4))
+        firsts.append(sbsend(1, c["ta16"], c["fT"]))
+        firsts.append(sbsend(1, sub(c["first"], n, 2 * n + w), sub(c["fl"], n, 2 * n + w)))
     prev = firsts[-1]
     for to, name in ((-1, "DN"), (1, "DP")):
-        for j in range(2):
-            src = R("OB", 4096 * j, 4096 * j + 4096)
+        for j in range(4):
+            src = R("OB", 2048 * j, 2048 * j + 2048)
             prev = send(to, lambda T, src=src: ap(T, src), lambda T, name=name, j=j: T[name][j], [src],
-                        [R(name, 64 * j, 64 * j + 64)], 1 << 20)[0]
+                        [R(name, 64 * j, 64 * j + 64)], 1 << 19)
             ops[prev]["behind"] = firsts
-    i_, _ = send(1, lambda T: T.CB[:], lambda T: T.DC[:], [R("CB", 0, 256)], [R("DC", 0, 256)], 65536)
+    i_ = send(1, lambda T: T.CB[:], lambda T: T.DC[:], [R("CB", 0, 256)], [R("DC", 0, 256)], 65536)
     ops[i_]["behind"] = firsts
     dma("sync", lambda T: [(T.CU[1:128:16, :], T.DC[:])], [R("DC", 0, 256)], [CUW], 65536)
 
     for a, b in ((256, 512), (512, 1024), (1024, 2048), (2048, 3072), (3072, WE)):
         base = 2048 if a >= 2048 else a
         act(R("SB", a, b), R("SB", a - base, b - base), bias=float(2 * base))
-    pieces = [(1020 * j, 1020 * j + 1020) for j in range(4)]
-    for name, co in (("WO", CO_O), ("WN", CO_N), ("WP", CO_P)):
-        for a, b in pieces:
-            ts(R(name, a, b), R("SB", a, b), co[1], co[0], AL.mult, AL.add, low=(name != "WO"))
-    for j in range(8):
-        o = R("WO", WE + 512 * j, min(2 * WE, WE + 512 * j + 512))
-        ops[iota(o, [[2, count(o)]], 1024 * j + 1, 0)]["behind"] = [prev]
-        act(o, o, scale=CO_O[1], low=True)
-        act(o, o, func=AF.Identity, bias=CO_O[0], low=True)
+    for a in range(0, WE, 680):
+        ts(R("WO", a, a + 680), R("SB", a, a + 680), CO_O[1], CO_O[0], AL.mult, AL.add)
+
+    def weights(h, j):
+        name, base, odd, co = (("WN", 0, 0, CO_N), ("WP", 0, 0, CO_P), ("WO", WE, 1, CO_O))[h]
+        gate = len(ops) - 1
+        o = R(name, base + 510 * j, base + 510 * j + 510)
+        ops[iota(o, [[2, 510]], 1020 * j + odd, 0)]["behind"] = [prev]
+        if OPT["wdve"][h]:
+            ops[ts(o, o, co[1], co[0], AL.mult, AL.add)]["behind"] = [gate]
+        else:
+            ops[act(o, o, scale=co[1])]["behind"] = [gate]
+            act(o, o, func=AF.Identity, bias=co[0])
+    where["const"] = False
 
     def table(buf):
         return R(buf, 0, 4096), R(buf, 4096, 8192)
 
     def load_table(buf, src, shifted):
-        for j in range(2):
+        for j in range(4):
             def pairs(T, j=j):
-                s = T[("te", "sa")[j]] if src is None else T[src][j]
-                o = T[buf]
-                a, b = 4096 * j, 4096 * j + 4096
-                if not shifted:
-                    return [(o[:, a:b], s[:, :])]
+                o, a, b = T[buf], 2048 * j, 2048 * j + 2048
                 if src is None:
-                    return []
+                    return [(o[:, a:b], T[("te", "sa")[j // 2]][:, a % 4096:a % 4096 + 2048])]
+                if not shifted:
+                    return [(o[:, a:b], T[src][j])]
                 return [(o[0:112, a:b], T[src][j, 16:128, :]), (o[112:128, a:b], T[src][j, 0:16, :])]
-            dma("pool", pairs, [] if src is None else [R(src, 64 * j, 64 * j + 64)], [R(buf, 4096 * j, 4096 * j + 4096)], 1 << 21)
+            dma("pool", pairs, [] if src is None else [R(src, 64 * j, 64 * j + 64)], [R(buf, 2048 * j, 2048 * j + 2048)], 1 << 20)
 
-    def put_new(buf, k, src):
+    def put_new(buf, c, src):
         for j in range(2):
-            a = 4096 * j + 2048 * k
-            act(R(buf, a, a + 2048, 4), sub(src, 512 * j, 512 * j + 512))
+            a = 4096 * j + 4 * c["i0"]
+            act(R(buf, a, a + 4 * n, 4), sub(src, n * j, n * j + n))
 
-    def offsets(c, lo, hi):
-        cp(sub(c["OF"], lo, hi), sub(c["PV"], lo, hi))
+    def hand_back(c, src, spare, after=()):
+        cut, dst = OPT["relay"][c["k"]], c["lnd"]
+        sbsend(-1, sub(src, n, n + cut), sub(dst, n, n + cut), R("SA", spare, spare + cut), after)
+        i = sbsend(-1, sub(src, 0, n), sub(dst, 0, n), None, after)
+        if cut < n:
+            i = sbsend(-1, sub(src, n + cut, 2 * n), sub(dst, n + cut, 2 * n), None, after)
+        return i
 
-    def vote(c, sg):
-        pv = sub(c["PV"], 128, 192)
-        mm([(pv, [(sub(Z8, 8 - m, 136 - m), sub(c["yes"], m, 512, 8)) for m in range(8)])])
-        act(sg, pv, func=AF.Sign, bias=-8.5)
+    ident = lambda v, sign: (I1 if sign > 0 else In) if width(v) == 2 else (FIp if sign > 0 else FIn)
 
-    def minus(bank, w, v, first):
-        cols = count(bank)
-        n = max(1, OPT["pieces"] * cols // 512) if width(v) == 4 else 1
-        for j in range(n):
-            a, b = cols * j // n, cols * (j + 1) // n
-            i = mm([(sub(bank, a, b), [(w, (v[0], v[1] + a * v[3], v[1] + (b - 1) * v[3] + 1, v[3]))])], first and j == 0, (not first) and j == n - 1)
-            if first and OPT["hold"] and bank[0][-1] in held:
-                ops[i]["behind"] = [held[bank[0][-1]]]
+    def vote(c, Z, terms):
+        VO = c["VO"]
+        mm([(VO, l, r) for l, r in terms] + [(VO, sub(Z, 8 - m, 136 - m), sub(c["yes"], m, n, 8)) for m in range(8)])
 
-    def hop(c, rnd, h, tabs, W, co, T1, S1, dl, dx, base, L, nbase, cast_row):
-        Tt, St = tabs
-        OF, PV, PS, PK, PT, VT, VS = c["OF"], c["PV"], c["PS"], c["PK"], c["PT"], c["VT"], c["VS"]
-        off1, off, x, sel = [sub(OF, 32 * n, 32 * n + 32) for n in range(4)]
-        p1, p0, px, psel = [sub(PV, 32 * n, 32 * n + 32) for n in range(4)]
-        neg = I[-1.0] if width(S1) == 2 else FIn
-        dpart = [(I[8.0], dl)] + dx
-        l = dl
-        act(PT, T1)
-        dT = slot(VT, 3)
-        phase[0] = 2 * (3 * rnd + h)
-        for s in (16, 8, 4, 2, 1):
-            step[:] = ["ab"[rnd], 0]
-            if OPT["search%d" % rnd] == "pe":
-                Sg = c["Sgb"] if rnd == 0 else slot(VS, 3)
-                hv = [(sub(PS, 0, 256), 0, 256), (sub(PK, 0, 256), 256, 512)] if OPT["halves"] else [(PS, 0, 512)]
-                cut = 512 - OPT["share%d" % rnd]
-                if cut < 512:
-                    sd = sub(slot(VS, 2), cut, 512)
-                    tt(sd, IND(St, sub(off, cut // 16, 32)), sub(S1, cut, 512), AL.subtract)
-                    act(sub(PK, cut - 256, 256), sd, scale=co[2])
-                for bank, a, b in hv:
-                    b = min(b, cut)
-                    if a == b:
-                        continue
-                    bank = sub(bank, 0, b - a)
-                    minus(bank, neg, sub(S1, a, b), True)
-                    act(sub(Sg, a, b), IND(St, sub(off, a // 16, b // 16)))
-                    minus(bank, I[1.0] if rnd == 0 else FIp, sub(Sg, a, b), False)
-                    act(bank, bank, scale=co[2])
+    def spread(c, v):
+        mm([(sub(c["K"], m, n, 8), SP[m], v) for m in range(8)])
+
+    def room(c, s, lo, r=None):
+        both = c["room"]
+        pa, pl = sub(both, 0, N), sub(both, N, 2 * N)
+        mm([(both, I1, CS[s]), (pa, N2, lo), (pl, IL, lo)] + ([(pa, N3, r), (pl, D[1][0], r)] if r else []))
+        act(c["al"], both, func=AF.Relu)
+
+    def bases(c, BH, base, lo, more=()):
+        items = base(sub(c["base"], 0, w)) + wrapped(sub(c["base"], w, N), S[8], lo)
+        for j, t in enumerate(more):
+            items += wrapped(sub(c["base"], (2 + j) * w, (3 + j) * w), S[1], t)
+        mm(items)
+        end = (2 + len(more)) * w
+        act(sub(BH, 0, end), sub(c["base"], 0, end))
+
+    def offsets(c, BH, dq, lo, r=None, four=False):
+        V = sub(c["K"], 256, 256 + N) if r and OPT["early"] else c["V"]
+        p0, px = sub(V, 0, w), sub(V, w, N)
+        known = [(V, I1, sub(BH, 0, N))] + dq(px) + ([(px, I1, sub(FOUR, 0, w))] if four else []) + wrapped(p0, S[1], lo) + wrapped(px, S[8], lo)
+        voted = wrapped(p0, D[1], r) + wrapped(px, D[8], r) if r else []
+        if r and OPT["early"]:
+            mm(known, stop=False)
+            mm(voted, start=False)
+        else:
+            mm(known + voted)
+        cp(c["both"], V)
+        return p0
+
+    def search(c, s, mode, tabs, W, co, T1, S1, BH, dq):
+        XS, XT, A = c["XS"], c["XT"], c["A"]
+        Tg, Sg, Wg = IND(tabs[0], c["off"]), IND(tabs[1], c["off"]), IND(W, c["x"])
+        if mode[0] != "1" and c["held"] != T1:
+            mm([(XT, ident(T1, 1), T1)])
+            c["held"] = T1
+        cuts = ((0, n // 2), (n // 2, n))
+        tcuts = cuts if OPT["halves"] > 1 else ((0, n),)
+        banks = [sub(bank, 0, b - a) for bank, (a, b) in zip((XS, c["K"]), cuts)]
+        part = lambda g_, a, b: IND(g_[1], sub(g_[2], a // 16, b // 16))
+        for X, (a, b), how in zip(banks, cuts, (mode[1], mode[-1])):
+            if how == "B":
+                tt(sub(c["Q"], a, b), part(Sg, a, b), sub(S1, a, b), AL.subtract)
+                if mode[0] != "3":
+                    act(X, sub(c["Q"], a, b), scale=co[2])
+                continue
+            Q = sub(c["Q16"] if where["phase"] < 6 else c["Q"], a, b)
+            if how == "A":
+                mm([(X, ident(S1, 1), sub(S1, a, b))], stop=False)
             else:
-                hv = [(PS, 0, 512)]
-                Sg = slot(VS, 3)
-                tt(Sg, IND(St, off), S1, AL.subtract)
-                act(PS, Sg, scale=co[2])
-            if s in OPT["tact"][c["k"]]:
-                act(dT, IND(Tt, off))
-                tt(dT, dT, PT, AL.subtract)
+                mm([(X, I1, sub(ZT, 0, b - a))], stop=False)
+                act(X, sub(S1, a, b))
+            act(Q, part(Sg, a, b))
+            mm([(X, ident(Q, -1), Q)], start=False)
+            act(X, X, scale=co[3])
+        for a, b in tcuts:
+            if mode[0] == "1":
+                tt(sub(A, a, b), part(Tg, a, b), sub(T1, a, b), AL.subtract)
             else:
-                tt(dT, IND(Tt, off), T1, AL.subtract)
-            tt(dT, IND(W, x), dT, AL.mult)
-            for bank, a, b in hv:
-                tt(sub(c["yes"], a, b), sub(dT, a, b), bank, AL.is_gt)
-            vote(c, c["sg2"])
-            pu = sub(PV, 192, 224)
-            mm([(pu, [(I[1.0], l)] + masked(s, c["sg2"]))])
-            ts(L, pu, 0.0, 254.0, AL.max, AL.min)
-            l = L
-            if s > 1:
-                mm([(p0, [(I[1.0], base), (I[1.0], l)]), (px, dpart + [(I[8.0], l)])])
-                offsets(c, 32, 96)
+                act(sub(A, a, b), part(Tg, a, b))
+                if mode[0] == "2":
+                    tt(sub(A, a, b), sub(A, a, b), sub(XT, a, b), AL.subtract)
+        if mode[0] != "3":
+            for a, b in tcuts:
+                tt(sub(A, a, b), part(Wg, a, b), sub(A, a, b), AL.mult)
+        else:
+            for X, (a, b) in zip(banks, cuts):
+                act(sub(c["Cw"], a, b), part(Wg, a, b))
+                tt(X, sub(A, a, b), sub(XT, a, b), AL.subtract)
+                tt(sub(A, a, b), sub(c["Cw"], a, b), X, AL.mult)
+                act(X, sub(c["Q"], a, b), scale=co[2])
+        for X, (a, b) in zip(banks, cuts):
+            tt(sub(c["yes"], a, b), sub(A, a, b), X, AL.is_gt)
+        vote(c, Z8, [(TM[s], c["a"])])
+        act(c["r"], c["VO"], func=AF.Relu, scale=2.0 * s, bias=BIAS[s])
+        p0 = offsets(c, BH, dq, c["lm"], c["r"], s == 1)
+        if s > 1:
+            room(c, s // 2, c["lm"], c["r"])
+        else:
+            ts(c["off1"], p0, 1.0, None, AL.add)
+            mm([(c["VO"], IL, c["lm"]), (c["VO"], D[1][0], c["r"])])
+            act(c["Lw"], c["VO"])
+
+    def slopes(c, tabs):
+        lo = (c["ta16"], c["sa16"]) if where["phase"] < 6 else (c["ta"], c["sa"])
+        for j in (1, 0):
+            act(lo[j], IND(tabs[j], c["off"]))
+            if where["phase"] < 6 and "TS"[j] in OPT["pslope"]:
+                act(c["Q16"], IND(tabs[j], c["off1"]))
+                mm([(c["K"], I1, c["Q16"]), (c["K"], In, lo[j])])
+                act(c[("tb", "sb")[j]], c["K"])
             else:
-                mm([(p0, [(I[1.0], base), (I[1.0], l)]), (p1, [(I[1.0], base), (I[1.0], ONE), (I[1.0], l)]),
-                    (px, dpart + [(I[1.0], FOUR), (I[8.0], l)])])
-                offsets(c, 0, 96)
-        xb = dpart + [(I[1.0], FOUR), (I[8.0], l)]
-        phase[0] += 1
-        step[:] = ["c", 0]
-        ta, sa_ = slot(VT, 0), slot(VS, 0)
-        bype = OPT["slope%d" % rnd]
-        for nm, tab, lo_, b_, bank, V in (("s", St, sa_, c["sb"], PV, VS), ("t", Tt, ta, c["tb"], PK, VT)):
-            (cp if nm in OPT["lodve"] else act)(lo_, IND(tab, off))
-            if nm in bype:
-                hi_ = (c["Sgb"] if nm == "s" else c["sr4"]) if rnd == 0 else slot(V, 2)
-                act(hi_, IND(tab, off1))
-                minus(bank, FIn, lo_, True)
-                minus(bank, I[1.0] if rnd == 0 else FIp, hi_, False)
-                act(b_, bank)
+                tt(c[("tb", "sb")[j]], IND(tabs[j], c["off1"]), lo[j], AL.subtract)
+        return lo
+
+    def between(c, side, lo, slope, v, by_pe, minus=None):
+        X = c["X" + side]
+        if side == "T":
+            c["held"] = None
+        if by_pe:
+            mm([(X, I1, ZT)], stop=False)
+        if v is None:
+            act(X, slope, scale=0.5)
+        else:
+            tt(X, slope, c["K"], AL.mult)
+        if by_pe:
+            items = []
+            for t, sign in ((lo, 1), (minus, -1)):
+                m = OPT["pieces"] if t and width(t) == 4 else 1
+                items += [(sub(X, n * j // m, n * (j + 1) // m), ident(t, sign), sub(t, n * j // m, n * (j + 1) // m)) for j in range(m) if t]
+            for j, item in enumerate(items):
+                mm([item], start=False, stop=j == len(items) - 1)
+        else:
+            tt(X, X, lo, AL.add)
+            if minus:
+                tt(X, X, minus, AL.subtract)
+
+    def refine(c, j, mode, lo, W, co, T1, S1, BH, dq):
+        XS, XT, A = c["XS"], c["XT"], c["A"]
+        v = c["v%d" % (j - 1)] if j else None
+        Wg = IND(W, c["x"])
+        mt, ms_ = mode
+        if j:
+            spread(c, v)
+        between(c, "S", lo[1], c["sb"], v, ms_ in "ab", S1 if ms_ != "b" else None)
+        if ms_ == "b":
+            tt(XS, XS, S1, AL.subtract)
+        act(XS, XS, scale=co[2])
+        between(c, "T", lo[0], c["tb"], v, mt in "abc", T1 if mt == "c" else None)
+        if mt in "ad":
+            tt(A, XT, T1, AL.subtract)
+            tt(A, Wg, A, AL.mult)
+        else:
+            act(c["Cw"], Wg)
+            if mt != "c":
+                tt(XT, XT, T1, AL.subtract)
+            tt(A, c["Cw"], XT, AL.mult)
+        tt(c["yes"], A, XS, AL.is_gt)
+        vote(c, ZL, [(I1, CN[j])] + ([(KC, v)] if j else []))
+        ts(c["v%d" % j], c["VO"], LO[j], HI[j], AL.max, AL.min)
+        if j < 2:
+            px = sub(c["V"], w, N)
+            mm([(px, I1, sub(BH, w, N)), (px, I1, sub(FOUR, 0, w))] + dq(px) + wrapped(px, S[8], c["Lw"])
+               + [x for i in range(j + 1) for x in wrapped(px, S[8], c["v%d" % i])])
+            cp(c["x"], px)
+
+    def final(c, mode, lo, v):
+        spread(c, v)
+        for side, j, slope in (("S", 1, c["sb"]), ("T", 0, c["tb"])):
+            X, out = c["X" + side], c[side + "1"]
+            if mode[j] == "w":
+                tt(X, slope, c["K"], AL.mult)
+                tt(out, X, lo[j], AL.add)
             else:
-                tt(b_, IND(tab, off1), lo_, AL.subtract)
-        for n, sg in ((1, c["sg8"]), (2, c["sg4"]), (3, c["sg2"])):
-            step[:] = ["def"[n - 1], 0]
-            if n == 1 and cast_row is None:
-                step[0] = "g"
-            if OPT["refine"] == "pe":
-                minus(PS, neg, S1, True)
-            if n == 1:
-                act(PV, PV if "s" in bype else c["sb"], scale=0.5)
-                act(PK, PK if "t" in bype else c["tb"], scale=0.5)
-            else:
-                tt(PV, c["sb"], PK, AL.mult)
-            tt(slot(VS, n), PV, sa_, AL.add)
-            if OPT["refine"] == "pe":
-                minus(PS, FIp, slot(VS, n), False)
-            else:
-                tt(PS, slot(VS, n), S1, AL.subtract)
-            act(PS, PS, scale=co[2])
-            if n == 3:
-                s8, s4, sA = c["sg8"], c["sg4"], sub(c["sAB"], 0, 32)
-                mm([(sub(PV, 224, 256), masked(1, s8) + masked(1, s4)),
-                    (sub(PV, 288, 320), [(I[1.0], SEVEN)] + masked(4, s8) + masked(2, s4))])
-                act(sA, sub(PV, 224, 256), func=AF.Sign, bias=1.0)
-                act(c["x"], sub(PV, 288, 320))
-                mm([(sub(PV, 256, 288), [(I[1.0], J1), (I[1.0], J2), (I[256.0], sA)] + masked(256, s4))])
-                act(c["low"], sub(PV, 256, 288), bias=-256.0)
-            if n > 1:
-                tt(PK, c["tb"], PK, AL.mult)
-            tt(slot(VT, n), PK, ta, AL.add)
-            dT = slot(VT, 3) if n < 3 else c["tb"]
-            if n in OPT["wact"]:
-                act(dT, IND(W, x))
-                tt(PK, slot(VT, n), PT, AL.subtract)
-                tt(dT, dT, PK, AL.mult)
-            else:
-                tt(dT, slot(VT, n), PT, AL.subtract)
-                tt(dT, IND(W, x), dT, AL.mult)
-            if n == 1 and cast_row is not None:
-                cast_of(c, off, cast_row, nbase)
-            tt(c["yes"], dT, PS, AL.is_gt)
-            if n < 3:
-                mm([(PK, [(BO, c["yes"])])])
-                sr = c["sr8"] if n == 1 else c["sr4"]
-                act(sr, PK, func=AF.Sign, bias=BK)
-            vote(c, sg)
-            if n < 3:
-                mm([(px, xb + masked(2, c["sg8"]) + (masked(1, c["sg4"]) if n == 2 else []))])
-                offsets(c, 64, 96)
-                mm([(PK, [(K4, c["sr8"])] + ([(K2, c["sr4"])] if n == 2 else []))])
-        s8, s4, s2 = c["sg8"], c["sg4"], c["sg2"]
-        gs = [(psel, [(I[1.0], J1), (I[1.0], J2)] + masked(768, s2))]
-        lo = 96
+                between(c, side, lo[j], slope, v, mode[j] == "p")
+                act(out, X)
+        c["held"] = None if mode[0] == "w" else c["T1"]
+
+    def relax(c, mode, lo, v, olds, new):
+        spread(c, v)
+        for side, j, slope in (("S", 1, c["sb"]), ("T", 0, c["tb"])):
+            X = c["X" + side]
+            between(c, side, lo[j], slope, v, mode[j] == "p", olds[j])
+            act(X, X, scale=0.25)
+            tt(sub(new, n * j, n * j + n), X, olds[j], AL.add)
+
+    fraction = lambda c: (lambda px: wrapped(px, D[8], c["v2"]))
+
+    def hop(c, rnd, h, tabs, W, co, T1, S1, dq):
+        modes = MODES[(rnd, h)]
+        where["phase"] = 2 * (3 * rnd + h)
+        BH, nxt = c["BH"][h % 2], c["BH"][1 - h % 2]
+        aside = (rnd, c["k"]) == (0, 0) and h < 2
+        for j, s in enumerate(STEPS):
+            if aside:
+                weights(h, j)
+            search(c, s, modes[0][j], tabs, W, co, T1, S1, BH, dq)
+        where["phase"] += 1
+        if (rnd, h) == (1, 2):
+            sbsend(-1, c["of"], c["own"]["of"])
+        lo = slopes(c, tabs)
         if h < 2:
-            gs += [(p0, [(I[1.0], nbase), (I[1.0], l)]), (px, [(I[16.0], l), (I[0.5], c["x"])] + masked(0.5, s2))]
-            lo = 32
-        mm(gs)
-        tt(psel, psel, c["low"], AL.max)
-        offsets(c, lo, 128)
-        mm([(sub(PV, 288, 320), [(I[1.0], c["x"])] + masked(1, s2))])
-        act(c["dq"], sub(PV, 288, 320))
-        for a, b in (((0, 256), (256, 512)) if OPT["halves"] else ((0, 512),)):
-            act(sub(c["S1"], a, b), IND(VS, sub(sel, a // 16, b // 16)))
-        (cp if OPT["seldve"] else act)(c["T1"], IND(VT, sel))
-        step[0] = "-"
+            home = sub(HB, w * c["k"], w * c["k"] + w)
+            bases(c, nxt, (lambda o: casts(c, o, c["off"], 0)) if h == 0 else (lambda o: [(o, I1, home)]), c["Lw"])
+            room(c, 16, c["Lw"])
+        for j in range(3):
+            if aside:
+                weights(h, 5 + j)
+            refine(c, j, modes[1][j], lo, W, co, T1, S1, BH, dq)
+        if h < 2:
+            offsets(c, nxt, fraction(c), c["Lw"])
+            final(c, modes[2], lo, c["v2"])
+        return lo
 
-    def relax(c, oldT, oldS):
-        minus(c["PS"], I[-1.0] if width(oldS) == 2 else FIn, oldS, True)
-        minus(c["PS"], FIp, c["S1"], False)
-        act(c["PS"], c["PS"], scale=0.25)
-        tt(c["sb"], c["PS"], oldS, AL.add)
-        tt(c["PK"], c["T1"], oldT, AL.subtract)
-        act(c["PK"], c["PK"], scale=0.25)
-        tt(c["tb"], c["PK"], oldT, AL.add)
-
-    half = lambda c: [(I[0.5], c["dq"])]
     WOE, WOF, WNn, WPp = R("WO", 0, WE), R("WO", 0, 2 * WE), R("WN", 0, WE), R("WP", 0, WE)
-    fl = [[R("FL", 1056 * k + a, 1056 * k + b) for a, b in ((0, 512), (512, 1024), (1024, 1056))] for k in range(2)]
-    lnd = [R("LND", 1056 * k, 1056 * k + 1056) for k in range(2)]
-    new = [R("CH%d" % k, 4096, 5120) for k in range(2)]
 
     load_table("SA", "DN", True)
-    for k, c in enumerate(C):
-        mm([(sub(c["PV"], 32, 64), [(I[1.0], DL0), (I[1.0], fl[k][2])]), (sub(c["PV"], 64, 96), [(I[16.0], DL0)])])
-        offsets(c, 32, 96)
-        hop(c, 0, 0, table("OB"), WOE, CO_O, fl[k][0], fl[k][1], DL0, [], fl[k][2], c["L0"], c["B0"], 0)
+    for c in each():
+        bases(c, c["BH"][0], lambda o: [(o, I1, c["fC"])], H4)
+        offsets(c, c["BH"][0], lambda px: [], H4)
+        room(c, 16, H4)
+        hop(c, 0, 0, table("OB"), WOE, CO_O, c["fT"], c["fS"], lambda px: [])
     load_table("SB", "DP", False)
-    for k, c in enumerate(C):
-        hop(c, 0, 1, table("SA"), WNn, CO_N, c["T1"], c["S1"], c["L0"], half(c), c["B0"], c["L1"], HB[k], None)
+    for c in each():
+        hop(c, 0, 1, table("SA"), WNn, CO_N, c["T1"], c["S1"], fraction(c))
     load_table("SA", None, False)
-    for k, c in enumerate(C):
-        hop(c, 0, 2, table("SB"), WPp, CO_P, c["T1"], c["S1"], c["L1"], half(c), HB[k], c["L0"], None, None)
-    for k, c in enumerate(C):
-        relax(c, fl[k][0], fl[k][1])
-        sbsend(-1, c["sb"], sub(lnd[k], 512, 1024), relay=R("SA", 512 * k, 512 * k + 512))
-        c["sent"] = sbsend(-1, c["tb"], sub(lnd[k], 0, 512))[0]
-        pd = sub(c["PV"], 352, 384)
-        mm([(pd, [(I[1.0], H1), (I[1.0], H2), (I[8.0], c["L0"]), (I[0.5], c["dq"])])])
-        di, dj = R("CI", 128 * k, 128 * k + 32), R("CI", 128 * k + 32, 128 * k + 64)
-        d2, d3, = R("CI", 128 * k + 64, 128 * k + 96), R("CI", 128 * k + 96, 128 * k + 128)
-        cp(di, pd)
-        ts(dj, di, 4, None, AL.arith_shift_right)
-        ts(d2, di, 15, None, AL.bitwise_and)
+    for c in each():
+        lo = hop(c, 0, 2, table("SB"), WPp, CO_P, c["T1"], c["S1"], fraction(c))
+        VO = c["VO"]
+        mm([(VO, I1, H4), (VO, I1, c["Lw"]), (VO, D[1][0], c["v2"])])
+        di, d1, d2, d3 = [R("I%d" % c["k"], N * j, N * j + N) for j in range(4)]
+        ts(di, VO, 8.0, None, AL.mult)
+        relax(c, OPT["relax"][0], lo, c["v2"], (c["fT"], c["fS"]), c["kept"])
+        c["sent"] = hand_back(c, c["kept"], c["i0"])
+        ts(d1, di, 4, None, AL.arith_shift_right)
+        ts(d2, di, 15, 1, AL.bitwise_and, AL.logical_shift_right)
         ts(d3, di, 1, None, AL.bitwise_and)
-        cp(c["L1"], dj)
-        cp(c["dq"], d2)
-        cp(c["par"], d3)
-        ts(dj, di, 1, None, AL.arith_shift_right)
-        ts(d3, d2, 1, None, AL.arith_shift_right)
-        cp(DH[k], dj)
-        cp(c["dqh"], d3)
-    for k, c in enumerate(C):
-        put_new("SB", k, new[k])
-    for k, c in enumerate(C):
-        i_, _ = send(2, lambda T, k=k: ap(T, new[k]), lambda T, k=k: T.DU[k], [new[k]], [R("DU", 64 * k, 64 * k + 64)], 1 << 19)
-        ops[i_]["behind"] = [C[0]["sent"], C[1]["sent"]]
-        i_ = dma("sync", lambda T, k=k: [(T.DS[k], ap(T, new[k]))], [new[k]], [R("DS", 64 * k, 64 * k + 64)], 1 << 19,
-                 after=[C[1]["sent"]])
+        ts(di, di, 15, None, AL.bitwise_and)
+        cp(c["l1"], d1)
+        cp(c["qh"], d2)
+        ts(c["par"], d3, float(WE), None, AL.mult)
+        ts(c["v0"], di, 0.0625, MK0, AL.mult, AL.mult)
+    for c in each():
+        put_new("SB", c, c["kept"])
+    for c in each():
+        k = c["k"]
+        i_ = send(2, lambda T, c=c: ap(T, c["kept"]), lambda T, k=k: T.DU[k], [c["kept"]], [R("DU", 64 * k, 64 * k + 64)], 1024 * n)
+        ops[i_]["behind"] = [x["sent"] for x in C]
 
-    odd = lambda c: [(I[1.0], c["dqh"]), (I[4080.0], c["par"])]
-    for k, c in enumerate(C):
-        PV, OF, VT, VS = c["PV"], c["OF"], c["VT"], c["VS"]
-        dl = c["L1"]
-        mm([(sub(PV, 0, 32), [(I[1.0], HB0), (I[1.0], ONE), (I[1.0], dl)]), (sub(PV, 32, 64), [(I[1.0], HB0), (I[1.0], dl)]),
-            (sub(PV, 64, 96), [(I[16.0], dl)] + odd(c)), (sub(PV, 96, 128), [(I[1.0], c["dq"])])])
-        offsets(c, 0, 128)
-        cast_of(c, sub(OF, 32, 64), 1, c["B0"], sub(CUW, 2048 * k, 2048 * k + 2048))
-        homes = [sub(t_, 2048 * k, 2048 * k + 2048) for t_ in table("SB")]
-        for V, tab, o, bank in ((VS, homes[1], c["S1"], c["PS"]), (VT, homes[0], c["T1"], c["PK"])):
-            act(slot(V, 0), IND(tab, sub(OF, 32, 64)))
-            tt(slot(V, 1), IND(tab, sub(OF, 0, 32)), slot(V, 0), AL.subtract)
-            act(bank, slot(V, 0))
-            tt(slot(V, 1), IND(KT, sub(OF, 96, 128)), slot(V, 1), AL.mult)
-            tt(o, bank, slot(V, 1), AL.add)
-        mm([(sub(PV, 32, 64), [(I[1.0], c["B0"]), (I[1.0], dl)])])
-        offsets(c, 32, 64)
-    for k in range(2):
-        put_new("SA", k, lnd[k])
+    where["phase"] = 6
+    for c in each():
+        p0, l1, a, b = sub(c["V"], 0, w), c["l1"], 4 * c["i0"], 4 * (c["i0"] + n)
+        mm([(p0, I1, sub(HB, 0, w))] + wrapped(p0, S[1], l1))
+        cp(c["off"], p0)
+        ts(c["off1"], p0, 1.0, None, AL.add)
+        lo = slopes(c, [sub(t_, a, b) for t_ in table("SB")])
+        BH = c["BH"][0]
+        bases(c, BH, lambda o: casts(c, o, c["off"], 1, sub(CUW, a, b)), l1, (c["qh"], c["par"]))
+        c["odd"] = lambda px, BH=BH: [(px, I1, sub(BH, j * w, j * w + w)) for j in (2, 3)]
+        offsets(c, BH, c["odd"], l1)
+        room(c, 16, l1)
+        final(c, OPT["step1"], lo, c["v0"])
+        for j in range(4):
+            weights(2, 4 * c["k"] + j)
+    for c in each():
+        put_new("SA", c, c["lnd"])
+        dma("sync", lambda T, c=c: [(T.DS[c["k"]], ap(T, c["lnd"]))], [c["lnd"]], [R("DS", 64 * c["k"], 64 * c["k"] + 64)], 1024 * n)
     load_table("SB", "DN", True)
-    for k in range(2):
-        dma("sync", lambda T, k=k: [(T.LND[0:112, 1056 * k:1056 * k + 1024], T.DU[k, 16:128, :]),
-                                    (T.LND[112:128, 1056 * k:1056 * k + 1024], T.DU[k, 0:16, :])],
-            [R("DU", 64 * k, 64 * k + 64)], [sub(lnd[k], 0, 1024)], 1 << 19)
-        put_new("SB", k, lnd[k])
-    for k, c in enumerate(C):
-        hop(c, 1, 0, table("SA"), WOF, CO_O, c["T1"], c["S1"], c["L1"], odd(c), c["B0"], c["L0"], c["B1"], 0)
+    for c in each():
+        def shifted(T, c=c):
+            a, b, k = c["lnd"][1], c["lnd"][2], c["k"]
+            return [(T.LND[0:112, a:b], T.DU[k, 16:128, :]), (T.LND[112:128, a:b], T.DU[k, 0:16, :])]
+        dma("sync", shifted, [R("DU", 64 * c["k"], 64 * c["k"] + 64)], [c["lnd"]], 1024 * n)
+        put_new("SB", c, c["lnd"])
+        dma("sync", lambda T, c=c: [(ap(T, c["lnd"]), T.DS[c["k"]])], [R("DS", 64 * c["k"], 64 * c["k"] + 64)], [c["lnd"]], 1024 * n)
+    for c in each():
+        hop(c, 1, 0, table("SA"), WOF, CO_O, c["T1"], c["S1"], c["odd"])
     load_table("SA", "DP", False)
-    for k in range(2):
-        dma("sync", lambda T, k=k: [(T.LND[:, 1056 * k:1056 * k + 1024], T.DS[k])],
-            [R("DS", 64 * k, 64 * k + 64)], [sub(lnd[k], 0, 1024)], 1 << 19)
-        put_new("SA", k, lnd[k])
-    free = [len(ops) - 1, len(ops) - 2, len(ops) - 4, len(ops) - 5]
-    _, credit = send(1, None, None, [], [], 0, after=free)
-    for k, c in enumerate(C):
-        hop(c, 1, 1, table("SB"), WNn, CO_N, c["T1"], c["S1"], c["L0"], half(c), c["B1"], c["L1"], HB[k], None)
-    for k, c in enumerate(C):
-        hop(c, 1, 2, table("SA"), WPp, CO_P, c["T1"], c["S1"], c["L1"], half(c), HB[k], c["L0"], None, None)
-        pd = sub(c["PV"], 352, 384)
-        mm([(pd, [(I[8.0], c["L0"]), (I[0.5], c["dq"])])])
-        tt(DH[k], pd, DH[k], AL.add)
-        add("dve", 80.0, lambda g, T, c=c, k=k: g.vector.transpose(ap(T, c["D"]), ap(T, DH[k])), [DH[k]], [c["D"]])
-        ld = sub(lnd[k], 1024, 1056)
+    for c in each():
+        put_new("SA", c, c["kept"])
+    for c in each():
+        hop(c, 1, 1, table("SB"), WNn, CO_N, c["T1"], c["S1"], fraction(c))
+    load_table("SB", None, False)
+    for c in each():
+        put_new("SB", c, c["lnd"])
+    for c in each():
+        hop(c, 1, 2, table("SA"), WPp, CO_P, c["T1"], c["S1"], fraction(c))
+        px, i0, ld = sub(c["V"], w, N), c["i0"], c["finD"]
+        mm(wrapped(px, S[8], c["Lw"]) + wrapped(px, S[8], c["l1"]) + wrapped(px, S[1], c["qh"]) + wrapped(px, D[8], c["v2"]))
+        add("dve", 80.0, lambda g, T, c=c, px=px: g.vector.transpose(ap(T, c["D"]), ap(T, px)), [px], [c["D"]])
         sbsend(-1, c["D"], ld)
-        dma("sync", lambda T, k=k, ld=ld: [(T.yd[gg, 512 * k:512 * k + 512],
-                                           T.LND[32 * (gg // 2):32 * (gg // 2) + 32, ld[1] + 16 * (gg % 2):ld[1] + 16 * (gg % 2) + 16])
-                                          for gg in range(8)], [ld], [], 16384)
-        relax(c, R("SA", 2048 * k + 1, 2048 * k + 2048, 4), R("SA", 4096 + 2048 * k + 1, 4096 + 2048 * k + 2048, 4))
-        for j, name, q in ((1, "ys", "sync"), (0, "yt", "act")):
-            ld = sub(lnd[k], 512 * j, 512 * j + 512)
-            sbsend(-1, sub(new[k], 512 * j, 512 * j + 512), ld, after=[credit],
-                   relay=R("SA", 1024 + 512 * k, 1536 + 512 * k) if j else None)
-            dma(q if k == 1 else "sync", lambda T, k=k, ld=ld, name=name: [(T[name][:, 512 * k:512 * k + 512], ap(T, ld))], [ld], [], 1 << 18)
+        dma("sync", lambda T, ld=ld, i0=i0: [(T.yd[gg, i0:i0 + n], T.FIN[32 * (gg // 2):32 * (gg // 2) + 32, ld[1] + 16 * (gg % 2):ld[1] + 16 * (gg % 2) + 16])
+                                             for gg in range(8)], [ld], [], 16384)
+        own = c["own"]
+        sbsend(-1, c["v2"], own["v2"])
+        lo = slopes(own, table("SB"))
+        relax(own, OPT["relax"][1], lo, own["v2"], [R("SB", o + 4 * i0 + 1, o + 4 * (i0 + n), 4) for o in (0, 4096)], c["lnd"])
+        for name, ld in (("ys", own["sb"]), ("yt", own["tb"])):
+            dma("sync", lambda T, ld=ld, name=name, i0=i0: [(T[name][:, i0:i0 + n], ap(T, ld))], [ld], [], 512 * n)
     return ops
 
 
-QUEUE = {"pe": "pe", "act": "act", "dve": "dve", "pool": "pool", "sync": "sync"}
+def needs_wait(o, p, kind):
+    if o["kind"] == "c" and p["kind"] == "c" and o["eng"] == p["eng"]:
+        return o["eng"] != "pe" and kind == "raw"
+    return True
 
 
 def schedule(ops):
     n = len(ops)
     succ = [[] for _ in ops]
-    for i, o in enumerate(ops):
-        o["pre"] = set(o["deps"]) | set(o.get("behind", ()))
-        for j in o["pre"]:
+    pre = [set(o["deps"]) | set(o.get("behind", ())) for o in ops]
+    for i in range(n):
+        for j in pre[i]:
             succ[j].append(i)
     lat = OPT["lat"]
     prio = [0.0] * n
@@ -653,59 +725,59 @@ def schedule(ops):
         o = ops[i]
         prio[i] = o["dur"] + o["lat"] + max([prio[s] + lat for s in succ[i]] or [0.0])
     for i, o in enumerate(ops):
-        prio[i] += (OPT["lead"][o["phase"]] if o["lead"] else 0.0) + OPT["bias"].get(o["cls"], 0.0)
-    left = [len(o["pre"]) for o in ops]
+        if o["chunk"] >= 0:
+            prio[i] += OPT["lead"][o["phase"] // 2] * (NCH - 1 - o["chunk"])
+    left = [len(p) for p in pre]
     ready = {e: [] for e in ("pe", "act", "dve", "pool", "sync", "none")}
-    est = [0.0] * n
+    est, end = [0.0] * n, [0.0] * n
     for i, o in enumerate(ops):
         if not left[i]:
             ready[o["eng"]].append(i)
     free = {e: 0.0 for e in ready}
-    res = {}
-    order = []
+    res, touch, order = {}, {}, []
+
+    def others(i):
+        return [j for b in ops[i]["banks"] for e, j in touch.get(b, {}).items() if e != ops[i]["eng"]]
+
     while len(order) < n:
         best = None
         for e, lst in ready.items():
             if lst:
-                t0 = max(free[e], min(est[i] for i in lst))
+                at = {i: max([est[i]] + [end[j] + lat for j in others(i)]) for i in lst}
+                t0 = max(free[e], min(at.values()))
                 if best is None or t0 < best[0]:
-                    best = (t0, e)
-        t0, e = best
-        cand = [i for i in ready[e] if est[i] <= t0 + OPT["slack"].get(e, 0.0)]
-        i = max(cand, key=lambda j: (prio[j], -j))
+                    best = (t0, e, at)
+        t0, e, at = best
+        i = max((j for j in ready[e] if at[j] <= t0 + OPT["slack"].get(e, 0.0)), key=lambda j: (prio[j], -j))
         ready[e].remove(i)
         o = ops[i]
-        s = max(t0, est[i])
-        o["start"] = s
-        issued = s + o["dur"]
+        for b in o["banks"]:
+            touch.setdefault(b, {})[e] = i
+        issued = max(t0, at[i]) + o["dur"]
         if e != "none":
             free[e] = issued
-        end = issued + o["lat"]
+        end[i] = issued + o["lat"]
         if "res" in o:
             r0 = max(res.get(o["res"], 0.0), issued)
             res[o["res"]] = r0 + o["busy"]
-            end = r0 + o["lat"]
-        o["end"] = end
+            end[i] = r0 + o["lat"]
         order.append(i)
         for j in succ[i]:
-            p = ops[j]
-            kind = p["deps"].get(i)
-            if kind is None or not needs_wait(o, p, kind):
-                t = issued
-            else:
-                t = end + lat
+            kind = ops[j]["deps"].get(i)
+            t = end[i] + lat if kind is not None and needs_wait(o, ops[j], kind) else issued
             est[j] = max(est[j], t)
             left[j] -= 1
             if not left[j]:
-                ready[p["eng"]].append(j)
+                ready[ops[j]["eng"]].append(j)
     return order
 
 
 def improve(sets, order):
     n = len(order)
     eng = [o["eng"] for o in sets[0]]
-    pre = [sets[0][i]["pre"] for i in range(n)]
-    waits = [[(j, o["deps"].get(j) is not None and needs_wait(sets[0][j], o, o["deps"][j])) for j in sorted(o["pre"])] for o in sets[0]]
+    banks = [o["banks"] for o in sets[0]]
+    pre = [set(o["deps"]) | set(o.get("behind", ())) for o in sets[0]]
+    waits = [[(j, o["deps"].get(j) is not None and needs_wait(sets[0][j], o, o["deps"][j])) for j in sorted(pre[i])] for i, o in enumerate(sets[0])]
     seed = [12345]
 
     def rand():
@@ -713,42 +785,58 @@ def improve(sets, order):
         return (seed[0] >> 8) / 8388608.0
 
     def frame(ops, lat, a, b):
-        st, tot, free, res = [0.0] * n, [0.0] * n, {}, {}
-        first = {}
+        st, tot, free, res, touch = [0.0] * n, [0.0] * n, {}, {}, {}
+        first, used = {}, {}
         for pos, i in enumerate(order):
             if pos == a:
-                first = dict(free)
+                first, used = dict(free), {k: dict(v) for k, v in touch.items()}
             o = ops[i]
             t = free.get(eng[i], 0.0)
             for j, w in waits[i]:
                 t = max(t, st[j] + (tot[j] + lat if w else ops[j]["dur"]))
+            for k in banks[i]:
+                for e, v in touch.setdefault(k, {}).items():
+                    if e != eng[i]:
+                        t = max(t, v)
             st[i] = t
             tot[i] = o["dur"] + o["lat"]
+            for k in banks[i]:
+                touch[k][eng[i]] = t + tot[i] + lat
             if eng[i] != "none":
                 free[eng[i]] = t + o["dur"]
             if "res" in o:
                 r0 = max(res.get(o["res"], 0.0), t + o["dur"])
                 res[o["res"]] = r0 + o["busy"]
                 tot[i] += r0 - t - o["dur"]
-        tail, nxt = list(tot), {}
-        for i in reversed(order[b:]):
+        tail, nxt, later = list(tot), {}, {}
+
+        def behind(i):
+            t = tail[i]
             if eng[i] != "none":
-                tail[i] = max(tail[i], ops[i]["dur"] + nxt.get(eng[i], 0.0))
-                nxt[eng[i]] = tail[i]
+                t = max(t, ops[i]["dur"] + nxt.get(eng[i], 0.0))
+            for k in banks[i]:
+                for e, v in later.get(k, {}).items():
+                    if e != eng[i]:
+                        t = max(t, tot[i] + lat + v)
+            return t
+        for i in reversed(order[b:]):
+            tail[i] = nxt[eng[i]] = behind(i)
+            for k in banks[i]:
+                later.setdefault(k, {})[eng[i]] = tail[i]
             for j, w in waits[i]:
                 tail[j] = max(tail[j], (tot[j] + lat if w else ops[j]["dur"]) + tail[i])
         inside = set(order[a:b])
         head, edge = {}, {}
         for i in inside:
-            head[i] = max([st[j] + (tot[j] + lat if w else ops[j]["dur"]) for j, w in waits[i] if j not in inside] + [first.get(eng[i], 0.0)])
+            head[i] = max([st[j] + (tot[j] + lat if w else ops[j]["dur"]) for j, w in waits[i] if j not in inside] + [first.get(eng[i], 0.0)]
+                          + [v for k in banks[i] for e, v in used.get(k, {}).items() if e != eng[i]])
             edge[i] = [(j, tot[j] + lat if w else ops[j]["dur"]) for j, w in waits[i] if j in inside]
-            if eng[i] != "none":
-                tail[i] = max(tail[i], ops[i]["dur"] + nxt.get(eng[i], 0.0))
-        return head, edge, tail, [o["dur"] for o in ops]
+            tail[i] = behind(i)
+        return head, edge, tail, [o["dur"] for o in ops], lat
 
     def walk(win, fr):
-        head, edge, tail, dur = fr
-        st, par, last = {}, {}, {}
+        head, edge, tail, dur, lat = fr
+        st, par, last, touch = {}, {}, {}, {}
         top, at = 0.0, -1
         for i in win:
             t, p = head[i], -1
@@ -763,15 +851,22 @@ def improve(sets, order):
                 if v >= t:
                     t, p = v, -2 - j
             last[e] = i
+            for k in banks[i]:
+                d = touch.setdefault(k, {})
+                for f, j in d.items():
+                    if f != e and st[j] + dur[j] + lat > t:
+                        t, p = st[j] + dur[j] + lat, -2 - j
+                d[e] = i
             st[i], par[i] = t, p
             if t + tail[i] > top:
                 top, at = t + tail[i], i
         return top, at, par
 
-    size = 300
+    size = OPT["size"]
     for sweep in range(OPT["sweeps"]):
-        for a in range(0, n - size // 3, size // 2):
-            b = min(n, a + size)
+        heat = OPT["heat"] * (1.0 - 0.8 * sweep / OPT["sweeps"])
+        for a in range(-(sweep * size // 5) % (size // 2) - size // 2, n - size // 3, size // 2):
+            a, b = max(a, 0), min(n, a + size)
             frs = [frame(ops, m["lat"], a, b) for ops, m in zip(sets, GUESS)]
             win = order[a:b]
             cur = [walk(win, fr) for fr in frs]
@@ -791,16 +886,25 @@ def improve(sets, order):
                     continue
                 u, v = pairs[int(rand() * len(pairs))]
                 x, y = win.index(u), win.index(v)
-                front = [v]
-                for z in reversed(win[x:y]):
-                    if any(z in pre[f] or (eng[z] == eng[f] and f != v and eng[z] != "none") for f in front):
-                        front.append(z)
-                if u in front:
-                    continue
-                new = win[:x] + front[::-1] + [z for z in win[x:y] if z not in front] + win[y + 1:]
+                if rand() < OPT["back"]:
+                    back = [u]
+                    for z in win[x + 1:y + 1]:
+                        if any(f in pre[z] for f in back):
+                            back.append(z)
+                    if v in back:
+                        continue
+                    new = win[:x] + [z for z in win[x:y + 1] if z not in back] + back + win[y + 1:]
+                else:
+                    front = [v]
+                    for z in reversed(win[x:y]):
+                        if any(z in pre[f] for f in front):
+                            front.append(z)
+                    if u in front:
+                        continue
+                    new = win[:x] + front[::-1] + [z for z in win[x:y] if z not in front] + win[y + 1:]
                 res = [walk(new, fr) for fr in frs]
                 s = sum(r[0] for r in res)
-                if s < score - OPT["heat"] * math.log(rand() + 1e-9) * (1.0 - move / OPT["moves"]):
+                if s < score - heat * math.log(rand() + 1e-9) * (1.0 - move / OPT["moves"]):
                     win, cur, score = new, res, s
                     if s < best[0]:
                         best = (s, new)
@@ -808,20 +912,21 @@ def improve(sets, order):
     return order
 
 
-GUESS = [{"g": 1.56, "f": 1.25, "pe": 0.42, "lat": 100.0, "link": 70.0},
-         {"g": 1.3, "f": 1.25, "pe": 0.42, "lat": 220.0, "link": 70.0},
-         {"g": 1.3, "f": 1.1, "pe": 0.38, "lat": 60.0, "link": 100.0}]
-
-
-def needs_wait(o, p, kind):
-    if o["kind"] == "c" and p["kind"] == "c" and o["eng"] == p["eng"]:
-        if o["eng"] == "pe":
-            return False
-        return kind == "raw"
-    return True
-
-
+GUESS = [{"g": 1.56, "f": 1.0, "lat": 150.0, "link": 70.0},
+         {"g": 1.1, "f": 1.2, "lat": 100.0, "link": 70.0},
+         {"g": 1.8, "f": 1.35, "lat": 280.0, "link": 100.0}]
 PLAN = {}
+
+
+def bank_turns(ops, order):
+    touch = {}
+    for i in order:
+        o = ops[i]
+        for b in o["banks"]:
+            for e, j in touch.get(b, {}).items():
+                if e != o["eng"]:
+                    o["deps"][j] = "raw"
+            touch.setdefault(b, {})[o["eng"]] = i
 
 
 def plan():
@@ -830,8 +935,9 @@ def plan():
         for m in GUESS[::-1]:
             OPT.update(m)
             sets.append(build())
-        PLAN["ops"] = sets[-1]
         PLAN["order"] = improve(sets[::-1], schedule(sets[-1]))
+        PLAN["ops"] = sets[-1]
+        bank_turns(PLAN["ops"], PLAN["order"])
     return PLAN["ops"], PLAN["order"]
 
 

import math
from concourse.mybir import AluOpType, ActivationFunctionType

AL = AluOpType
AF = ActivationFunctionType
WE = 4080
NCH, NC, WM = 2, 512, 32
STEPS = (16, 8, 4, 2, 1)

MODES = {
    (0, 0): (("1A", "1A", "1A", "1A", "1A"), ("ba", "ba", "ba"), "pp"),
    (0, 1): (("1AC", "1AC", "1AC", "1AC", "1AC"), ("ba", "ba", "ba"), "pp"),
    (0, 2): (("1AC", "1AC", "1AC", "1AC", "1AC"), ("ba", "ba", "ba"), "pp"),
    (1, 0): (("1CB", "1C", "1C", "1C", "1CB"), ("ea", "ea", "ea"), "ww"),
    (1, 1): (("1CB", "1C", "1C", "1C", "1CB"), ("ea", "ea", "ea"), "ww"),
    (1, 2): (("1CB", "1C", "1C", "1C", "1CB"), ("ea", "ea", "ea"), "ww"),
}
OPT = {"sweeps": 8, "heat": 500.0, "moves": 400, "size": 160, "lead": [1500.0] * 6, "pieces": 2, "pslope": "", "back": 0.5, "slack": {"dve": 100.0, "act": 450.0, "pe": 300.0},
       "wdve": (0, 0, 1), "step1": "wp", "relax": ("pp", "vp"), "halves": 1, "strict": False, "early": True, "relay": (384, 384),
       "g": 1.56, "f": 1.0, "pe": 0.42, "lat": 120.0, "link": 70.0, "hbm": 250.0}

SCRATCH = {
    "SA": ("sbuf", [128, 8192], "float32"), "SB": ("sbuf", [128, 8192], "float32"),
    "WO": ("sbuf", [128, 2 * WE], "float32"), "WN": ("sbuf", [128, WE], "float32"), "WP": ("sbuf", [128, WE], "float32"),
    "LND": ("sbuf", [128, 2048], "float32"), "FIN": ("sbuf", [128, 2048 + 32 * NCH], "float32"),
    "FI": ("sbuf", [128, 256], "float32"), "CO": ("sbuf", [128, 32], "float32"), "SM": ("sbuf", [128, 192], "float32"),
    "OB": ("sbuf", [128, 8192], "bfloat16"), "CU": ("sbuf", [128, 4096], "bfloat16"),
    "FL": ("sbuf", [128, 2048 + 32 * NCH], "bfloat16"), "MT": ("sbuf", [128, 128 * 29 + 144 * 4], "bfloat16"),
    "ST": ("sbuf", [128, 1792], "bfloat16"), "CB": ("sbuf", [128, 256], "bfloat16"),
    "OFS": ("sbuf", [128, 64], "uint16"), "CI": ("sbuf", [128, 256], "int32"), "PI": ("sbuf", [128, 4], "int32"),
    "DN": ("dram", [4, 128, 2048], "bfloat16"), "DP": ("dram", [4, 128, 2048], "bfloat16"),
    "DC": ("dram", [128, 256], "bfloat16"), "DU": ("dram", [NCH, 128, 2 * NC], "float32"),
    "DS": ("dram", [NCH, 128, 2 * NC], "float32"),
}
for _k in range(NCH):
    SCRATCH["F%d" % _k] = ("sbuf", [128, 9 * NC + 32], "float32")
    SCRATCH["B%d" % _k] = ("sbuf", [128, 4 * NC + 32], "bfloat16")
    SCRATCH["W%d" % _k] = ("sbuf", [128, 30 * WM], "bfloat16")
    SCRATCH["I%d" % _k] = ("sbuf", [128, 8 * WM], "int32")
    SCRATCH["OF%d" % _k] = ("sbuf", [128, 6 * WM], "uint16")
    for _b in ("XS", "XT", "XK", "V"):
        SCRATCH[_b + str(_k)] = ("psum", [128, 512], "float32")
SEMAPHORES = ["c_pe", "c_act", "c_dve", "c_pool"] + ["s%d" % _i for _i in range(120)]
BYTES = {"float32": 4, "int32": 4, "bfloat16": 2, "uint16": 2}


def R(buf, a, b, step=1):
    return (buf, a, b, step)


def sub(r, a, b, step=1):
    return (r[0], r[1] + a * r[3], min(r[2], r[1] + b * r[3]), step * r[3])


def IND(win, off):
    return ("*", win, off)


def count(r):
    if r[0] == "*":
        return 16 * count(r[2])
    return len(range(r[1], r[2], r[3]))


def is_psum(r):
    return r[0] != "*" and SCRATCH[r[0]][0] == "psum"


def width(r):
    return BYTES[SCRATCH[(r[1] if r[0] == "*" else r)[0]][2]]


def ap(T, r):
    if isinstance(r, tuple):
        if r[0] == "*":
            return ap(T, r[1]).indirect(ap(T, r[2]))
        if r[3] == 1:
            return T[r[0]][:, r[1]:r[2]]
        return T[r[0]][:, r[1]:r[2]:r[3]]
    return r


def parts(rs):
    out = []
    for r in rs:
        if isinstance(r, tuple):
            out.extend([r[1], r[2]] if r[0] == "*" else [r])
    return out


def build():
    ops, hist, groups, nsem, where = [], {}, {}, [0], {"phase": 0, "chunk": -1, "const": True}
    cyc = 0.83 * OPT["f"]

    def new_sem():
        nsem[0] += 1
        return "s%d" % (nsem[0] - 1)

    def add(eng, dur, fn, reads, writes, after=(), kind="c", lat=0.0, **kw):
        i = len(ops)
        deps = {}
        spans = []
        for rs, wr in ((parts(reads), False), (parts(writes), True)):
            for r in rs:
                w = BYTES[SCRATCH[r[0]][2]]
                spans.append((r, wr, w, (r[1] * w) // 16, (r[2] * w + 15) // 16))
        for r, wr, w, lo, hi in spans:
            for (l2, h2, j, w2) in hist.get(r[0], ()):
                if j != i and l2 < hi and lo < h2 and (wr or w2):
                    deps[j] = "raw"
        for r, wr, w, lo, hi in spans:
            h = hist.setdefault(r[0], [])
            if wr and r[3] == 1 and (r[1] * w) % 16 == 0 and (r[2] * w) % 16 == 0:
                h[:] = [x for x in h if not (lo <= x[0] and x[1] <= hi)]
            elif not wr and not where["const"] and r[0] in ("MT", "ST", "FI", "CO", "SM"):
                continue
            h.append((lo, hi, i, wr))
        for j in after:
            deps[j] = "raw"
        o = {"eng": eng, "dur": dur, "fn": fn, "deps": deps, "kind": kind, "lat": lat, "phase": where["phase"],
             "chunk": where["chunk"], "banks": sorted({s[0][0] for s in spans if is_psum(s[0])})}
        o.update(kw)
        ops.append(o)
        return i

    def dve_time(n, c, gather):
        if gather:
            return 50.0 + n * OPT["g"] * cyc
        return 20.0 + max(64.0, n * c) * cyc

    def tt(out, a, b, op):
        c = 1.0 if (is_psum(a) or is_psum(b)) else 2.0
        return add("dve", dve_time(count(out), c, a[0] == "*"),
                   lambda g, T: g.vector.tensor_tensor(ap(T, out), ap(T, a), ap(T, b), op), [a, b], [out])

    def ts(out, a, s1, s2, op0, op1=None):
        c = 0.5 if (width(out) == 2 and width(a) == 2) else 1.0

        def fn(g, T):
            if op1 is None:
                return g.vector.tensor_scalar(ap(T, out), ap(T, a), ap(T, s1), None, op0)
            return g.vector.tensor_scalar(ap(T, out), ap(T, a), ap(T, s1), ap(T, s2), op0, op1)
        return add("dve", dve_time(count(out), c, a[0] == "*"), fn, [a, s1, s2], [out])

    def cp(out, a):
        c = 0.5 if (width(out) == 2 and width(a) == 2) else 1.0
        return add("dve", dve_time(count(out), c, a[0] == "*"),
                   lambda g, T: g.vector.tensor_copy(ap(T, out), ap(T, a)), [a], [out])

    def ms(out, v):
        return add("dve", dve_time(count(out), width(out) / 4.0, False),
                   lambda g, T: g.vector.memset(ap(T, out), v), [], [out])

    def act(out, a, func=None, scale=1.0, bias=0.0):
        func = func or (AF.Copy if bias == 0.0 else AF.Identity)
        n = count(out)
        d = 65.0 + n * OPT["g"] * cyc if a[0] == "*" else 60.0 + max(64, n) * cyc
        return add("act", d, lambda g, T: g.scalar.activation(ap(T, out), ap(T, a), func, bias=ap(T, bias), scale=ap(T, scale)),
                   [a, scale, bias], [out])

    def mm(items, start=True, stop=True):
        bank = items[0][0][0]
        d = 30.0 + sum(max(64, count(r)) * (4 if width(r) == 4 else 1) * OPT["pe"] * OPT["f"] for _, _, r in items)
        new, head = [], None
        for o, _, _ in items:
            new.append(start and (head is None or head[3] > 1 or o[1] < head[1] or o[2] > head[2]))
            head = o if new[-1] else head

        def fn(g, T):
            ins = None
            for n, (o, l, r) in enumerate(items):
                ins = g.tensor.matmul(ap(T, o), ap(T, l), ap(T, r), new[n], (new + [stop])[n + 1])
            return ins
        i = add("pe", d, fn, [x for _, l, r in items for x in (l, r)], [o for o, _, _ in items])
        if bank[0] == "X":
            if bank in groups:
                ops[i]["deps"].setdefault(groups[bank], "ord")
            groups[bank] = i
            if not stop and (OPT["strict"] or bank[1] == "K"):
                ops[i]["deps"].update({x[2]: "raw" for x in hist[bank] if x[2] != i})
        return i

    def iota(out, pattern, base, cm):
        def fn(g, T):
            if SCRATCH[out[0]][2] == "int32":
                return g.iota(ap(T, out), pattern, base, cm)
            return g.iota(ap(T, out), pattern, base, cm, allow_small_or_imprecise_dtypes=True)
        return add("pool", 130.0 + 2 * count(out) * cyc, fn, [], [out])

    def dma(q, pairs, reads, writes, nbytes, after=()):
        return add(q, 700.0 if q == "pool" else 100.0, pairs, reads, writes, after, "dma",
                   1800.0 + nbytes / OPT["hbm"], sem=new_sem(), res="hbm" if nbytes > 200000 else "small", busy=nbytes / OPT["hbm"])

    def send(to, src, dst, src_r, dst_r, nbytes, relay=None, after=()):
        if relay is not None:
            i = add("pool", 300.0, (src, dst), src_r, [], after, "send", 1500.0 + 0.7 * nbytes / OPT["link"],
                    sem=new_sem(), rsem=new_sem(), hsem=new_sem(), relay=relay, to=to, res="relay", busy=nbytes / OPT["link"])
            add("none", 0.0, None, [], dst_r, [i], "recv", 2500.0 + nbytes / OPT["link"], sem=ops[i]["rsem"], to=to, relay=relay)
            return i
        i = add("pool", 300.0, (src, dst), src_r, [], after, "send", 1500.0 + nbytes / OPT["link"],
                sem=new_sem(), rsem=new_sem(), to=to, res="link%d" % to, busy=nbytes / OPT["link"])
        add("none", 0.0, None, [], dst_r, [i], "recv", 500.0, sem=ops[i]["rsem"], to=to)
        return i

    def sbsend(to, src, dst, relay=None, after=()):
        return send(to, lambda T: ap(T, src), lambda T: ap(T, dst), [src], [dst], 128 * count(src) * width(src), relay, after)

    used = {"MT": 0, "ST": 0, "SM": 0}

    def tile(buf, n):
        used[buf] += n
        return R(buf, used[buf] - n, used[buf])
    mat = lambda: tile("MT", 128)
    col = lambda: sub(tile("SM", 4), 0, 1)
    I1, In, IL, IU, UP, DN_, BO, N2, N3, KC = [mat() for _ in range(10)]
    TM = {s: mat() for s in STEPS}
    S = {1: (IL, UP), 8: (mat(), mat())}
    D = {1: (mat(), mat()), 8: (mat(), mat())}
    SP = [mat() for _ in range(8)]
    Z8, ZL, ZC = tile("MT", 144), tile("MT", 144), [tile("MT", 144), tile("MT", 144)]
    FIp, FIn = R("FI", 0, 128), R("FI", 128, 256)
    ZT, IO, QG = tile("ST", 512), tile("ST", 128), tile("ST", 128)
    CS = {s: tile("ST", 128) for s in STEPS}
    CN = [tile("ST", 64) for _ in range(3)]
    FOUR, H4, HB = tile("ST", 64), tile("ST", 64), tile("ST", 64)
    MC, PG, MK0, MK1, M4, M8, SG, TMP = [col() for _ in range(8)]
    BIAS = {s: col() for s in STEPS}
    LO, HI = [col() for _ in range(3)], [col() for _ in range(3)]
    RM = [col() for _ in range(8)]
    C64 = tile("SM", 64)
    CO_O, CO_P, CO_N = [[R("CO", a + j, a + j + 1) for j in range(3)] + [R("CO", b, b + 1)] for a, b in ((0, 16), (8, 20), (12, 24))]
    CUW = R("CU", 0, 4096)
    n, w, N = NC, WM, 2 * WM

    def chunk(k):
        d = {"k": k, "i0": n * k, "held": None}
        for j, nm in enumerate(("tb", "sb", "ta", "sa", "T1", "S1", "A", "Q", "Cw")):
            d[nm] = R("F%d" % k, n * j, n * j + n)
        d["new"], d["D"] = R("F%d" % k, 0, 2 * n), R("F%d" % k, 9 * n, 9 * n + 32)
        for j, nm in enumerate(("yes", "Q16", "ta16", "sa16")):
            d[nm] = R("B%d" % k, n * j, n * j + n)
        d["first"], d["Cg"] = R("B%d" % k, 2 * n, 4 * n + w), d["Q16"]
        for j, nm in enumerate(("r", "Lw", "v0", "v1", "v2", "l1", "qh", "par", "a", "lm")):
            d[nm] = R("W%d" % k, N * j, N * j + N)
        d["al"] = R("W%d" % k, 8 * N, 10 * N)
        d["BH"] = [R("W%d" % k, (10 + 2 * j) * N, (12 + 2 * j) * N) for j in range(2)]
        v, of = "V%d" % k, "OF%d" % k
        d["VO"], d["room"], d["base"], d["V"] = R(v, 0, N), R(v, N, 3 * N), R(v, 3 * N, 5 * N), R(v, 5 * N, 6 * N)
        d["off"], d["x"], d["off1"], d["both"] = R(of, 0, w), R(of, w, N), R(of, N, N + w), R(of, 0, N)
        d["XS"], d["XT"], d["K"] = R("XS%d" % k, 0, n), R("XT%d" % k, 0, n), R("XK%d" % k, 0, n)
        f0 = (2 * n + w) * k
        d["fT"], d["fS"], d["fC"], d["fl"] = R("FL", f0, f0 + n), R("FL", f0 + n, f0 + 2 * n), R("FL", f0 + 2 * n, f0 + 2 * n + w), R("FL", f0, f0 + 2 * n + w)
        d["lnd"] = R("LND", 2 * n * k, 2 * n * k + 2 * n)
        d["kept"], d["finD"] = R("FIN", 2 * n * k, 2 * n * k + 2 * n), R("FIN", 2048 + w * k, 2048 + w * k + w)
        d["of"] = R(of, 0, 3 * w)
        d["own"] = dict(d, of=R(of, 3 * w, 6 * w), off=R(of, 3 * w, 4 * w), off1=R(of, 5 * w, 6 * w), v2=R("W%d" % k, 14 * N, 15 * N),
                        ta=sub(d["kept"], 0, n), sa=sub(d["kept"], n, 2 * n), tb=sub(d["lnd"], 0, n), sb=sub(d["lnd"], n, 2 * n))
        return d
    C = [chunk(k) for k in range(NCH)]

    def each():
        for c in C:
            where["chunk"] = c["k"]
            yield c
        where["chunk"] = -1

    ld_cu = dma("sync", lambda T: [(T.CI[:], T.cu[:])], [], [R("CI", 0, 256)], 131072)
    ld_co = dma("act", lambda T: [(T.CO[:, 0:3], T.co[:]), (T.CO[0:112, 4:7], T.co[16:128, :]), (T.CO[112:128, 4:7], T.co[0:16, :])],
                [], [R("CO", 0, 8)], 4096)
    before = [ld_cu, ld_co]
    for c in C:
        a, b = 4 * c["i0"], 4 * c["i0"] + 4 * n
        for q, name, o in (("sync", "te", 0), ("act", "sa", 4096)):
            i_ = dma(q, lambda T, name=name, a=a, b=b, o=o: [(T.OB[:, o + a:o + b], T[name][:, a:b])], [], [R("OB", o + a, o + b)], 256 * (b - a))
            ops[i_]["behind"] = list(before)
            before.append(i_)
    sbsend(-1, R("CO", 4, 7), R("CO", 12, 15))
    sbsend(1, R("CO", 0, 3), R("CO", 8, 11))

    ms(CUW, 0.0)
    ms(ZT, 0.0)
    cp(R("CB", 0, 256), R("CI", 0, 256))
    dma("sync", lambda T: [(T.CU[0:128:16, :], T.CB[:])], [R("CB", 0, 256)], [CUW], 65536)
    iota(MC, [[0, 1]], 0, 1)
    iota(C64, [[64, 64]], 0, 0)
    iota(IO, [[1, 128]], 0, -1)
    iota(QG, [[1, 8], [0, 16]], 0, 0)
    iota(R("SB", 0, 256), [[2, 256]], 0, 0)
    iota(H4, [[0, 8], [32, 8]], 0, 0)
    iota(HB, [[256, 16], [0, 4]], 0, 0)
    ts(PG, MC, -7.5, 0.0625, AL.add, AL.mult)
    PGI = R("PI", 0, 1)
    cp(PGI, PG)
    cp(PG, PGI)
    ts(TMP, PG, -16.0, None, AL.mult)
    tt(MC, MC, TMP, AL.add)
    ts(M4, MC, 4.0, None, AL.mult)
    ts(R("OFS", 0, 64), C64, M4, None, AL.add)
    ts(I1, IO, 0.0, None, AL.is_equal)
    for r in range(2):
        ms(ZC[r], 0.0)
        ts(sub(ZC[r], 16, 144, 16), sub(I1, r, 128, 16), 256.0, None, AL.mult)
    ts(MK0, MC, 8.0, None, AL.is_lt)
    ts(MK1, MC, 8.0, None, AL.is_ge)
    ts(SG, MK1, 2.0, -1.0, AL.mult, AL.add)
    ts(M8, MK1, -8.0, MC, AL.mult, AL.add)
    ts(TMP, M8, 4.0, None, AL.mult)
    ts(H4, H4, TMP, None, AL.add)
    act(In, I1, scale=-1.0)
    ts(IL, I1, MK0, None, AL.mult)
    ts(IU, I1, MK1, None, AL.mult)
    ts(UP, IO, 8.0, MK0, AL.is_equal, AL.mult)
    ts(DN_, IO, -8.0, MK1, AL.is_equal, AL.mult)
    tt(D[1][0], IL, DN_, AL.subtract)
    tt(D[1][1], UP, IU, AL.subtract)
    tt(N2, UP, IL, AL.subtract)
    tt(N3, D[1][1], D[1][0], AL.subtract)
    act(KC, D[1][1], scale=-1.0)
    for a in range(2):
        act(S[8][a], S[1][a], scale=8.0)
        act(D[8][a], D[1][a], scale=8.0)
    ts(BO, QG, PG, None, AL.is_equal)
    ms(Z8, 0.0)
    cp(sub(Z8, 8, 136, 8), sub(BO, 0, 128, 8))
    ms(ZL, 0.0)
    cp(sub(ZL, 8, 136, 16), sub(BO, 0, 128, 16))
    ts(FOUR, sub(ZT, 0, N), MK1, -254.0, AL.add, AL.mult)
    for s in STEPS:
        ts(TM[s], I1, SG, 0.5 / s, AL.mult, AL.mult)
        ts(BIAS[s], MK1, -2.0 * s, -16.0 * s, AL.mult, AL.add)
        ts(sub(CS[s], 0, N), FOUR, 1.0 * s, None, AL.add)
        ts(sub(CS[s], N, 2 * N), sub(ZT, 0, N), MK0, -1.0 * s, AL.add, AL.mult)
    ts(TMP, MK0, -8.5, None, AL.mult)
    for j, (up, dl) in enumerate(((-0.5, 0.25), (0.0, 0.125), (0.0625, 0.0625))):
        ts(HI[j], MK1, up, TMP, AL.mult, AL.add)
        ts(CN[j], sub(ZT, 0, N), HI[j], None, AL.add)
        ts(HI[j], MK1, 2.0 - dl, dl, AL.mult, AL.add)
        ts(LO[j], HI[j], -1.0, None, AL.mult)
    ms(FOUR, 4.0)
    for m in range(8):
        ts(RM[m], M8, 1.0 * m, SG, AL.is_equal, AL.mult)
        ts(RM[m], RM[m], -1.0, None, AL.mult)
        act(SP[m], BO, scale=RM[m])
    act(FIp, I1)
    act(FIn, I1, scale=-1.0)
    for co in (CO_O, CO_P, CO_N):
        act(co[3], co[2], scale=-1.0)

    def wrapped(out, mats, t):
        return [(out, mats[0], sub(t, 0, N, 2)), (out, mats[1], sub(t, 1, N, 2))]

    def casts(c, out, off, row, win=CUW):
        act(c["Cg"], IND(win, off))
        return [(out, sub(ZC[row], 16 - m, 144 - m), sub(c["Cg"], m, n, 16)) for m in range(16)]

    firsts = []
    for c in each():
        a, pw = 4 * c["i0"], sub(c["base"], 0, w)
        mm(casts(c, pw, R("OFS", w * c["k"], w * c["k"] + w), 0))
        act(sub(c["first"], 2 * n, 2 * n + w), pw)
        cp(c["ta16"], R("OB", a, a + 4 * n, 4))
        act(c["sa16"], R("OB", 4096 + a, 4096 + a + 4 * n, 4))
        firsts.append(sbsend(1, c["ta16"], c["fT"]))
        firsts.append(sbsend(1, sub(c["first"], n, 2 * n + w), sub(c["fl"], n, 2 * n + w)))
    prev = firsts[-1]
    for to, name in ((-1, "DN"), (1, "DP")):
        for j in range(4):
            src = R("OB", 2048 * j, 2048 * j + 2048)
            prev = send(to, lambda T, src=src: ap(T, src), lambda T, name=name, j=j: T[name][j], [src],
                        [R(name, 64 * j, 64 * j + 64)], 1 << 19)
            ops[prev]["behind"] = firsts
    i_ = send(1, lambda T: T.CB[:], lambda T: T.DC[:], [R("CB", 0, 256)], [R("DC", 0, 256)], 65536)
    ops[i_]["behind"] = firsts
    dma("sync", lambda T: [(T.CU[1:128:16, :], T.DC[:])], [R("DC", 0, 256)], [CUW], 65536)

    for a, b in ((256, 512), (512, 1024), (1024, 2048), (2048, 3072), (3072, WE)):
        base = 2048 if a >= 2048 else a
        act(R("SB", a, b), R("SB", a - base, b - base), bias=float(2 * base))
    for a in range(0, WE, 680):
        ts(R("WO", a, a + 680), R("SB", a, a + 680), CO_O[1], CO_O[0], AL.mult, AL.add)

    def weights(h, j):
        name, base, odd, co = (("WN", 0, 0, CO_N), ("WP", 0, 0, CO_P), ("WO", WE, 1, CO_O))[h]
        gate = len(ops) - 1
        o = R(name, base + 510 * j, base + 510 * j + 510)
        ops[iota(o, [[2, 510]], 1020 * j + odd, 0)]["behind"] = [prev]
        if OPT["wdve"][h]:
            ops[ts(o, o, co[1], co[0], AL.mult, AL.add)]["behind"] = [gate]
        else:
            ops[act(o, o, scale=co[1])]["behind"] = [gate]
            act(o, o, func=AF.Identity, bias=co[0])
    where["const"] = False

    def table(buf):
        return R(buf, 0, 4096), R(buf, 4096, 8192)

    def load_table(buf, src, shifted):
        for j in range(4):
            def pairs(T, j=j):
                o, a, b = T[buf], 2048 * j, 2048 * j + 2048
                if src is None:
                    return [(o[:, a:b], T[("te", "sa")[j // 2]][:, a % 4096:a % 4096 + 2048])]
                if not shifted:
                    return [(o[:, a:b], T[src][j])]
                return [(o[0:112, a:b], T[src][j, 16:128, :]), (o[112:128, a:b], T[src][j, 0:16, :])]
            dma("pool", pairs, [] if src is None else [R(src, 64 * j, 64 * j + 64)], [R(buf, 2048 * j, 2048 * j + 2048)], 1 << 20)

    def put_new(buf, c, src):
        for j in range(2):
            a = 4096 * j + 4 * c["i0"]
            act(R(buf, a, a + 4 * n, 4), sub(src, n * j, n * j + n))

    def hand_back(c, src, spare, after=()):
        cut, dst = OPT["relay"][c["k"]], c["lnd"]
        sbsend(-1, sub(src, n, n + cut), sub(dst, n, n + cut), R("SA", spare, spare + cut), after)
        i = sbsend(-1, sub(src, 0, n), sub(dst, 0, n), None, after)
        if cut < n:
            i = sbsend(-1, sub(src, n + cut, 2 * n), sub(dst, n + cut, 2 * n), None, after)
        return i

    ident = lambda v, sign: (I1 if sign > 0 else In) if width(v) == 2 else (FIp if sign > 0 else FIn)

    def vote(c, Z, terms):
        VO = c["VO"]
        mm([(VO, l, r) for l, r in terms] + [(VO, sub(Z, 8 - m, 136 - m), sub(c["yes"], m, n, 8)) for m in range(8)])

    def spread(c, v):
        mm([(sub(c["K"], m, n, 8), SP[m], v) for m in range(8)])

    def room(c, s, lo, r=None):
        both = c["room"]
        pa, pl = sub(both, 0, N), sub(both, N, 2 * N)
        mm([(both, I1, CS[s]), (pa, N2, lo), (pl, IL, lo)] + ([(pa, N3, r), (pl, D[1][0], r)] if r else []))
        act(c["al"], both, func=AF.Relu)

    def bases(c, BH, base, lo, more=()):
        items = base(sub(c["base"], 0, w)) + wrapped(sub(c["base"], w, N), S[8], lo)
        for j, t in enumerate(more):
            items += wrapped(sub(c["base"], (2 + j) * w, (3 + j) * w), S[1], t)
        mm(items)
        end = (2 + len(more)) * w
        act(sub(BH, 0, end), sub(c["base"], 0, end))

    def offsets(c, BH, dq, lo, r=None, four=False):
        V = sub(c["K"], 256, 256 + N) if r and OPT["early"] else c["V"]
        p0, px = sub(V, 0, w), sub(V, w, N)
        known = [(V, I1, sub(BH, 0, N))] + dq(px) + ([(px, I1, sub(FOUR, 0, w))] if four else []) + wrapped(p0, S[1], lo) + wrapped(px, S[8], lo)
        voted = wrapped(p0, D[1], r) + wrapped(px, D[8], r) if r else []
        if r and OPT["early"]:
            mm(known, stop=False)
            mm(voted, start=False)
        else:
            mm(known + voted)
        cp(c["both"], V)
        return p0

    def search(c, s, mode, tabs, W, co, T1, S1, BH, dq):
        XS, XT, A = c["XS"], c["XT"], c["A"]
        Tg, Sg, Wg = IND(tabs[0], c["off"]), IND(tabs[1], c["off"]), IND(W, c["x"])
        if mode[0] != "1" and c["held"] != T1:
            mm([(XT, ident(T1, 1), T1)])
            c["held"] = T1
        cuts = ((0, n // 2), (n // 2, n))
        tcuts = cuts if OPT["halves"] > 1 else ((0, n),)
        banks = [sub(bank, 0, b - a) for bank, (a, b) in zip((XS, c["K"]), cuts)]
        part = lambda g_, a, b: IND(g_[1], sub(g_[2], a // 16, b // 16))
        for X, (a, b), how in zip(banks, cuts, (mode[1], mode[-1])):
            if how == "B":
                tt(sub(c["Q"], a, b), part(Sg, a, b), sub(S1, a, b), AL.subtract)
                if mode[0] != "3":
                    act(X, sub(c["Q"], a, b), scale=co[2])
                continue
            Q = sub(c["Q16"] if where["phase"] < 6 else c["Q"], a, b)
            if how == "A":
                mm([(X, ident(S1, 1), sub(S1, a, b))], stop=False)
            else:
                mm([(X, I1, sub(ZT, 0, b - a))], stop=False)
                act(X, sub(S1, a, b))
            act(Q, part(Sg, a, b))
            mm([(X, ident(Q, -1), Q)], start=False)
            act(X, X, scale=co[3])
        for a, b in tcuts:
            if mode[0] == "1":
                tt(sub(A, a, b), part(Tg, a, b), sub(T1, a, b), AL.subtract)
            else:
                act(sub(A, a, b), part(Tg, a, b))
                if mode[0] == "2":
                    tt(sub(A, a, b), sub(A, a, b), sub(XT, a, b), AL.subtract)
        if mode[0] != "3":
            for a, b in tcuts:
                tt(sub(A, a, b), part(Wg, a, b), sub(A, a, b), AL.mult)
        else:
            for X, (a, b) in zip(banks, cuts):
                act(sub(c["Cw"], a, b), part(Wg, a, b))
                tt(X, sub(A, a, b), sub(XT, a, b), AL.subtract)
                tt(sub(A, a, b), sub(c["Cw"], a, b), X, AL.mult)
                act(X, sub(c["Q"], a, b), scale=co[2])
        for X, (a, b) in zip(banks, cuts):
            tt(sub(c["yes"], a, b), sub(A, a, b), X, AL.is_gt)
        vote(c, Z8, [(TM[s], c["a"])])
        act(c["r"], c["VO"], func=AF.Relu, scale=2.0 * s, bias=BIAS[s])
        p0 = offsets(c, BH, dq, c["lm"], c["r"], s == 1)
        if s > 1:
            room(c, s // 2, c["lm"], c["r"])
        else:
            ts(c["off1"], p0, 1.0, None, AL.add)
            mm([(c["VO"], IL, c["lm"]), (c["VO"], D[1][0], c["r"])])
            act(c["Lw"], c["VO"])

    def slopes(c, tabs):
        lo = (c["ta16"], c["sa16"]) if where["phase"] < 6 else (c["ta"], c["sa"])
        for j in (1, 0):
            act(lo[j], IND(tabs[j], c["off"]))
            if where["phase"] < 6 and "TS"[j] in OPT["pslope"]:
                act(c["Q16"], IND(tabs[j], c["off1"]))
                mm([(c["K"], I1, c["Q16"]), (c["K"], In, lo[j])])
                act(c[("tb", "sb")[j]], c["K"])
            else:
                tt(c[("tb", "sb")[j]], IND(tabs[j], c["off1"]), lo[j], AL.subtract)
        return lo

    def between(c, side, lo, slope, v, by_pe, minus=None):
        X = c["X" + side]
        if side == "T":
            c["held"] = None
        if by_pe:
            mm([(X, I1, ZT)], stop=False)
        if v is None:
            act(X, slope, scale=0.5)
        else:
            tt(X, slope, c["K"], AL.mult)
        if by_pe:
            items = []
            for t, sign in ((lo, 1), (minus, -1)):
                m = OPT["pieces"] if t and width(t) == 4 else 1
                items += [(sub(X, n * j // m, n * (j + 1) // m), ident(t, sign), sub(t, n * j // m, n * (j + 1) // m)) for j in range(m) if t]
            for j, item in enumerate(items):
                mm([item], start=False, stop=j == len(items) - 1)
        else:
            tt(X, X, lo, AL.add)
            if minus:
                tt(X, X, minus, AL.subtract)

    def refine(c, j, mode, lo, W, co, T1, S1, BH, dq):
        XS, XT, A = c["XS"], c["XT"], c["A"]
        v = c["v%d" % (j - 1)] if j else None
        Wg = IND(W, c["x"])
        mt, ms_ = mode
        if j:
            spread(c, v)
        between(c, "S", lo[1], c["sb"], v, ms_ in "ab", S1 if ms_ != "b" else None)
        if ms_ == "b":
            tt(XS, XS, S1, AL.subtract)
        act(XS, XS, scale=co[2])
        between(c, "T", lo[0], c["tb"], v, mt in "abc", T1 if mt == "c" else None)
        if mt in "ad":
            tt(A, XT, T1, AL.subtract)
            tt(A, Wg, A, AL.mult)
        else:
            act(c["Cw"], Wg)
            if mt != "c":
                tt(XT, XT, T1, AL.subtract)
            tt(A, c["Cw"], XT, AL.mult)
        tt(c["yes"], A, XS, AL.is_gt)
        vote(c, ZL, [(I1, CN[j])] + ([(KC, v)] if j else []))
        ts(c["v%d" % j], c["VO"], LO[j], HI[j], AL.max, AL.min)
        if j < 2:
            px = sub(c["V"], w, N)
            mm([(px, I1, sub(BH, w, N)), (px, I1, sub(FOUR, 0, w))] + dq(px) + wrapped(px, S[8], c["Lw"])
               + [x for i in range(j + 1) for x in wrapped(px, S[8], c["v%d" % i])])
            cp(c["x"], px)

    def final(c, mode, lo, v):
        spread(c, v)
        for side, j, slope in (("S", 1, c["sb"]), ("T", 0, c["tb"])):
            X, out = c["X" + side], c[side + "1"]
            if mode[j] == "w":
                tt(X, slope, c["K"], AL.mult)
                tt(out, X, lo[j], AL.add)
            else:
                between(c, side, lo[j], slope, v, mode[j] == "p")
                act(out, X)
        c["held"] = None if mode[0] == "w" else c["T1"]

    def relax(c, mode, lo, v, olds, new):
        spread(c, v)
        for side, j, slope in (("S", 1, c["sb"]), ("T", 0, c["tb"])):
            X = c["X" + side]
            between(c, side, lo[j], slope, v, mode[j] == "p", olds[j])
            act(X, X, scale=0.25)
            tt(sub(new, n * j, n * j + n), X, olds[j], AL.add)

    fraction = lambda c: (lambda px: wrapped(px, D[8], c["v2"]))

    def hop(c, rnd, h, tabs, W, co, T1, S1, dq):
        modes = MODES[(rnd, h)]
        where["phase"] = 2 * (3 * rnd + h)
        BH, nxt = c["BH"][h % 2], c["BH"][1 - h % 2]
        aside = (rnd, c["k"]) == (0, 0) and h < 2
        for j, s in enumerate(STEPS):
            if aside:
                weights(h, j)
            search(c, s, modes[0][j], tabs, W, co, T1, S1, BH, dq)
        where["phase"] += 1
        if (rnd, h) == (1, 2):
            sbsend(-1, c["of"], c["own"]["of"])
        lo = slopes(c, tabs)
        if h < 2:
            home = sub(HB, w * c["k"], w * c["k"] + w)
            bases(c, nxt, (lambda o: casts(c, o, c["off"], 0)) if h == 0 else (lambda o: [(o, I1, home)]), c["Lw"])
            room(c, 16, c["Lw"])
        for j in range(3):
            if aside:
                weights(h, 5 + j)
            refine(c, j, modes[1][j], lo, W, co, T1, S1, BH, dq)
        if h < 2:
            offsets(c, nxt, fraction(c), c["Lw"])
            final(c, modes[2], lo, c["v2"])
        return lo

    WOE, WOF, WNn, WPp = R("WO", 0, WE), R("WO", 0, 2 * WE), R("WN", 0, WE), R("WP", 0, WE)

    load_table("SA", "DN", True)
    for c in each():
        bases(c, c["BH"][0], lambda o: [(o, I1, c["fC"])], H4)
        offsets(c, c["BH"][0], lambda px: [], H4)
        room(c, 16, H4)
        hop(c, 0, 0, table("OB"), WOE, CO_O, c["fT"], c["fS"], lambda px: [])
    load_table("SB", "DP", False)
    for c in each():
        hop(c, 0, 1, table("SA"), WNn, CO_N, c["T1"], c["S1"], fraction(c))
    load_table("SA", None, False)
    for c in each():
        lo = hop(c, 0, 2, table("SB"), WPp, CO_P, c["T1"], c["S1"], fraction(c))
        VO = c["VO"]
        mm([(VO, I1, H4), (VO, I1, c["Lw"]), (VO, D[1][0], c["v2"])])
        di, d1, d2, d3 = [R("I%d" % c["k"], N * j, N * j + N) for j in range(4)]
        ts(di, VO, 8.0, None, AL.mult)
        relax(c, OPT["relax"][0], lo, c["v2"], (c["fT"], c["fS"]), c["kept"])
        c["sent"] = hand_back(c, c["kept"], c["i0"])
        ts(d1, di, 4, None, AL.arith_shift_right)
        ts(d2, di, 15, 1, AL.bitwise_and, AL.logical_shift_right)
        ts(d3, di, 1, None, AL.bitwise_and)
        ts(di, di, 15, None, AL.bitwise_and)
        cp(c["l1"], d1)
        cp(c["qh"], d2)
        ts(c["par"], d3, float(WE), None, AL.mult)
        ts(c["v0"], di, 0.0625, MK0, AL.mult, AL.mult)
    for c in each():
        put_new("SB", c, c["kept"])
    for c in each():
        k = c["k"]
        i_ = send(2, lambda T, c=c: ap(T, c["kept"]), lambda T, k=k: T.DU[k], [c["kept"]], [R("DU", 64 * k, 64 * k + 64)], 1024 * n)
        ops[i_]["behind"] = [x["sent"] for x in C]

    where["phase"] = 6
    for c in each():
        p0, l1, a, b = sub(c["V"], 0, w), c["l1"], 4 * c["i0"], 4 * (c["i0"] + n)
        mm([(p0, I1, sub(HB, 0, w))] + wrapped(p0, S[1], l1))
        cp(c["off"], p0)
        ts(c["off1"], p0, 1.0, None, AL.add)
        lo = slopes(c, [sub(t_, a, b) for t_ in table("SB")])
        BH = c["BH"][0]
        bases(c, BH, lambda o: casts(c, o, c["off"], 1, sub(CUW, a, b)), l1, (c["qh"], c["par"]))
        c["odd"] = lambda px, BH=BH: [(px, I1, sub(BH, j * w, j * w + w)) for j in (2, 3)]
        offsets(c, BH, c["odd"], l1)
        room(c, 16, l1)
        final(c, OPT["step1"], lo, c["v0"])
        for j in range(4):
            weights(2, 4 * c["k"] + j)
    for c in each():
        put_new("SA", c, c["lnd"])
        dma("sync", lambda T, c=c: [(T.DS[c["k"]], ap(T, c["lnd"]))], [c["lnd"]], [R("DS", 64 * c["k"], 64 * c["k"] + 64)], 1024 * n)
    load_table("SB", "DN", True)
    for c in each():
        def shifted(T, c=c):
            a, b, k = c["lnd"][1], c["lnd"][2], c["k"]
            return [(T.LND[0:112, a:b], T.DU[k, 16:128, :]), (T.LND[112:128, a:b], T.DU[k, 0:16, :])]
        dma("sync", shifted, [R("DU", 64 * c["k"], 64 * c["k"] + 64)], [c["lnd"]], 1024 * n)
        put_new("SB", c, c["lnd"])
        dma("sync", lambda T, c=c: [(ap(T, c["lnd"]), T.DS[c["k"]])], [R("DS", 64 * c["k"], 64 * c["k"] + 64)], [c["lnd"]], 1024 * n)
    for c in each():
        hop(c, 1, 0, table("SA"), WOF, CO_O, c["T1"], c["S1"], c["odd"])
    load_table("SA", "DP", False)
    for c in each():
        put_new("SA", c, c["kept"])
    for c in each():
        hop(c, 1, 1, table("SB"), WNn, CO_N, c["T1"], c["S1"], fraction(c))
    load_table("SB", None, False)
    for c in each():
        put_new("SB", c, c["lnd"])
    for c in each():
        hop(c, 1, 2, table("SA"), WPp, CO_P, c["T1"], c["S1"], fraction(c))
        px, i0, ld = sub(c["V"], w, N), c["i0"], c["finD"]
        mm(wrapped(px, S[8], c["Lw"]) + wrapped(px, S[8], c["l1"]) + wrapped(px, S[1], c["qh"]) + wrapped(px, D[8], c["v2"]))
        add("dve", 80.0, lambda g, T, c=c, px=px: g.vector.transpose(ap(T, c["D"]), ap(T, px)), [px], [c["D"]])
        sbsend(-1, c["D"], ld)
        dma("sync", lambda T, ld=ld, i0=i0: [(T.yd[gg, i0:i0 + n], T.FIN[32 * (gg // 2):32 * (gg // 2) + 32, ld[1] + 16 * (gg % 2):ld[1] + 16 * (gg % 2) + 16])
                                             for gg in range(8)], [ld], [], 16384)
        own = c["own"]
        sbsend(-1, c["v2"], own["v2"])
        lo = slopes(own, table("SB"))
        relax(own, OPT["relax"][1], lo, own["v2"], [R("SB", o + 4 * i0 + 1, o + 4 * (i0 + n), 4) for o in (0, 4096)], c["lnd"])
        for name, ld in (("ys", own["sb"]), ("yt", own["tb"])):
            dma("sync", lambda T, ld=ld, name=name, i0=i0: [(T[name][:, i0:i0 + n], ap(T, ld))], [ld], [], 512 * n)
    return ops


def needs_wait(o, p, kind):
    if o["kind"] == "c" and p["kind"] == "c" and o["eng"] == p["eng"]:
        return o["eng"] != "pe" and kind == "raw"
    return True


def schedule(ops):
    n = len(ops)
    succ = [[] for _ in ops]
    pre = [set(o["deps"]) | set(o.get("behind", ())) for o in ops]
    for i in range(n):
        for j in pre[i]:
            succ[j].append(i)
    lat = OPT["lat"]
    prio = [0.0] * n
    for i in range(n - 1, -1, -1):
        o = ops[i]
        prio[i] = o["dur"] + o["lat"] + max([prio[s] + lat for s in succ[i]] or [0.0])
    for i, o in enumerate(ops):
        if o["chunk"] >= 0:
            prio[i] += OPT["lead"][o["phase"] // 2] * (NCH - 1 - o["chunk"])
    left = [len(p) for p in pre]
    ready = {e: [] for e in ("pe", "act", "dve", "pool", "sync", "none")}
    est, end = [0.0] * n, [0.0] * n
    for i, o in enumerate(ops):
        if not left[i]:
            ready[o["eng"]].append(i)
    free = {e: 0.0 for e in ready}
    res, touch, order = {}, {}, []

    def others(i):
        return [j for b in ops[i]["banks"] for e, j in touch.get(b, {}).items() if e != ops[i]["eng"]]

    while len(order) < n:
        best = None
        for e, lst in ready.items():
            if lst:
                at = {i: max([est[i]] + [end[j] + lat for j in others(i)]) for i in lst}
                t0 = max(free[e], min(at.values()))
                if best is None or t0 < best[0]:
                    best = (t0, e, at)
        t0, e, at = best
        i = max((j for j in ready[e] if at[j] <= t0 + OPT["slack"].get(e, 0.0)), key=lambda j: (prio[j], -j))
        ready[e].remove(i)
        o = ops[i]
        for b in o["banks"]:
            touch.setdefault(b, {})[e] = i
        issued = max(t0, at[i]) + o["dur"]
        if e != "none":
            free[e] = issued
        end[i] = issued + o["lat"]
        if "res" in o:
            r0 = max(res.get(o["res"], 0.0), issued)
            res[o["res"]] = r0 + o["busy"]
            end[i] = r0 + o["lat"]
        order.append(i)
        for j in succ[i]:
            kind = ops[j]["deps"].get(i)
            t = end[i] + lat if kind is not None and needs_wait(o, ops[j], kind) else issued
            est[j] = max(est[j], t)
            left[j] -= 1
            if not left[j]:
                ready[ops[j]["eng"]].append(j)
    return order


def improve(sets, order):
    n = len(order)
    eng = [o["eng"] for o in sets[0]]
    banks = [o["banks"] for o in sets[0]]
    pre = [set(o["deps"]) | set(o.get("behind", ())) for o in sets[0]]
    waits = [[(j, o["deps"].get(j) is not None and needs_wait(sets[0][j], o, o["deps"][j])) for j in sorted(pre[i])] for i, o in enumerate(sets[0])]
    seed = [12345]

    def rand():
        seed[0] = (seed[0] * 1103515245 + 12345) % 2147483648
        return (seed[0] >> 8) / 8388608.0

    def frame(ops, lat, a, b):
        st, tot, free, res, touch = [0.0] * n, [0.0] * n, {}, {}, {}
        first, used = {}, {}
        for pos, i in enumerate(order):
            if pos == a:
                first, used = dict(free), {k: dict(v) for k, v in touch.items()}
            o = ops[i]
            t = free.get(eng[i], 0.0)
            for j, w in waits[i]:
                t = max(t, st[j] + (tot[j] + lat if w else ops[j]["dur"]))
            for k in banks[i]:
                for e, v in touch.setdefault(k, {}).items():
                    if e != eng[i]:
                        t = max(t, v)
            st[i] = t
            tot[i] = o["dur"] + o["lat"]
            for k in banks[i]:
                touch[k][eng[i]] = t + tot[i] + lat
            if eng[i] != "none":
                free[eng[i]] = t + o["dur"]
            if "res" in o:
                r0 = max(res.get(o["res"], 0.0), t + o["dur"])
                res[o["res"]] = r0 + o["busy"]
                tot[i] += r0 - t - o["dur"]
        tail, nxt, later = list(tot), {}, {}

        def behind(i):
            t = tail[i]
            if eng[i] != "none":
                t = max(t, ops[i]["dur"] + nxt.get(eng[i], 0.0))
            for k in banks[i]:
                for e, v in later.get(k, {}).items():
                    if e != eng[i]:
                        t = max(t, tot[i] + lat + v)
            return t
        for i in reversed(order[b:]):
            tail[i] = nxt[eng[i]] = behind(i)
            for k in banks[i]:
                later.setdefault(k, {})[eng[i]] = tail[i]
            for j, w in waits[i]:
                tail[j] = max(tail[j], (tot[j] + lat if w else ops[j]["dur"]) + tail[i])
        inside = set(order[a:b])
        head, edge = {}, {}
        for i in inside:
            head[i] = max([st[j] + (tot[j] + lat if w else ops[j]["dur"]) for j, w in waits[i] if j not in inside] + [first.get(eng[i], 0.0)]
                          + [v for k in banks[i] for e, v in used.get(k, {}).items() if e != eng[i]])
            edge[i] = [(j, tot[j] + lat if w else ops[j]["dur"]) for j, w in waits[i] if j in inside]
            tail[i] = behind(i)
        return head, edge, tail, [o["dur"] for o in ops], lat

    def walk(win, fr):
        head, edge, tail, dur, lat = fr
        st, par, last, touch = {}, {}, {}, {}
        top, at = 0.0, -1
        for i in win:
            t, p = head[i], -1
            for j, w in edge[i]:
                v = st[j] + w
                if v > t:
                    t, p = v, j
            e = eng[i]
            j = last.get(e)
            if j is not None and e != "none":
                v = st[j] + dur[j]
                if v >= t:
                    t, p = v, -2 - j
            last[e] = i
            for k in banks[i]:
                d = touch.setdefault(k, {})
                for f, j in d.items():
                    if f != e and st[j] + dur[j] + lat > t:
                        t, p = st[j] + dur[j] + lat, -2 - j
                d[e] = i
            st[i], par[i] = t, p
            if t + tail[i] > top:
                top, at = t + tail[i], i
        return top, at, par

    size = OPT["size"]
    for sweep in range(OPT["sweeps"]):
        heat = OPT["heat"] * (1.0 - 0.8 * sweep / OPT["sweeps"])
        for a in range(-(sweep * size // 5) % (size // 2) - size // 2, n - size // 3, size // 2):
            a, b = max(a, 0), min(n, a + size)
            frs = [frame(ops, m["lat"], a, b) for ops, m in zip(sets, GUESS)]
            win = order[a:b]
            cur = [walk(win, fr) for fr in frs]
            score = sum(c[0] for c in cur)
            best = (score, win)
            for move in range(OPT["moves"]):
                c = cur[int(rand() * len(cur))]
                i, pairs = c[1], []
                while i != -1:
                    p = c[2][i]
                    if p <= -2:
                        p = -2 - p
                        if p not in pre[i]:
                            pairs.append((p, i))
                    i = p
                if not pairs:
                    continue
                u, v = pairs[int(rand() * len(pairs))]
                x, y = win.index(u), win.index(v)
                if rand() < OPT["back"]:
                    back = [u]
                    for z in win[x + 1:y + 1]:
                        if any(f in pre[z] for f in back):
                            back.append(z)
                    if v in back:
                        continue
                    new = win[:x] + [z for z in win[x:y + 1] if z not in back] + back + win[y + 1:]
                else:
                    front = [v]
                    for z in reversed(win[x:y]):
                        if any(z in pre[f] for f in front):
                            front.append(z)
                    if u in front:
                        continue
                    new = win[:x] + front[::-1] + [z for z in win[x:y] if z not in front] + win[y + 1:]
                res = [walk(new, fr) for fr in frs]
                s = sum(r[0] for r in res)
                if s < score - heat * math.log(rand() + 1e-9) * (1.0 - move / OPT["moves"]):
                    win, cur, score = new, res, s
                    if s < best[0]:
                        best = (s, new)
            order[a:b] = best[1]
    return order


GUESS = [{"g": 1.56, "f": 1.0, "lat": 150.0, "link": 70.0},
         {"g": 1.1, "f": 1.2, "lat": 100.0, "link": 70.0},
         {"g": 1.8, "f": 1.35, "lat": 280.0, "link": 100.0}]
PLAN = {}


def bank_turns(ops, order):
    touch = {}
    for i in order:
        o = ops[i]
        for b in o["banks"]:
            for e, j in touch.get(b, {}).items():
                if e != o["eng"]:
                    o["deps"][j] = "raw"
            touch.setdefault(b, {})[o["eng"]] = i


def plan():
    if not PLAN:
        sets = []
        for m in GUESS[::-1]:
            OPT.update(m)
            sets.append(build())
        PLAN["order"] = improve(sets[::-1], schedule(sets[-1]))
        PLAN["ops"] = sets[-1]
        bank_turns(PLAN["ops"], PLAN["order"])
    return PLAN["ops"], PLAN["order"]


def rank_program(g, core, T, topo):
    rank = T.rank_of(core)
    cores = T.cores
    n = len(cores)
    ops, order = plan()

    def helper(src, dst):
        if topo.chip(src) == topo.chip(dst):
            return None
        for h in topo.cores_of(src):
            if h not in cores and topo.die(h) != topo.die(src) and topo.may_write(h, dst):
                return h
        return None

    def spare(src, h, dst):
        return [e for e in topo.engines(src, h) if e not in topo.engines(src, dst)]

    if rank is None:
        ends = []
        for i in order:
            o = ops[i]
            if o["kind"] != "send" or "relay" not in o:
                continue
            for r in range(n):
                src, dst = cores[r], cores[(r + o["to"]) % n]
                if helper(src, dst) == core:
                    rid, pid, _ = topo.addr(dst)
                    g.wait_ge(T.sem[o["hsem"]], len(spare(src, core, dst)))
                    g.remote_dma(o["fn"][1](T), ap(T, o["relay"]), T.sem[o["rsem"]], T.sem[o["sem"]], pid, rid, topo.mask(core, dst))
                    ends.append((o["sem"], len(topo.engines(core, dst))))
        for sem, cnt in ends:
            g.wait_ge(T.sem[sem], cnt)
        return
    queue = {"pe": g.tensor, "act": g.scalar, "dve": g.vector, "pool": g, "sync": g.sync}
    known = {e: {} for e in queue}
    done = {}
    counter = {e: 0 for e in queue}
    total = {}
    for i in order:
        o = ops[i]
        e = o["eng"]
        if o["kind"] == "recv":
            src = cores[(rank - o["to"]) % n]
            if "relay" in o and helper(src, core) is not None:
                src = helper(src, core)
            cnt = len(topo.engines(src, core))
            done[i] = (o["sem"], cnt, {})
            total[o["sem"]] = cnt
            continue
        kn = known[e]
        need = [done[j] for j, kind in o["deps"].items() if needs_wait(ops[j], o, kind)]
        for sem, cnt, clock in sorted(need, key=lambda d: -len(d[2])):
            top = max(d[1] for d in need if d[0] == sem)
            if cnt == top and kn.get(sem, 0) < cnt:
                queue[e].wait_ge(T.sem[sem], cnt)
                kn[sem] = cnt
                for s, v in clock.items():
                    if kn.get(s, 0) < v:
                        kn[s] = v
        if o["kind"] == "c":
            counter[e] += 1
            sem, cnt = "c_" + e, counter[e]
            o["fn"](g, T).then_inc(T.sem[sem], 1)
        elif o["kind"] == "dma":
            pairs = o["fn"](T)
            sem, cnt = o["sem"], 16 * len(pairs)
            for out, src in pairs:
                queue[e].dma_start(out, src).then_inc(T.sem[sem], 16)
        else:
            dst = cores[(rank + o["to"]) % n]
            rid, pid, _ = topo.addr(dst)
            sem, cnt = o["sem"], len(topo.engines(core, dst))
            src, land = o["fn"]
            h = helper(core, dst) if "relay" in o else None
            if h is not None:
                rid, pid, _ = topo.addr(h)
                es = spare(core, h, dst)
                cnt = len(es)
                g.remote_dma(ap(T, o["relay"]), src(T), T.sem[o["hsem"]], T.sem[sem], pid, rid, sum(1 << x for x in es))
            elif src is None:
                g.remote_sem_update(T.sem[o["rsem"]], T.sem[sem], pid, rid, topo.mask(core, dst))
            else:
                g.remote_dma(land(T), src(T), T.sem[o["rsem"]], T.sem[sem], pid, rid, topo.mask(core, dst))
        done[i] = (sem, cnt, dict(kn))
        total[sem] = cnt
    waited = {}
    for kn in known.values():
        for s, v in kn.items():
            waited[s] = max(waited.get(s, 0), v)
    for sem, cnt in total.items():
        if waited.get(sem, 0) < cnt:
            g.sync.wait_ge(T.sem[sem], cnt)
